import numpy as np
import ml_dtypes


def mxq(x, axis, fmt="e4m3"):
    dtype, down = {"e4m3": (ml_dtypes.float8_e4m3fn, 7), "e5m2": (ml_dtypes.float8_e5m2, 14)}[fmt]
    v = np.moveaxis(np.asarray(x, np.float32).astype(ml_dtypes.bfloat16).astype(np.float64), axis, -1)
    blocks = v.reshape(v.shape[:-1] + (-1, 32))
    amax = np.abs(blocks).max(-1, keepdims=True)
    byte = np.maximum(np.where(amax > 0, np.frexp(amax)[1] - 1 + 127, 0) - down, 1)
    scale = np.exp2(byte - 127.0)
    codes = (blocks / scale).astype(np.float32).astype(dtype).astype(np.float64)
    return np.moveaxis((codes * scale).reshape(v.shape), -1, axis)


WIDE = False


def mx_kscale(k):
    if not WIDE:
        return np.ones(k)
    levels = np.array([10, -10, 5, -5, 0])
    if k % 512:
        return np.exp2(np.random.permutation(np.resize(levels, k // 32))).repeat(32)
    a = np.empty((k // 512, 16))
    for p in range(k // 512):
        a[p, :8] = np.random.permutation(np.resize(levels, 8))
        for g in range(8):
            far = levels[np.abs(levels - a[p, g]) >= 10]
            a[p, g + 8] = far[np.random.randint(len(far))]
    return np.exp2(a.ravel()).repeat(32)


def f64(x):
    return np.asarray(x).astype(np.float64)


def striped(idx):
    return np.tile(idx.reshape(-1, 16).T, (8, 1)).astype(np.uint16)


def unstriped(offs):
    return offs[:16].T.reshape(-1).astype(np.int64)


E2M1 = np.array([0.0, 0.5, 1.0, 1.5, 2.0, 3.0, 4.0, 6.0, -0.0, -0.5, -1.0, -1.5, -2.0, -3.0, -4.0, -6.0])


def pack_weight(w, fmt):
    k, n = w.shape
    w = f64(np.asarray(w, np.float32).astype(ml_dtypes.bfloat16)).reshape(k // 32, 32, n)
    amax = np.abs(w).max(1)
    if fmt == "e4m3":
        byte = np.frexp(amax)[1] - 1 + 127 - 7
    else:
        mant, ex = np.frexp(amax / 6.0)
        byte = np.where(mant > 0.5, ex, ex - 1) + 127
    byte = np.clip(np.where(amax > 0, byte, 1), 1, 254)
    scaled = (w * np.exp2(127.0 - byte)[:, None, :]).reshape(k, n).astype(np.float32)
    by_word = np.ascontiguousarray(scaled.reshape(k // 512, 128, 4, n).transpose(0, 1, 3, 2))
    if fmt == "e4m3":
        words = by_word.astype(ml_dtypes.float8_e4m3fn).view(np.uint8)
    else:
        c = by_word.astype(ml_dtypes.float4_e2m1fn).view(np.uint8) & 0xF
        words = (c[..., 0::2] | (c[..., 1::2] << 4)).reshape(k // 512, 128, 2 * n)
    return np.ascontiguousarray(words), np.ascontiguousarray(byte.astype(np.uint8).reshape(k // 512, 16, n))


def unpack_weight(words, scales, fmt):
    g, _, n = scales.shape
    words = np.ascontiguousarray(words).reshape(g, 128, n, -1)
    if fmt == "e4m3":
        vals = words.view(ml_dtypes.float8_e4m3fn).astype(np.float64)
    else:
        nib = np.empty((g, 128, n, 4), np.uint8)
        nib[..., 0::2] = words & 0xF
        nib[..., 1::2] = words >> 4
        vals = E2M1[nib]
    vals = vals * np.repeat(np.exp2(scales.astype(np.float64) - 127.0), 8, axis=1)[..., None]
    return vals.transpose(0, 1, 3, 2).reshape(g * 512, n)


def gelu(v):
    return 0.5 * v * (1.0 + np.tanh(np.sqrt(2.0 / np.pi) * (v + 0.044715 * v**3)))


K, L, T, Q, E, C, D = 1024, 512, 768, 512, 4, 128, 128
H, N = 512, 256


def by_expert(wq, xq, C):
    return np.concatenate([wq[e].T @ xq[:, e * C:(e + 1) * C] for e in range(E)], axis=1)


def setup_inputs():
    n = np.random.standard_normal
    s = mx_kscale(K)
    v = mx_kscale(L)
    u = mx_kscale(H)
    slots1, slots2 = np.random.permutation(T)[:E * C], np.random.permutation(Q)[:E * D]
    x = pack_weight(n((K, T)) * s[:, None], "e4m3")
    z = pack_weight(n((L, Q)) * v[:, None], "e4m3")
    w1 = [pack_weight(m, "e2m1") for m in n((E, K, H)) / np.sqrt(K) / s[None, :, None] * u]
    w2 = [pack_weight(m, "e2m1") for m in n((E, H, N)) / np.sqrt(H) / u[None, :, None]]
    return {
        "x_words": x[0],
        "x_scales": x[1],
        "z_words": z[0],
        "z_scales": z[1],
        "w1_words": np.stack([m[0] for m in w1]),
        "w1_scales": np.stack([m[1] for m in w1]),
        "wz": (n((E, L, H)) / np.sqrt(L) / v[None, :, None] * u).astype(np.float32),
        "w2_words": np.stack([m[0] for m in w2]),
        "w2_scales": np.stack([m[1] for m in w2]),
        "gate1": (np.tile(np.random.uniform(0.2, 1.0, E * C), (128, 1))).astype(np.float32),
        "gate2": (np.tile(np.random.uniform(0.2, 1.0, E * D), (128, 1))).astype(np.float32),
        "offs": striped(slots1),
        "offs2": striped(slots2),
    }


def reference(x_words, x_scales, z_words, z_scales, w1_words, w1_scales, wz, w2_words, w2_scales, gate1, gate2, offs, offs2):
    w1 = np.stack([unpack_weight(w1_words[e], w1_scales[e], "e2m1") for e in range(E)])
    wzq = mxq(f64(wz), 1, "e4m3")
    w2 = np.stack([unpack_weight(w2_words[e], w2_scales[e], "e2m1") for e in range(E)])
    idx, idx2 = unstriped(offs), unstriped(offs2)
    xq = unpack_weight(x_words, x_scales, "e4m3")[:, idx]
    zq = unpack_weight(z_words, z_scales, "e4m3")[:, idx2]
    h = gelu(by_expert(w1, xq, C))
    p = gelu(by_expert(wzq, zq, D))
    out = np.zeros((N, T + Q))
    out[:, idx] = f64(gate1[:1]) * by_expert(w2, mxq(h, 0, "e4m3"), C)
    out[:, T + idx2] = f64(gate2[:1]) * by_expert(w2, mxq(p, 0, "e4m3"), D)
    return out

@@ -1,0 +1,314 @@
+from contextlib import ExitStack
+
+import concourse.mybir as mybir
+from concourse.masks import make_identity
+
+F32 = mybir.dt.float32
+BF16 = mybir.dt.bfloat16
+I32 = mybir.dt.int32
+U32 = mybir.dt.uint32
+U16 = mybir.dt.uint16
+U8 = mybir.dt.uint8
+FP8X4 = mybir.dt.float8_e4m3fn_x4
+FP4X4 = mybir.dt.float4_e2m1fn_x4
+GELU = mybir.ActivationFunctionType.Gelu_apprx_tanh
+MULT = mybir.AluOpType.mult
+
+P = 128
+K, L, T, Q, E, C = 1024, 512, 768, 512, 4, 128
+H, N = 512, 256
+S = E * C
+FLOPS = 2 * S * (K * H + L * H + 2 * H * N)
+
+
+def tile_moe_mmo_gelu_kernel(
+    tc, x_words, x_scales, z_words, z_scales, w1_words, w1_scales, wz, w2_words, w2_scales, gate1, gate2, offs, offs2, out
+):
+    nc = tc.nc
+    with ExitStack() as ctx:
+        keep = ctx.enter_context(tc.tile_pool(name="keep", bufs=1))
+        stage = ctx.enter_context(tc.tile_pool(name="stage", bufs=1))
+        psum = ctx.enter_context(tc.psum_pool(name="psum", bufs=1))
+
+        def sb(name, shape, dtype):
+            return keep.tile(shape, dtype, name=name, align_bytes=64)
+
+        offs_t = keep.tile([P, S // 16], U16, name="offs_t")
+        offs2_t = keep.tile([P, S // 16], U16, name="offs2_t")
+        xw = sb("xw", [P, 2, T], I32)
+        xs = sb("xs", [P, 2, T], U8)
+        zw = sb("zw", [P, Q], I32)
+        zs = sb("zs", [P, 1, Q], U8)
+        w1w = [sb("w1w%d" % e, [P, 2, 2 * H], U8) for e in range(E)]
+        w1s = sb("w1s", [P, 2 * E, H], U8)
+        w2w = sb("w2w", [P, E, 2 * N], U8)
+        w2s = sb("w2s", [P, E, N], U8)
+        wz_raw = [stage.tile([P, 4, H], F32, name="wz_raw%d" % e, offset=8192 * e) for e in range(E)]
+        g1 = sb("g1", [P, S], F32)
+        g2 = sb("g2", [P, S], F32)
+        ident = sb("ident", [P, P], F32)
+        out_text = [sb("out_text%d" % h, [P, T], F32) for h in range(2)]
+        out_patch = [sb("out_patch%d" % h, [P, Q], F32) for h in range(2)]
+
+        def zero_plane(plane, engine):
+            engine.memset(plane[:].rearrange("p a w -> p (a w)").bitcast(I32), 0)
+
+        def load_plane(plane, rows, queue):
+            for r in range(4):
+                queue.dma_start(plane[r:P:32, :, :].bitcast(I32), rows[r:16:4, :, :].bitcast(I32))
+
+        zero_plane(xs, nc.vector)
+        zero_plane(w1s, nc.vector)
+        zero_plane(zs, nc.vector)
+        zero_plane(w2s, nc.gpsimd)
+        load_plane(w2s, w2_scales.rearrange("e s b n -> b (e s) n"), nc.gpsimd)
+        make_identity(nc, ident[:])
+        for h in range(2):
+            nc.gpsimd.memset(out_text[h][:], 0.0)
+
+        nc.sync.dma_start(g2[:], gate2)
+        load_plane(xs, x_scales.rearrange("s b t -> b s t"), nc.sync)
+        nc.sync.dma_start(offs_t[:], offs)
+        nc.sync.dma_start(w1w[0][:].bitcast(I32), w1_words[0].rearrange("s p b -> p s b").bitcast(I32))
+        nc.sync.dma_start(xw[:], x_words.rearrange("s p t d -> p s (t d)").bitcast(I32))
+        nc.sync.dma_start(offs2_t[:], offs2)
+        load_plane(w1s, w1_scales.rearrange("e s b i -> b (e s) i"), nc.sync)
+        nc.sync.dma_start(w1w[1][:].bitcast(I32), w1_words[1].rearrange("s p b -> p s b").bitcast(I32))
+        nc.sync.dma_start(zw[:], z_words[0].rearrange("p t d -> p (t d)").bitcast(I32))
+        load_plane(zs, z_scales.rearrange("s b t -> b s t"), nc.sync)
+        nc.sync.dma_start(wz_raw[0][:], wz[0].rearrange("(p j) c -> p j c", j=4))
+        nc.sync.dma_start(w1w[2][:].bitcast(I32), w1_words[2].rearrange("s p b -> p s b").bitcast(I32))
+        nc.sync.dma_start(w2w[:].bitcast(I32), w2_words.rearrange("e s p b -> p (e s) b").bitcast(I32))
+        nc.sync.dma_start(w1w[3][:].bitcast(I32), w1_words[3].rearrange("s p b -> p s b").bitcast(I32))
+        nc.sync.dma_start(g1[:], gate1)
+        nc.sync.dma_start(wz_raw[2][:], wz[2].rearrange("(p j) c -> p j c", j=4))
+        nc.sync.dma_start(wz_raw[1][:], wz[1].rearrange("(p j) c -> p j c", j=4))
+        nc.sync.dma_start(wz_raw[3][:], wz[3].rearrange("(p j) c -> p j c", j=4))
+
+        GROUPS = [[0],[1],[2,3]]
+        xg, xsg, place = {}, {}, {}
+        for group in GROUPS:
+            for s in range(2):
+                xg[group[0], s] = sb("xg%d_%d" % (group[0], s), [P, len(group) * C], U32)
+                xsg[group[0], s] = sb("xsg%d_%d" % (group[0], s), [P, len(group) * C], U8)
+            for a, e in enumerate(group):
+                place[e] = (group[0], slice(a * C, (a + 1) * C))
+        zg = [sb("zg%d" % g, [P, 2 * C], U32) for g in range(2)]
+        zsg = [sb("zsg%d" % g, [P, 2 * C], U8) for g in range(2)]
+        st = {}
+        REUSE = {("p", 0): 16384, ("t", 3): 24576, ("t", 2): 17408, ("t", 1): 0}
+
+        def cols(group):
+            return offs_t[:, 8 * group[0] : 8 * group[-1] + 8]
+
+        def gs(group, s):
+            nc.vector.tensor_copy(xsg[group[0], s][:], xs[:, s, :].indirect(cols(group)))
+
+        def gw(group, s):
+            nc.vector.tensor_copy(xg[group[0], s][:], xw[:, s, :].bitcast(U32).indirect(cols(group)))
+
+        def gzs(g):
+            nc.vector.tensor_copy(zsg[g][:], zs[:, 0, :].indirect(offs2_t[:, 16 * g : 16 * g + 16]))
+
+        def gzw(g):
+            nc.vector.tensor_copy(zg[g][:], zw[:].bitcast(U32).indirect(offs2_t[:, 16 * g : 16 * g + 16]))
+
+        def mt(e):
+            acc = psum.tile([P, H], F32, name="bank_t%d" % e)
+            st["acc_t", e] = acc
+            g, sl = place[e]
+            for s in range(2):
+                nc.tensor.matmul_mx(
+                    out=acc[:],
+                    lhsT=xg[g, s][:, sl].bitcast(FP8X4),
+                    lhsT_scale=xsg[g, s][:, sl],
+                    rhs=w1w[e][:, s, :].bitcast(FP4X4),
+                    rhs_scale=w1s[:, 2 * e + s, :],
+                    start=(s == 0),
+                    stop=(s == 1),
+                )
+
+        def gt(e):
+            hrow = sb("hrow%d" % e, [P, 2, P, 2], BF16)
+            st["hrow", e] = hrow
+            nc.scalar.activation(hrow[:], st["acc_t", e][:].rearrange("c (p u k) -> c u p k", u=2, k=2), GELU)
+
+        def tt(e):
+            turned = st["acc_t", e][:, 0 : 2 * C].rearrange("p (u c) -> p u c", u=2)
+            st["turned", e] = turned
+            words = st["hrow", e][:].rearrange("c u p k -> c (u p k)").bitcast(F32)
+            for u in range(2):
+                nc.tensor.transpose(turned[:, u, :], words[:, u * P : (u + 1) * P], ident[:])
+
+        def ct(e):
+            hidden = sb("hidden_t%d" % e, [P, C * 4], BF16)
+            st["hidden", "t", e] = hidden
+            nc.scalar.copy(
+                hidden[:].bitcast(F32).rearrange("p (c u) -> p c u", u=2),
+                st["turned", e].rearrange("p u c -> p c u"),
+            )
+
+        def cast(e, lo, hi):
+            if lo == 0:
+                st["wz_bf", e] = sb("wz_bf%d" % e, [P, 4 * H], BF16)
+            nc.scalar.copy(
+                st["wz_bf", e][:].rearrange("p (t m j) -> p m j t", t=4, j=4)[:, lo:hi],
+                wz_raw[e][:].rearrange("p j (m t) -> p m j t", t=4)[:, lo:hi],
+            )
+
+        def qw(e):
+            codes = sb("wz_codes%d" % e, [P, H], U32)
+            scales = sb("wz_scales%d" % e, [P, H], U8)
+            st["wzq", e] = (codes, scales)
+            nc.vector.quantize_mx(out=codes[:].bitcast(FP8X4), scales=scales[:], in_=st["wz_bf", e][:])
+
+        def mp(e):
+            codes, scales = st["wzq", e]
+            acc = psum.tile([P, H], F32, name="bank_p%d" % e)
+            st["acc_p", e] = acc
+            g, a = divmod(e, 2)
+            for t in range(4):
+                nc.tensor.matmul_mx(
+                    out=acc[:, t * C : (t + 1) * C],
+                    lhsT=codes[:, t * P : (t + 1) * P].bitcast(FP8X4),
+                    lhsT_scale=scales[:, t * P : (t + 1) * P],
+                    rhs=zg[g][:, a * C : (a + 1) * C].bitcast(FP8X4),
+                    rhs_scale=zsg[g][:, a * C : (a + 1) * C],
+                    start=True,
+                    stop=True,
+                )
+
+        def gp(e):
+            hidden = sb("hidden_p%d" % e, [P, C * 4], BF16)
+            st["hidden", "p", e] = hidden
+            nc.scalar.activation(
+                hidden[:].rearrange("p (c t) -> p c t", t=4), st["acc_p", e][:].rearrange("p (t c) -> p c t", t=4), GELU
+            )
+
+        def qh(k, e):
+            codes = sb("h_codes_%s%d" % (k, e), [P, C], U32)
+            scales = sb("h_scales_%s%d" % (k, e), [P, C], U8)
+            st["hq", k, e] = (codes, scales)
+            nc.vector.quantize_mx(out=codes[:].bitcast(FP8X4), scales=scales[:], in_=st["hidden", k, e][:])
+
+        def m2(k, e):
+            codes, scales = st["hq", k, e]
+            acc = st["acc_" + k, e][:, 2 * C : 4 * C].rearrange("p (h c) -> p h c", h=2)
+            st["acc2", k, e] = acc
+            for h in range(2):
+                nc.tensor.matmul_mx(
+                    out=acc[:, h, :],
+                    lhsT=w2w[:, e, 2 * P * h : 2 * P * (h + 1)].bitcast(FP4X4),
+                    lhsT_scale=w2s[:, e, P * h : P * (h + 1)],
+                    rhs=codes[:].bitcast(FP8X4),
+                    rhs_scale=scales[:],
+                    start=True,
+                    stop=True,
+                )
+
+        def ev(k, e):
+            if (k, e) in REUSE:
+                sums = stage.tile([P, 2, C], F32, name="sums_%s%d" % (k, e), offset=REUSE[k, e])
+            else:
+                sums = sb("sums_%s%d" % (k, e), [P, 2, C], F32)
+            st["sums", k, e] = sums
+            nc.scalar.copy(sums[:], st["acc2", k, e])
+
+        def sc(k, e, h):
+            window, offsets, gate = (out_text, offs_t, g1) if k == "t" else (out_patch, offs2_t, g2)
+            nc.vector.tensor_tensor(
+                window[h][:].indirect(offsets[:, 8 * e : 8 * e + 8]), st["sums", k, e][:, h, :], gate[:, e * C : (e + 1) * C], MULT
+            )
+
+        gw([0], 1)
+        gw([0], 0)
+        gw([1], 0)
+        gs([1], 0)
+        gw([1], 1)
+        gs([1], 1)
+        mt(1)
+        cast(0, 0, 128)
+        qw(0)
+        cast(1, 0, 128)
+        gs([2, 3], 1)
+        gs([0], 0)
+        gzs(0)
+        gzw(1)
+        gw([2, 3], 1)
+        gw([2, 3], 0)
+        cast(2, 0, 128)
+        gt(1)
+        gs([2, 3], 0)
+        tt(1)
+        ct(1)
+        qh("t", 1)
+        m2("t", 1)
+        gzw(0)
+        ev("t", 1)
+        sc("t", 1, 0)
+        mt(2)
+        mt(3)
+        gt(3)
+        qw(2)
+        qw(1)
+        mp(1)
+        gp(1)
+        qh("p", 1)
+        gzs(1)
+        m2("p", 1)
+        tt(3)
+        gs([0], 1)
+        mt(0)
+        gt(0)
+        tt(0)
+        gt(2)
+        tt(2)
+        ct(2)
+        ct(0)
+        qh("t", 0)
+        m2("t", 0)
+        qh("t", 2)
+        m2("t", 2)
+        ev("t", 2)
+        ev("t", 0)
+        sc("t", 0, 0)
+        sc("t", 0, 1)
+        sc("t", 1, 1)
+        sc("t", 2, 1)
+        sc("t", 2, 0)
+        cast(3, 0, 128)
+        qw(3)
+        mp(2)
+        mp(3)
+        mp(0)
+        gp(0)
+        qh("p", 0)
+        m2("p", 0)
+        ev("p", 0)
+        sc("p", 0, 1)
+        sc("p", 0, 0)
+        ct(3)
+        qh("t", 3)
+        m2("t", 3)
+        gp(3)
+        qh("p", 3)
+        m2("p", 3)
+        ev("t", 3)
+        ev("p", 1)
+        sc("p", 1, 1)
+        sc("t", 3, 1)
+        nc.sync.dma_start(out[1 * P : 2 * P, 0:T], out_text[1][:])
+        ev("p", 3)
+        sc("p", 3, 1)
+        gp(2)
+        qh("p", 2)
+        m2("p", 2)
+        ev("p", 2)
+        sc("p", 2, 1)
+        nc.sync.dma_start(out[1 * P : 2 * P, T : T + Q], out_patch[1][:])
+        sc("p", 1, 0)
+        sc("t", 3, 0)
+        nc.sync.dma_start(out[0 * P : 1 * P, 0:T], out_text[0][:])
+        sc("p", 3, 0)
+        sc("p", 2, 0)
+        nc.sync.dma_start(out[0 * P : 1 * P, T : T + Q], out_patch[0][:])

@@ -33,6 +33,11 @@ def tile_moe_mmo_gelu_kernel(
         def sb(name, shape, dtype):
             return keep.tile(shape, dtype, name=name, align_bytes=64)
 
+        PLACE = {"wz_raw0": 0, "wz_bf0": 8192, "hidden_t0": 12288, "hidden_p0": 16384, "hrow0": 13312, "sums_t0": 14336, "sums_p0": 15360, "wz_raw1": 16384, "wz_bf1": 24576, "hidden_t1": 28672, "hidden_p1": 31744, "hrow1": 29696, "sums_t1": 30720, "sums_p1": 48128, "wz_raw2": 31744, "wz_bf2": 39936, "hidden_t2": 44032, "hidden_p2": 47104, "hrow2": 45056, "sums_t2": 17408, "sums_p2": 46080, "wz_raw3": 47104, "wz_bf3": 55296, "hidden_t3": 59392, "hidden_p3": 60416, "hrow3": 61440, "sums_t3": 62464, "sums_p3": 63488}
+
+        def sg(name, shape, dtype):
+            return stage.tile(shape, dtype, name=name, align_bytes=64, offset=PLACE[name])
+
         offs_t = keep.tile([P, S // 16], U16, name="offs_t")
         offs2_t = keep.tile([P, S // 16], U16, name="offs2_t")
         xw = sb("xw", [P, 2, T], I32)
@@ -43,7 +48,7 @@ def tile_moe_mmo_gelu_kernel(
         w1s = sb("w1s", [P, 2 * E, H], U8)
         w2w = sb("w2w", [P, E, 2 * N], U8)
         w2s = sb("w2s", [P, E, N], U8)
-        wz_raw = [stage.tile([P, 4, H], F32, name="wz_raw%d" % e, offset=8192 * e) for e in range(E)]
+        wz_raw = [sg("wz_raw%d" % e, [P, 4, H], F32) for e in range(E)]
         g1 = sb("g1", [P, S], F32)
         g2 = sb("g2", [P, S], F32)
         ident = sb("ident", [P, P], F32)
@@ -66,23 +71,23 @@ def tile_moe_mmo_gelu_kernel(
         for h in range(2):
             nc.gpsimd.memset(out_text[h][:], 0.0)
 
-        nc.sync.dma_start(g2[:], gate2)
         load_plane(xs, x_scales.rearrange("s b t -> b s t"), nc.sync)
-        nc.sync.dma_start(offs_t[:], offs)
         nc.sync.dma_start(w1w[0][:].bitcast(I32), w1_words[0].rearrange("s p b -> p s b").bitcast(I32))
+        nc.sync.dma_start(offs_t[:], offs)
         nc.sync.dma_start(xw[:], x_words.rearrange("s p t d -> p s (t d)").bitcast(I32))
-        nc.sync.dma_start(offs2_t[:], offs2)
-        load_plane(w1s, w1_scales.rearrange("e s b i -> b (e s) i"), nc.sync)
-        nc.sync.dma_start(w1w[1][:].bitcast(I32), w1_words[1].rearrange("s p b -> p s b").bitcast(I32))
-        nc.sync.dma_start(zw[:], z_words[0].rearrange("p t d -> p (t d)").bitcast(I32))
         load_plane(zs, z_scales.rearrange("s b t -> b s t"), nc.sync)
+        nc.sync.dma_start(w1w[1][:].bitcast(I32), w1_words[1].rearrange("s p b -> p s b").bitcast(I32))
+        load_plane(w1s, w1_scales.rearrange("e s b i -> b (e s) i"), nc.sync)
+        nc.sync.dma_start(offs2_t[:], offs2)
+        nc.sync.dma_start(zw[:], z_words[0].rearrange("p t d -> p (t d)").bitcast(I32))
         nc.sync.dma_start(wz_raw[0][:], wz[0].rearrange("(p j) c -> p j c", j=4))
         nc.sync.dma_start(w1w[2][:].bitcast(I32), w1_words[2].rearrange("s p b -> p s b").bitcast(I32))
         nc.sync.dma_start(w2w[:].bitcast(I32), w2_words.rearrange("e s p b -> p (e s) b").bitcast(I32))
-        nc.sync.dma_start(w1w[3][:].bitcast(I32), w1_words[3].rearrange("s p b -> p s b").bitcast(I32))
-        nc.sync.dma_start(g1[:], gate1)
-        nc.sync.dma_start(wz_raw[2][:], wz[2].rearrange("(p j) c -> p j c", j=4))
         nc.sync.dma_start(wz_raw[1][:], wz[1].rearrange("(p j) c -> p j c", j=4))
+        nc.sync.dma_start(g1[:], gate1)
+        nc.sync.dma_start(w1w[3][:].bitcast(I32), w1_words[3].rearrange("s p b -> p s b").bitcast(I32))
+        nc.sync.dma_start(wz_raw[2][:], wz[2].rearrange("(p j) c -> p j c", j=4))
+        nc.sync.dma_start(g2[:], gate2)
         nc.sync.dma_start(wz_raw[3][:], wz[3].rearrange("(p j) c -> p j c", j=4))
 
         GROUPS = [[0],[1],[2,3]]
@@ -96,7 +101,6 @@ def tile_moe_mmo_gelu_kernel(
         zg = [sb("zg%d" % g, [P, 2 * C], U32) for g in range(2)]
         zsg = [sb("zsg%d" % g, [P, 2 * C], U8) for g in range(2)]
         st = {}
-        REUSE = {("p", 0): 16384, ("t", 3): 24576, ("t", 2): 17408, ("t", 1): 0}
 
         def cols(group):
             return offs_t[:, 8 * group[0] : 8 * group[-1] + 8]
@@ -129,7 +133,7 @@ def tile_moe_mmo_gelu_kernel(
                 )
 
         def gt(e):
-            hrow = sb("hrow%d" % e, [P, 2, P, 2], BF16)
+            hrow = sg("hrow%d" % e, [P, 2, P, 2], BF16)
             st["hrow", e] = hrow
             nc.scalar.activation(hrow[:], st["acc_t", e][:].rearrange("c (p u k) -> c u p k", u=2, k=2), GELU)
 
@@ -141,7 +145,7 @@ def tile_moe_mmo_gelu_kernel(
                 nc.tensor.transpose(turned[:, u, :], words[:, u * P : (u + 1) * P], ident[:])
 
         def ct(e):
-            hidden = sb("hidden_t%d" % e, [P, C * 4], BF16)
+            hidden = sg("hidden_t%d" % e, [P, C * 4], BF16)
             st["hidden", "t", e] = hidden
             nc.scalar.copy(
                 hidden[:].bitcast(F32).rearrange("p (c u) -> p c u", u=2),
@@ -150,8 +154,8 @@ def tile_moe_mmo_gelu_kernel(
 
         def cast(e, lo, hi):
             if lo == 0:
-                st["wz_bf", e] = sb("wz_bf%d" % e, [P, 4 * H], BF16)
-            nc.scalar.copy(
+                st["wz_bf", e] = sg("wz_bf%d" % e, [P, 4 * H], BF16)
+            (nc.vector.tensor_copy if e in [0] else nc.scalar.copy)(
                 st["wz_bf", e][:].rearrange("p (t m j) -> p m j t", t=4, j=4)[:, lo:hi],
                 wz_raw[e][:].rearrange("p j (m t) -> p m j t", t=4)[:, lo:hi],
             )
@@ -179,7 +183,7 @@ def tile_moe_mmo_gelu_kernel(
                 )
 
         def gp(e):
-            hidden = sb("hidden_p%d" % e, [P, C * 4], BF16)
+            hidden = sg("hidden_p%d" % e, [P, C * 4], BF16)
             st["hidden", "p", e] = hidden
             nc.scalar.activation(
                 hidden[:].rearrange("p (c t) -> p c t", t=4), st["acc_p", e][:].rearrange("p (t c) -> p c t", t=4), GELU
@@ -207,10 +211,7 @@ def tile_moe_mmo_gelu_kernel(
                 )
 
         def ev(k, e):
-            if (k, e) in REUSE:
-                sums = stage.tile([P, 2, C], F32, name="sums_%s%d" % (k, e), offset=REUSE[k, e])
-            else:
-                sums = sb("sums_%s%d" % (k, e), [P, 2, C], F32)
+            sums = sg("sums_%s%d" % (k, e), [P, 2, C], F32)
             st["sums", k, e] = sums
             nc.scalar.copy(sums[:], st["acc2", k, e])
 
@@ -220,95 +221,95 @@ def tile_moe_mmo_gelu_kernel(
                 window[h][:].indirect(offsets[:, 8 * e : 8 * e + 8]), st["sums", k, e][:, h, :], gate[:, e * C : (e + 1) * C], MULT
             )
 
-        gw([0], 1)
+        gs([0], 0)
+        gs([0], 1)
         gw([0], 0)
-        gw([1], 0)
+        gw([0], 1)
         gs([1], 0)
-        gw([1], 1)
         gs([1], 1)
-        mt(1)
+        gw([1], 0)
+        gw([1], 1)
+        gs([2, 3], 0)
+        gs([2, 3], 1)
+        gw([2, 3], 0)
+        gw([2, 3], 1)
+        gzs(0)
+        gzw(0)
+        gzs(1)
+        gzw(1)
         cast(0, 0, 128)
         qw(0)
         cast(1, 0, 128)
-        gs([2, 3], 1)
-        gs([0], 0)
-        gzs(0)
-        gzw(1)
-        gw([2, 3], 1)
-        gw([2, 3], 0)
-        cast(2, 0, 128)
-        gt(1)
-        gs([2, 3], 0)
-        tt(1)
-        ct(1)
-        qh("t", 1)
-        m2("t", 1)
-        gzw(0)
-        ev("t", 1)
-        sc("t", 1, 0)
-        mt(2)
-        mt(3)
-        gt(3)
-        qw(2)
         qw(1)
-        mp(1)
-        gp(1)
-        qh("p", 1)
-        gzs(1)
-        m2("p", 1)
-        tt(3)
-        gs([0], 1)
-        mt(0)
-        gt(0)
-        tt(0)
-        gt(2)
-        tt(2)
-        ct(2)
-        ct(0)
-        qh("t", 0)
-        m2("t", 0)
-        qh("t", 2)
-        m2("t", 2)
-        ev("t", 2)
-        ev("t", 0)
-        sc("t", 0, 0)
-        sc("t", 0, 1)
-        sc("t", 1, 1)
-        sc("t", 2, 1)
-        sc("t", 2, 0)
+        cast(2, 0, 128)
+        qw(2)
         cast(3, 0, 128)
         qw(3)
-        mp(2)
-        mp(3)
         mp(0)
         gp(0)
         qh("p", 0)
         m2("p", 0)
-        ev("p", 0)
-        sc("p", 0, 1)
-        sc("p", 0, 0)
-        ct(3)
-        qh("t", 3)
-        m2("t", 3)
-        gp(3)
-        qh("p", 3)
-        m2("p", 3)
-        ev("t", 3)
-        ev("p", 1)
-        sc("p", 1, 1)
-        sc("t", 3, 1)
-        nc.sync.dma_start(out[1 * P : 2 * P, 0:T], out_text[1][:])
-        ev("p", 3)
-        sc("p", 3, 1)
+        mp(1)
+        gp(1)
+        qh("p", 1)
+        m2("p", 1)
+        mp(2)
         gp(2)
         qh("p", 2)
         m2("p", 2)
-        ev("p", 2)
-        sc("p", 2, 1)
-        nc.sync.dma_start(out[1 * P : 2 * P, T : T + Q], out_patch[1][:])
+        mp(3)
+        gp(3)
+        qh("p", 3)
+        m2("p", 3)
+        mt(0)
+        gt(0)
+        tt(0)
+        ct(0)
+        qh("t", 0)
+        m2("t", 0)
+        mt(1)
+        gt(1)
+        tt(1)
+        ct(1)
+        qh("t", 1)
+        m2("t", 1)
+        mt(2)
+        gt(2)
+        tt(2)
+        ct(2)
+        qh("t", 2)
+        m2("t", 2)
+        mt(3)
+        gt(3)
+        tt(3)
+        ct(3)
+        qh("t", 3)
+        m2("t", 3)
+        ev("p", 0)
+        sc("p", 0, 0)
+        sc("p", 0, 1)
+        ev("p", 1)
         sc("p", 1, 0)
+        sc("p", 1, 1)
+        ev("p", 2)
+        sc("p", 2, 0)
+        sc("p", 2, 1)
+        ev("t", 1)
+        sc("t", 1, 0)
+        sc("t", 1, 1)
+        ev("t", 0)
+        sc("t", 0, 0)
+        sc("t", 0, 1)
+        ev("t", 2)
+        sc("t", 2, 0)
+        sc("t", 2, 1)
+        ev("t", 3)
         sc("t", 3, 0)
         nc.sync.dma_start(out[0 * P : 1 * P, 0:T], out_text[0][:])
+        sc("t", 3, 1)
+        nc.sync.dma_start(out[1 * P : 2 * P, 0:T], out_text[1][:])
+        ev("p", 3)
         sc("p", 3, 0)
-        sc("p", 2, 0)
         nc.sync.dma_start(out[0 * P : 1 * P, T : T + Q], out_patch[0][:])
+        sc("p", 3, 1)
+        nc.sync.dma_start(out[1 * P : 2 * P, T : T + Q], out_patch[1][:])

@@ -1,7 +1,6 @@
 from contextlib import ExitStack
 
 import concourse.mybir as mybir
-from concourse.masks import make_identity
 
 F32 = mybir.dt.float32
 BF16 = mybir.dt.bfloat16
@@ -13,12 +12,121 @@ FP8X4 = mybir.dt.float8_e4m3fn_x4
 FP4X4 = mybir.dt.float4_e2m1fn_x4
 GELU = mybir.ActivationFunctionType.Gelu_apprx_tanh
 MULT = mybir.AluOpType.mult
+ADD = mybir.AluOpType.add
+IS_EQUAL = mybir.AluOpType.is_equal
 
 P = 128
 K, L, T, Q, E, C = 1024, 512, 768, 512, 4, 128
 H, N = 512, 256
 S = E * C
 FLOPS = 2 * S * (K * H + L * H + 2 * H * N)
+
+LOADS = [
+    ("offs",),
+    ("offs2",),
+    ("xs",),
+    ("xw",),
+    ("w1w", 0, 1),
+    ("w1s",),
+    ("w1w", 1, 2),
+    ("zw",),
+    ("w1w", 2, 4),
+    ("zs",),
+    ("w2w", 0, 2),
+    ("wz", 0, 0),
+    ("g", "t", 0, 2),
+    ("wz", 1, 0),
+    ("w2w", 2, 4),
+    ("g", "t", 2, 4),
+    ("wz", 2, 0),
+    ("g", "p", 0, 2),
+    ("wz", 3, 0),
+    ("g", "p", 2, 4),
+]
+STEPS = [
+    ("gxs", 0, 0, 4),
+    ("gxs", 1, 0, 4),
+    ("gxw", 0, 0, 1),
+    ("gxw", 1, 0, 1),
+    ("gxw", 0, 1, 2),
+    ("gxw", 1, 1, 2),
+    ("gxw", 0, 2, 4),
+    ("gxw", 1, 2, 4),
+    ("gzw", 0, 2),
+    ("gzw", 2, 4),
+    ("gzs", 0, 2),
+    ("gzs", 2, 4),
+    ("mt", 0),
+    ("mt", 1),
+    ("mt", 2),
+    ("mt", 3),
+    ("gt", 0),
+    ("gt", 1),
+    ("gt", 2),
+    ("gt", 3),
+    ("tt", 0),
+    ("ct", 0),
+    ("tt", 1),
+    ("ct", 1),
+    ("tt", 2),
+    ("ct", 2),
+    ("tt", 3),
+    ("ct", 3),
+    ("qh", "t", 0),
+    ("m2", "t", 0),
+    ("qh", "t", 1),
+    ("m2", "t", 1),
+    ("cast", 0, 0),
+    ("qw", 0),
+    ("mp", 0),
+    ("qh", "t", 2),
+    ("m2", "t", 2),
+    ("qh", "t", 3),
+    ("m2", "t", 3),
+    ("ev", "t", 0),
+    ("sc", "t", 0),
+    ("ev", "t", 1),
+    ("sc", "t", 1),
+    ("cast", 1, 0),
+    ("qw", 1),
+    ("mp", 1),
+    ("gp", 0),
+    ("qh", "p", 0),
+    ("m2", "p", 0),
+    ("ev", "t", 2),
+    ("sc", "t", 2),
+    ("ev", "t", 3),
+    ("sc", "t", 3),
+    ("cast", 2, 0),
+    ("qw", 2),
+    ("mp", 2),
+    ("gp", 1),
+    ("qh", "p", 1),
+    ("m2", "p", 1),
+    ("ev", "p", 0),
+    ("sc", "p", 0),
+    ("cast", 3, 0),
+    ("qw", 3),
+    ("mp", 3),
+    ("gp", 2),
+    ("qh", "p", 2),
+    ("m2", "p", 2),
+    ("ev", "p", 1),
+    ("sc", "p", 1),
+    ("gp", 3),
+    ("qh", "p", 3),
+    ("m2", "p", 3),
+    ("ev", "p", 2),
+    ("sc", "p", 2),
+    ("ev", "p", 3),
+    ("sc", "p", 3),
+]
+WZ_PARTS = [1,1,1,1]
+CAST_PARTS = [1,1,1,1]
+CAST_ON = {(0, 0): "v"}
+ON = {"h_scales_t0": ("zs", 0), "h_scales_t1": ("zs", 128), "h_scales_t2": ("wz_raw0_0", 2048), "h_scales_t3": ("wz_raw0_0", 3072), "sums_t0": ("wz_raw0_0", 0), "hidden_p0": ("wz_raw1_0", 0), "sums_t2": ("wz_raw1_0", 1024), "sums_t3": ("wz_raw1_0", 2048), "sums_p0": ("wz_raw2_0", 0), "hidden_p1": ("wz_raw2_0", 1024), "hidden_p2": ("wz_raw3_0", 0), "sums_p1": ("wz_raw3_0", 1024), "sums_p2": ("wz_codes3", 0), "sums_t1": ("wz_raw0_0", 1024)}
+POOL_PLANES = ["w2s"]
+ACT_PLANES = []
 
 
 def tile_moe_mmo_gelu_kernel(
@@ -29,103 +137,147 @@ def tile_moe_mmo_gelu_kernel(
         keep = ctx.enter_context(tc.tile_pool(name="keep", bufs=1))
         stage = ctx.enter_context(tc.tile_pool(name="stage", bufs=1))
         psum = ctx.enter_context(tc.psum_pool(name="psum", bufs=1))
+        place = {}
+        top = [0]
 
         def sb(name, shape, dtype):
             return keep.tile(shape, dtype, name=name, align_bytes=64)
 
-        PLACE = {"wz_raw0": 0, "wz_bf0": 8192, "hidden_t0": 12288, "hidden_p0": 16384, "hrow0": 13312, "sums_t0": 14336, "sums_p0": 15360, "wz_raw1": 16384, "wz_bf1": 24576, "hidden_t1": 28672, "hidden_p1": 31744, "hrow1": 29696, "sums_t1": 30720, "sums_p1": 48128, "wz_raw2": 31744, "wz_bf2": 39936, "hidden_t2": 44032, "hidden_p2": 47104, "hrow2": 45056, "sums_t2": 17408, "sums_p2": 46080, "wz_raw3": 47104, "wz_bf3": 55296, "hidden_t3": 59392, "hidden_p3": 60416, "hrow3": 61440, "sums_t3": 62464, "sums_p3": 63488}
-
-        def sg(name, shape, dtype):
-            return stage.tile(shape, dtype, name=name, align_bytes=64, offset=PLACE[name])
+        def sg(name, shape, dtype, size):
+            if name in ON:
+                host, shift = ON[name]
+                place[name] = place[host] + shift
+            else:
+                place[name] = top[0]
+                top[0] = top[0] + size
+            return stage.tile(shape, dtype, name=name, align_bytes=64, offset=place[name])
 
         offs_t = keep.tile([P, S // 16], U16, name="offs_t")
         offs2_t = keep.tile([P, S // 16], U16, name="offs2_t")
         xw = sb("xw", [P, 2, T], I32)
         xs = sb("xs", [P, 2, T], U8)
-        zw = sb("zw", [P, Q], I32)
-        zs = sb("zs", [P, 1, Q], U8)
-        w1w = [sb("w1w%d" % e, [P, 2, 2 * H], U8) for e in range(E)]
+        zw = sg("zw", [P, Q], I32, 4 * Q)
+        zs = sg("zs", [P, 1, Q], U8, Q)
         w1s = sb("w1s", [P, 2 * E, H], U8)
-        w2w = sb("w2w", [P, E, 2 * N], U8)
         w2s = sb("w2s", [P, E, N], U8)
-        wz_raw = [sg("wz_raw%d" % e, [P, 4, H], F32) for e in range(E)]
-        g1 = sb("g1", [P, S], F32)
-        g2 = sb("g2", [P, S], F32)
         ident = sb("ident", [P, P], F32)
+        ones = sb("ones", [P, 32], F32)
+        column = sb("column", [P, 32], F32)
+        row = sb("row", [P, 32], F32)
+        zero = sb("zero", [P, 1], F32)
         out_text = [sb("out_text%d" % h, [P, T], F32) for h in range(2)]
         out_patch = [sb("out_patch%d" % h, [P, Q], F32) for h in range(2)]
+        planes = {
+            "xs": (xs, x_scales.rearrange("s b t -> b s t")),
+            "zs": (zs, z_scales.rearrange("s b t -> b s t")),
+            "w1s": (w1s, w1_scales.rearrange("e s b i -> b (e s) i")),
+            "w2s": (w2s, w2_scales.rearrange("e s b n -> b (e s) n")),
+        }
 
         def zero_plane(plane, engine):
             engine.memset(plane[:].rearrange("p a w -> p (a w)").bitcast(I32), 0)
 
-        def load_plane(plane, rows, queue):
+        def load_plane(name, queue):
+            plane, rows = planes[name]
             for r in range(4):
                 queue.dma_start(plane[r:P:32, :, :].bitcast(I32), rows[r:16:4, :, :].bitcast(I32))
 
-        zero_plane(xs, nc.vector)
-        zero_plane(w1s, nc.vector)
-        zero_plane(zs, nc.vector)
-        zero_plane(w2s, nc.gpsimd)
-        load_plane(w2s, w2_scales.rearrange("e s b n -> b (e s) n"), nc.gpsimd)
-        make_identity(nc, ident[:])
+        zero_plane(xs, nc.gpsimd)
+        for name in POOL_PLANES:
+            zero_plane(planes[name][0], nc.gpsimd)
+            load_plane(name, nc.gpsimd)
+        nc.vector.memset(zero[:], 0.0)
+        nc.vector.memset(ones[:], 1.0)
+        for name in ["w1s", "zs", "w2s"]:
+            if name not in POOL_PLANES:
+                zero_plane(planes[name][0], nc.vector)
+        for name in ACT_PLANES:
+            load_plane(name, nc.scalar)
+        nc.vector.tensor_tensor_scan(column[:], ones[:], ones[:], 0.0, MULT, ADD)
+        nc.vector.memset(ident[:], 0.0)
+        nc.vector.transpose(row[:], column[:])
+        for a in range(4):
+            rows = slice(32 * a, 32 * a + 32)
+            nc.vector.tensor_tensor(ident[rows, rows], column[rows, :], row[rows, :], IS_EQUAL)
         for h in range(2):
-            nc.gpsimd.memset(out_text[h][:], 0.0)
+            nc.scalar.activation(out_text[h][:], zero[:].to_broadcast([P, T]), GELU)
 
-        load_plane(xs, x_scales.rearrange("s b t -> b s t"), nc.sync)
-        nc.sync.dma_start(w1w[0][:].bitcast(I32), w1_words[0].rearrange("s p b -> p s b").bitcast(I32))
-        nc.sync.dma_start(offs_t[:], offs)
-        nc.sync.dma_start(xw[:], x_words.rearrange("s p t d -> p s (t d)").bitcast(I32))
-        load_plane(zs, z_scales.rearrange("s b t -> b s t"), nc.sync)
-        nc.sync.dma_start(w1w[1][:].bitcast(I32), w1_words[1].rearrange("s p b -> p s b").bitcast(I32))
-        load_plane(w1s, w1_scales.rearrange("e s b i -> b (e s) i"), nc.sync)
-        nc.sync.dma_start(offs2_t[:], offs2)
-        nc.sync.dma_start(zw[:], z_words[0].rearrange("p t d -> p (t d)").bitcast(I32))
-        nc.sync.dma_start(wz_raw[0][:], wz[0].rearrange("(p j) c -> p j c", j=4))
-        nc.sync.dma_start(w1w[2][:].bitcast(I32), w1_words[2].rearrange("s p b -> p s b").bitcast(I32))
-        nc.sync.dma_start(w2w[:].bitcast(I32), w2_words.rearrange("e s p b -> p (e s) b").bitcast(I32))
-        nc.sync.dma_start(wz_raw[1][:], wz[1].rearrange("(p j) c -> p j c", j=4))
-        nc.sync.dma_start(g1[:], gate1)
-        nc.sync.dma_start(w1w[3][:].bitcast(I32), w1_words[3].rearrange("s p b -> p s b").bitcast(I32))
-        nc.sync.dma_start(wz_raw[2][:], wz[2].rearrange("(p j) c -> p j c", j=4))
-        nc.sync.dma_start(g2[:], gate2)
-        nc.sync.dma_start(wz_raw[3][:], wz[3].rearrange("(p j) c -> p j c", j=4))
+        w1w, w2w, gate, wz_raw = {}, {}, {}, {}
 
-        GROUPS = [[0],[1],[2,3]]
-        xg, xsg, place = {}, {}, {}
-        for group in GROUPS:
-            for s in range(2):
-                xg[group[0], s] = sb("xg%d_%d" % (group[0], s), [P, len(group) * C], U32)
-                xsg[group[0], s] = sb("xsg%d_%d" % (group[0], s), [P, len(group) * C], U8)
-            for a, e in enumerate(group):
-                place[e] = (group[0], slice(a * C, (a + 1) * C))
-        zg = [sb("zg%d" % g, [P, 2 * C], U32) for g in range(2)]
-        zsg = [sb("zsg%d" % g, [P, 2 * C], U8) for g in range(2)]
-        st = {}
+        def load(item):
+            kind = item[0]
+            if kind in planes:
+                load_plane(kind, nc.sync)
+            elif kind == "offs":
+                nc.sync.dma_start(offs_t[:], offs)
+            elif kind == "offs2":
+                nc.sync.dma_start(offs2_t[:], offs2)
+            elif kind == "xw":
+                nc.sync.dma_start(xw[:], x_words.rearrange("s p t d -> p s (t d)").bitcast(I32))
+            elif kind == "zw":
+                nc.sync.dma_start(zw[:], z_words[0].rearrange("p t d -> p (t d)").bitcast(I32))
+            elif kind == "w1w":
+                lo, hi = item[1], item[2]
+                t = sb("w1w%d" % lo, [P, 2 * (hi - lo), 2 * H], U8)
+                nc.sync.dma_start(t[:].bitcast(I32), w1_words[lo:hi].rearrange("e s p b -> p (e s) b").bitcast(I32))
+                for e in range(lo, hi):
+                    w1w[e] = t[:, 2 * (e - lo) : 2 * (e - lo) + 2, :]
+            elif kind == "w2w":
+                lo, hi = item[1], item[2]
+                t = sb("w2w%d" % lo, [P, hi - lo, 2 * N], U8)
+                nc.sync.dma_start(t[:].bitcast(I32), w2_words[lo:hi].rearrange("e s p b -> p (e s) b").bitcast(I32))
+                for e in range(lo, hi):
+                    w2w[e] = t[:, e - lo, :]
+            elif kind == "g":
+                k, lo, hi = item[1], item[2], item[3]
+                t = sb("g%s%d" % (k, lo), [P, (hi - lo) * C], F32)
+                nc.sync.dma_start(t[:], (gate1 if k == "t" else gate2)[:, lo * C : hi * C])
+                for e in range(lo, hi):
+                    gate[k, e] = t[:, (e - lo) * C : (e - lo + 1) * C]
+            else:
+                e, part = item[1], item[2]
+                width = H // WZ_PARTS[e]
+                t = sg("wz_raw%d_%d" % (e, part), [P, 4, width], F32, 16 * width)
+                wz_raw[e, part] = t
+                nc.sync.dma_start(t[:], wz[e].rearrange("(p j) c -> p j c", j=4)[:, :, part * width : (part + 1) * width])
 
-        def cols(group):
-            return offs_t[:, 8 * group[0] : 8 * group[-1] + 8]
+        for item in LOADS:
+            load(item)
 
-        def gs(group, s):
-            nc.vector.tensor_copy(xsg[group[0], s][:], xs[:, s, :].indirect(cols(group)))
+        xg, xsg, zg, zsg, st = {}, {}, {}, {}, {}
 
-        def gw(group, s):
-            nc.vector.tensor_copy(xg[group[0], s][:], xw[:, s, :].bitcast(U32).indirect(cols(group)))
+        def gxs(s, lo, hi):
+            t = sg("xsg%d_%d" % (s, lo), [P, (hi - lo) * C], U8, (hi - lo) * C)
+            nc.vector.tensor_copy(t[:], xs[:, s, :].indirect(offs_t[:, 8 * lo : 8 * hi]))
+            for e in range(lo, hi):
+                xsg[s, e] = t[:, (e - lo) * C : (e - lo + 1) * C]
 
-        def gzs(g):
-            nc.vector.tensor_copy(zsg[g][:], zs[:, 0, :].indirect(offs2_t[:, 16 * g : 16 * g + 16]))
+        def gxw(s, lo, hi):
+            t = sg("xg%d_%d" % (s, lo), [P, (hi - lo) * C], U32, 4 * (hi - lo) * C)
+            nc.vector.tensor_copy(t[:], xw[:, s, :].bitcast(U32).indirect(offs_t[:, 8 * lo : 8 * hi]))
+            for e in range(lo, hi):
+                xg[s, e] = t[:, (e - lo) * C : (e - lo + 1) * C]
 
-        def gzw(g):
-            nc.vector.tensor_copy(zg[g][:], zw[:].bitcast(U32).indirect(offs2_t[:, 16 * g : 16 * g + 16]))
+        def gzs(lo, hi):
+            t = sg("zsg%d" % lo, [P, (hi - lo) * C], U8, (hi - lo) * C)
+            nc.vector.tensor_copy(t[:], zs[:, 0, :].indirect(offs2_t[:, 8 * lo : 8 * hi]))
+            for e in range(lo, hi):
+                zsg[e] = t[:, (e - lo) * C : (e - lo + 1) * C]
+
+        def gzw(lo, hi):
+            t = sg("zg%d" % lo, [P, (hi - lo) * C], U32, 4 * (hi - lo) * C)
+            nc.vector.tensor_copy(t[:], zw[:].bitcast(U32).indirect(offs2_t[:, 8 * lo : 8 * hi]))
+            for e in range(lo, hi):
+                zg[e] = t[:, (e - lo) * C : (e - lo + 1) * C]
 
         def mt(e):
             acc = psum.tile([P, H], F32, name="bank_t%d" % e)
             st["acc_t", e] = acc
-            g, sl = place[e]
             for s in range(2):
                 nc.tensor.matmul_mx(
                     out=acc[:],
-                    lhsT=xg[g, s][:, sl].bitcast(FP8X4),
-                    lhsT_scale=xsg[g, s][:, sl],
+                    lhsT=xg[s, e].bitcast(FP8X4),
+                    lhsT_scale=xsg[s, e],
                     rhs=w1w[e][:, s, :].bitcast(FP4X4),
                     rhs_scale=w1s[:, 2 * e + s, :],
                     start=(s == 0),
@@ -133,7 +285,7 @@ def tile_moe_mmo_gelu_kernel(
                 )
 
         def gt(e):
-            hrow = sg("hrow%d" % e, [P, 2, P, 2], BF16)
+            hrow = sg("hrow%d" % e, [P, 2, P, 2], BF16, 1024)
             st["hrow", e] = hrow
             nc.scalar.activation(hrow[:], st["acc_t", e][:].rearrange("c (p u k) -> c u p k", u=2, k=2), GELU)
 
@@ -145,24 +297,27 @@ def tile_moe_mmo_gelu_kernel(
                 nc.tensor.transpose(turned[:, u, :], words[:, u * P : (u + 1) * P], ident[:])
 
         def ct(e):
-            hidden = sg("hidden_t%d" % e, [P, C * 4], BF16)
+            hidden = sg("hidden_t%d" % e, [P, C * 4], BF16, 1024)
             st["hidden", "t", e] = hidden
             nc.scalar.copy(
                 hidden[:].bitcast(F32).rearrange("p (c u) -> p c u", u=2),
                 st["turned", e].rearrange("p u c -> p c u"),
             )
 
-        def cast(e, lo, hi):
-            if lo == 0:
-                st["wz_bf", e] = sg("wz_bf%d" % e, [P, 4 * H], BF16)
-            (nc.vector.tensor_copy if e in [0] else nc.scalar.copy)(
-                st["wz_bf", e][:].rearrange("p (t m j) -> p m j t", t=4, j=4)[:, lo:hi],
-                wz_raw[e][:].rearrange("p j (m t) -> p m j t", t=4)[:, lo:hi],
+        def cast(e, part):
+            if part == 0:
+                st["wz_bf", e] = sg("wz_bf%d" % e, [P, 4 * H], BF16, 4096)
+            width = P // CAST_PARTS[e]
+            held, inside = divmod(part * width, P // WZ_PARTS[e])
+            engine = {"v": nc.vector.tensor_copy, "s": nc.scalar.copy, "g": nc.gpsimd.tensor_copy}[CAST_ON.get((e, part), "s")]
+            engine(
+                st["wz_bf", e][:].rearrange("p (t m j) -> p m j t", t=4, j=4)[:, part * width : (part + 1) * width],
+                wz_raw[e, held][:].rearrange("p j (m t) -> p m j t", t=4)[:, inside : inside + width],
             )
 
         def qw(e):
-            codes = sb("wz_codes%d" % e, [P, H], U32)
-            scales = sb("wz_scales%d" % e, [P, H], U8)
+            codes = sg("wz_codes%d" % e, [P, H], U32, 2048)
+            scales = sg("wz_scales%d" % e, [P, H], U8, 512)
             st["wzq", e] = (codes, scales)
             nc.vector.quantize_mx(out=codes[:].bitcast(FP8X4), scales=scales[:], in_=st["wz_bf", e][:])
 
@@ -170,28 +325,27 @@ def tile_moe_mmo_gelu_kernel(
             codes, scales = st["wzq", e]
             acc = psum.tile([P, H], F32, name="bank_p%d" % e)
             st["acc_p", e] = acc
-            g, a = divmod(e, 2)
             for t in range(4):
                 nc.tensor.matmul_mx(
                     out=acc[:, t * C : (t + 1) * C],
                     lhsT=codes[:, t * P : (t + 1) * P].bitcast(FP8X4),
                     lhsT_scale=scales[:, t * P : (t + 1) * P],
-                    rhs=zg[g][:, a * C : (a + 1) * C].bitcast(FP8X4),
-                    rhs_scale=zsg[g][:, a * C : (a + 1) * C],
+                    rhs=zg[e].bitcast(FP8X4),
+                    rhs_scale=zsg[e],
                     start=True,
                     stop=True,
                 )
 
         def gp(e):
-            hidden = sg("hidden_p%d" % e, [P, C * 4], BF16)
+            hidden = sg("hidden_p%d" % e, [P, C * 4], BF16, 1024)
             st["hidden", "p", e] = hidden
             nc.scalar.activation(
                 hidden[:].rearrange("p (c t) -> p c t", t=4), st["acc_p", e][:].rearrange("p (t c) -> p c t", t=4), GELU
             )
 
         def qh(k, e):
-            codes = sb("h_codes_%s%d" % (k, e), [P, C], U32)
-            scales = sb("h_scales_%s%d" % (k, e), [P, C], U8)
+            codes = sg("h_codes_%s%d" % (k, e), [P, C], U32, 512)
+            scales = sg("h_scales_%s%d" % (k, e), [P, C], U8, 128)
             st["hq", k, e] = (codes, scales)
             nc.vector.quantize_mx(out=codes[:].bitcast(FP8X4), scales=scales[:], in_=st["hidden", k, e][:])
 
@@ -202,7 +356,7 @@ def tile_moe_mmo_gelu_kernel(
             for h in range(2):
                 nc.tensor.matmul_mx(
                     out=acc[:, h, :],
-                    lhsT=w2w[:, e, 2 * P * h : 2 * P * (h + 1)].bitcast(FP4X4),
+                    lhsT=w2w[e][:, 2 * P * h : 2 * P * (h + 1)].bitcast(FP4X4),
                     lhsT_scale=w2s[:, e, P * h : P * (h + 1)],
                     rhs=codes[:].bitcast(FP8X4),
                     rhs_scale=scales[:],
@@ -211,105 +365,44 @@ def tile_moe_mmo_gelu_kernel(
                 )
 
         def ev(k, e):
-            sums = sg("sums_%s%d" % (k, e), [P, 2, C], F32)
+            sums = sg("sums_%s%d" % (k, e), [P, 2, C], F32, 1024)
             st["sums", k, e] = sums
             nc.scalar.copy(sums[:], st["acc2", k, e])
 
-        def sc(k, e, h):
-            window, offsets, gate = (out_text, offs_t, g1) if k == "t" else (out_patch, offs2_t, g2)
+        def sch(k, e, h):
+            window, offsets = (out_text, offs_t) if k == "t" else (out_patch, offs2_t)
             nc.vector.tensor_tensor(
-                window[h][:].indirect(offsets[:, 8 * e : 8 * e + 8]), st["sums", k, e][:, h, :], gate[:, e * C : (e + 1) * C], MULT
+                window[h][:].indirect(offsets[:, 8 * e : 8 * e + 8]), st["sums", k, e][:, h, :], gate[k, e], MULT
             )
+            if e == E - 1:
+                columns = slice(0, T) if k == "t" else slice(T, T + Q)
+                nc.sync.dma_start(out[h * P : (h + 1) * P, columns], window[h][:])
 
-        gs([0], 0)
-        gs([0], 1)
-        gw([0], 0)
-        gw([0], 1)
-        gs([1], 0)
-        gs([1], 1)
-        gw([1], 0)
-        gw([1], 1)
-        gs([2, 3], 0)
-        gs([2, 3], 1)
-        gw([2, 3], 0)
-        gw([2, 3], 1)
-        gzs(0)
-        gzw(0)
-        gzs(1)
-        gzw(1)
-        cast(0, 0, 128)
-        qw(0)
-        cast(1, 0, 128)
-        qw(1)
-        cast(2, 0, 128)
-        qw(2)
-        cast(3, 0, 128)
-        qw(3)
-        mp(0)
-        gp(0)
-        qh("p", 0)
-        m2("p", 0)
-        mp(1)
-        gp(1)
-        qh("p", 1)
-        m2("p", 1)
-        mp(2)
-        gp(2)
-        qh("p", 2)
-        m2("p", 2)
-        mp(3)
-        gp(3)
-        qh("p", 3)
-        m2("p", 3)
-        mt(0)
-        gt(0)
-        tt(0)
-        ct(0)
-        qh("t", 0)
-        m2("t", 0)
-        mt(1)
-        gt(1)
-        tt(1)
-        ct(1)
-        qh("t", 1)
-        m2("t", 1)
-        mt(2)
-        gt(2)
-        tt(2)
-        ct(2)
-        qh("t", 2)
-        m2("t", 2)
-        mt(3)
-        gt(3)
-        tt(3)
-        ct(3)
-        qh("t", 3)
-        m2("t", 3)
-        ev("p", 0)
-        sc("p", 0, 0)
-        sc("p", 0, 1)
-        ev("p", 1)
-        sc("p", 1, 0)
-        sc("p", 1, 1)
-        ev("p", 2)
-        sc("p", 2, 0)
-        sc("p", 2, 1)
-        ev("t", 1)
-        sc("t", 1, 0)
-        sc("t", 1, 1)
-        ev("t", 0)
-        sc("t", 0, 0)
-        sc("t", 0, 1)
-        ev("t", 2)
-        sc("t", 2, 0)
-        sc("t", 2, 1)
-        ev("t", 3)
-        sc("t", 3, 0)
-        nc.sync.dma_start(out[0 * P : 1 * P, 0:T], out_text[0][:])
-        sc("t", 3, 1)
-        nc.sync.dma_start(out[1 * P : 2 * P, 0:T], out_text[1][:])
-        ev("p", 3)
-        sc("p", 3, 0)
-        nc.sync.dma_start(out[0 * P : 1 * P, T : T + Q], out_patch[0][:])
-        sc("p", 3, 1)
-        nc.sync.dma_start(out[1 * P : 2 * P, T : T + Q], out_patch[1][:])
+        def sc(k, e):
+            for h in range(2):
+                sch(k, e, h)
+
+        def text(e):
+            mt(e)
+            gt(e)
+            tt(e)
+            ct(e)
+            qh("t", e)
+            m2("t", e)
+            ev("t", e)
+
+        def patch(e):
+            qw(e)
+            mp(e)
+            gp(e)
+            qh("p", e)
+            m2("p", e)
+            ev("p", e)
+
+        def casts(e):
+            for part in range(CAST_PARTS[e]):
+                cast(e, part)
+
+        steps = {"mt": mt, "gt": gt, "tt": tt, "ct": ct, "qh": qh, "m2": m2, "ev": ev, "cast": cast, "qw": qw, "mp": mp, "gp": gp, "gxs": gxs, "gxw": gxw, "gzs": gzs, "gzw": gzw, "text": text, "patch": patch, "casts": casts, "sc": sc, "sch": sch}
+        for step in STEPS:
+            steps[step[0]](*step[1:])

@@ -22,11 +22,11 @@ S = E * C
 FLOPS = 2 * S * (K * H + L * H + 2 * H * N)
 
 LOADS = [
+    ("w1w", 0, 1),
     ("offs",),
-    ("offs2",),
     ("xs",),
     ("xw",),
-    ("w1w", 0, 1),
+    ("offs2",),
     ("w1s",),
     ("w1w", 1, 2),
     ("zw",),
@@ -182,9 +182,9 @@ def tile_moe_mmo_gelu_kernel(
             for r in range(4):
                 queue.dma_start(plane[r:P:32, :, :].bitcast(I32), rows[r:16:4, :, :].bitcast(I32))
 
-        zero_plane(xs, nc.gpsimd)
+        zero_plane(xs, nc.vector)
         for name in POOL_PLANES:
-            zero_plane(planes[name][0], nc.gpsimd)
+            zero_plane(planes[name][0], nc.vector)
             load_plane(name, nc.gpsimd)
         nc.vector.memset(zero[:], 0.0)
         nc.vector.memset(ones[:], 1.0)

@@ -22,36 +22,33 @@ S = E * C
 FLOPS = 2 * S * (K * H + L * H + 2 * H * N)
 
 LOADS = [
-    ("w1w", 0, 1),
+    ("xw", 0),
     ("offs",),
+    ("xw", 1),
     ("xs",),
-    ("xw",),
-    ("offs2",),
+    ("w1w", 0, 1),
     ("w1s",),
+    ("offs2",),
     ("w1w", 1, 2),
     ("zw",),
     ("w1w", 2, 4),
     ("zs",),
     ("w2w", 0, 2),
     ("wz", 0, 0),
-    ("g", "t", 0, 2),
     ("wz", 1, 0),
     ("w2w", 2, 4),
-    ("g", "t", 2, 4),
     ("wz", 2, 0),
-    ("g", "p", 0, 2),
     ("wz", 3, 0),
-    ("g", "p", 2, 4),
 ]
 STEPS = [
-    ("gxs", 0, 0, 4),
-    ("gxs", 1, 0, 4),
-    ("gxw", 0, 0, 1),
-    ("gxw", 1, 0, 1),
-    ("gxw", 0, 1, 2),
-    ("gxw", 1, 1, 2),
-    ("gxw", 0, 2, 4),
-    ("gxw", 1, 2, 4),
+    ("gxw", 0, 0, 4),
+    ("gxw", 1, 0, 4),
+    ("gxs", 0, 0, 1),
+    ("gxs", 1, 0, 1),
+    ("gxs", 0, 1, 2),
+    ("gxs", 1, 1, 2),
+    ("gxs", 0, 2, 4),
+    ("gxs", 1, 2, 4),
     ("gzw", 0, 2),
     ("gzw", 2, 4),
     ("gzs", 0, 2),
@@ -76,7 +73,7 @@ STEPS = [
     ("m2", "t", 0),
     ("qh", "t", 1),
     ("m2", "t", 1),
-    ("cast", 0, 0),
+    ("cast", 0, 0, 4, "v"),
     ("qw", 0),
     ("mp", 0),
     ("qh", "t", 2),
@@ -87,7 +84,7 @@ STEPS = [
     ("sc", "t", 0),
     ("ev", "t", 1),
     ("sc", "t", 1),
-    ("cast", 1, 0),
+    ("cast", 1, 0, 4, "s"),
     ("qw", 1),
     ("mp", 1),
     ("gp", 0),
@@ -97,15 +94,16 @@ STEPS = [
     ("sc", "t", 2),
     ("ev", "t", 3),
     ("sc", "t", 3),
-    ("cast", 2, 0),
+    ("cast", 2, 0, 4, "s"),
     ("qw", 2),
     ("mp", 2),
+    ("cast", 3, 2, 4, "v"),
     ("gp", 1),
     ("qh", "p", 1),
     ("m2", "p", 1),
     ("ev", "p", 0),
     ("sc", "p", 0),
-    ("cast", 3, 0),
+    ("cast", 3, 0, 2, "s"),
     ("qw", 3),
     ("mp", 3),
     ("gp", 2),
@@ -123,8 +121,9 @@ STEPS = [
 ]
 WZ_PARTS = [1,1,1,1]
 CAST_PARTS = [1,1,1,1]
-CAST_ON = {(0, 0): "v"}
-ON = {"h_scales_t0": ("zs", 0), "h_scales_t1": ("zs", 128), "h_scales_t2": ("wz_raw0_0", 2048), "h_scales_t3": ("wz_raw0_0", 3072), "sums_t0": ("wz_raw0_0", 0), "hidden_p0": ("wz_raw1_0", 0), "sums_t2": ("wz_raw1_0", 1024), "sums_t3": ("wz_raw1_0", 2048), "sums_p0": ("wz_raw2_0", 0), "hidden_p1": ("wz_raw2_0", 1024), "hidden_p2": ("wz_raw3_0", 0), "sums_p1": ("wz_raw3_0", 1024), "sums_p2": ("wz_codes3", 0), "sums_t1": ("wz_raw0_0", 1024)}
+CAST_ON = {}
+ON = {"h_scales_t0": ("zs", 0), "h_scales_t1": ("zs", 128), "h_scales_t2": ("wz_raw0_0", 2048), "h_scales_t3": ("wz_raw0_0", 3072), "sums_t0": ("wz_raw0_0", 0), "sums_t1": ("wz_raw0_0", 1024), "hidden_p0": ("wz_raw1_0", 0), "sums_t2": ("wz_raw1_0", 1024), "sums_t3": ("wz_raw1_0", 2048), "hidden_p1": ("wz_raw2_0", 0), "sums_p0": ("wz_raw2_0", 1024), "hidden_p2": ("wz_raw3_0", 0), "sums_p1": ("wz_raw3_0", 1024), "sums_p2": ("wz_codes3", 0)}
+BANK = {}
 POOL_PLANES = ["w2s"]
 ACT_PLANES = []
 
@@ -154,7 +153,7 @@ def tile_moe_mmo_gelu_kernel(
 
         offs_t = keep.tile([P, S // 16], U16, name="offs_t")
         offs2_t = keep.tile([P, S // 16], U16, name="offs2_t")
-        xw = sb("xw", [P, 2, T], I32)
+        xw = [sb("xw%d" % s, [P, T], I32) for s in range(2)]
         xs = sb("xs", [P, 2, T], U8)
         zw = sg("zw", [P, Q], I32, 4 * Q)
         zs = sg("zs", [P, 1, Q], U8, Q)
@@ -183,6 +182,10 @@ def tile_moe_mmo_gelu_kernel(
                 queue.dma_start(plane[r:P:32, :, :].bitcast(I32), rows[r:16:4, :, :].bitcast(I32))
 
         zero_plane(xs, nc.vector)
+        gate_rows = {}
+        for k, source in (("t", gate1), ("p", gate2)):
+            gate_rows[k] = sb("gate_row_" + k, [P, 4], F32)
+            nc.gpsimd.dma_start(gate_rows[k][:], source[0].rearrange("(p j) -> p j", j=4))
         for name in POOL_PLANES:
             zero_plane(planes[name][0], nc.vector)
             load_plane(name, nc.gpsimd)
@@ -203,6 +206,14 @@ def tile_moe_mmo_gelu_kernel(
             nc.scalar.activation(out_text[h][:], zero[:].to_broadcast([P, T]), GELU)
 
         w1w, w2w, gate, wz_raw = {}, {}, {}, {}
+        for a, k in enumerate("tp"):
+            spread = psum.tile([P, 4, P], F32, name="bank_p%d" % a)
+            for j in range(4):
+                nc.tensor.transpose(spread[:, j, :], gate_rows[k][:, j : j + 1].to_broadcast([P, P]), ident[:])
+            whole = sb("gate_" + k, [P, S], F32)
+            nc.scalar.copy(whole[:].rearrange("p (q j) -> p q j", j=4), spread[:].rearrange("p j q -> p q j"))
+            for e in range(E):
+                gate[k, e] = whole[:, e * C : (e + 1) * C]
 
         def load(item):
             kind = item[0]
@@ -213,7 +224,7 @@ def tile_moe_mmo_gelu_kernel(
             elif kind == "offs2":
                 nc.sync.dma_start(offs2_t[:], offs2)
             elif kind == "xw":
-                nc.sync.dma_start(xw[:], x_words.rearrange("s p t d -> p s (t d)").bitcast(I32))
+                nc.sync.dma_start(xw[item[1]][:], x_words[item[1]].rearrange("p t d -> p (t d)").bitcast(I32))
             elif kind == "zw":
                 nc.sync.dma_start(zw[:], z_words[0].rearrange("p t d -> p (t d)").bitcast(I32))
             elif kind == "w1w":
@@ -228,12 +239,6 @@ def tile_moe_mmo_gelu_kernel(
                 nc.sync.dma_start(t[:].bitcast(I32), w2_words[lo:hi].rearrange("e s p b -> p (e s) b").bitcast(I32))
                 for e in range(lo, hi):
                     w2w[e] = t[:, e - lo, :]
-            elif kind == "g":
-                k, lo, hi = item[1], item[2], item[3]
-                t = sb("g%s%d" % (k, lo), [P, (hi - lo) * C], F32)
-                nc.sync.dma_start(t[:], (gate1 if k == "t" else gate2)[:, lo * C : hi * C])
-                for e in range(lo, hi):
-                    gate[k, e] = t[:, (e - lo) * C : (e - lo + 1) * C]
             else:
                 e, part = item[1], item[2]
                 width = H // WZ_PARTS[e]
@@ -254,7 +259,7 @@ def tile_moe_mmo_gelu_kernel(
 
         def gxw(s, lo, hi):
             t = sg("xg%d_%d" % (s, lo), [P, (hi - lo) * C], U32, 4 * (hi - lo) * C)
-            nc.vector.tensor_copy(t[:], xw[:, s, :].bitcast(U32).indirect(offs_t[:, 8 * lo : 8 * hi]))
+            nc.vector.tensor_copy(t[:], xw[s][:].bitcast(U32).indirect(offs_t[:, 8 * lo : 8 * hi]))
             for e in range(lo, hi):
                 xg[s, e] = t[:, (e - lo) * C : (e - lo + 1) * C]
 
@@ -304,15 +309,13 @@ def tile_moe_mmo_gelu_kernel(
                 st["turned", e].rearrange("p u c -> p c u"),
             )
 
-        def cast(e, part):
-            if part == 0:
+        def cast(e, lo, hi, on):
+            if ("wz_bf", e) not in st:
                 st["wz_bf", e] = sg("wz_bf%d" % e, [P, 4 * H], BF16, 4096)
-            width = P // CAST_PARTS[e]
-            held, inside = divmod(part * width, P // WZ_PARTS[e])
-            engine = {"v": nc.vector.tensor_copy, "s": nc.scalar.copy, "g": nc.gpsimd.tensor_copy}[CAST_ON.get((e, part), "s")]
+            engine = {"v": nc.vector.tensor_copy, "s": nc.scalar.copy}[on]
             engine(
-                st["wz_bf", e][:].rearrange("p (t m j) -> p m j t", t=4, j=4)[:, part * width : (part + 1) * width],
-                wz_raw[e, held][:].rearrange("p j (m t) -> p m j t", t=4)[:, inside : inside + width],
+                st["wz_bf", e][:].rearrange("p (t m j) -> p m j t", t=4, j=4)[:, :, :, lo:hi],
+                wz_raw[e, 0][:].rearrange("p j (m t) -> p m j t", t=4)[:, :, :, lo:hi],
             )
 
         def qw(e):
@@ -323,7 +326,7 @@ def tile_moe_mmo_gelu_kernel(
 
         def mp(e):
             codes, scales = st["wzq", e]
-            acc = psum.tile([P, H], F32, name="bank_p%d" % e)
+            acc = psum.tile([P, H], F32, name=BANK.get(e, "bank_p%d" % e))
             st["acc_p", e] = acc
             for t in range(4):
                 nc.tensor.matmul_mx(

@@ -16,116 +16,20 @@ ADD = mybir.AluOpType.add
 IS_EQUAL = mybir.AluOpType.is_equal
 
 P = 128
-K, L, T, Q, E, C = 1024, 512, 768, 512, 4, 128
+K, L = 1024, 512
+T, Q = 768, 512
+E, C = 4, 128
 H, N = 512, 256
 S = E * C
 FLOPS = 2 * S * (K * H + L * H + 2 * H * N)
 
-LOADS = [
-    ("xw", 0),
-    ("offs",),
-    ("xw", 1),
-    ("xs",),
-    ("w1w", 0, 1),
-    ("w1s",),
-    ("offs2",),
-    ("w1w", 1, 2),
-    ("zw",),
-    ("w1w", 2, 4),
-    ("zs",),
-    ("w2w", 0, 2),
-    ("wz", 0, 0),
-    ("wz", 1, 0),
-    ("w2w", 2, 4),
-    ("wz", 2, 0),
-    ("wz", 3, 0),
-]
-STEPS = [
-    ("gxw", 0, 0, 4),
-    ("gxw", 1, 0, 4),
-    ("gxs", 0, 0, 1),
-    ("gxs", 1, 0, 1),
-    ("gxs", 0, 1, 2),
-    ("gxs", 1, 1, 2),
-    ("gxs", 0, 2, 4),
-    ("gxs", 1, 2, 4),
-    ("gzw", 0, 2),
-    ("gzw", 2, 4),
-    ("gzs", 0, 2),
-    ("gzs", 2, 4),
-    ("mt", 0),
-    ("mt", 1),
-    ("mt", 2),
-    ("mt", 3),
-    ("gt", 0),
-    ("gt", 1),
-    ("gt", 2),
-    ("gt", 3),
-    ("tt", 0),
-    ("ct", 0),
-    ("tt", 1),
-    ("ct", 1),
-    ("tt", 2),
-    ("ct", 2),
-    ("tt", 3),
-    ("ct", 3),
-    ("qh", "t", 0),
-    ("m2", "t", 0),
-    ("qh", "t", 1),
-    ("m2", "t", 1),
-    ("cast", 0, 0, 4, "v"),
-    ("qw", 0),
-    ("mp", 0),
-    ("qh", "t", 2),
-    ("m2", "t", 2),
-    ("qh", "t", 3),
-    ("m2", "t", 3),
-    ("ev", "t", 0),
-    ("sc", "t", 0),
-    ("ev", "t", 1),
-    ("sc", "t", 1),
-    ("cast", 1, 0, 4, "s"),
-    ("qw", 1),
-    ("mp", 1),
-    ("gp", 0),
-    ("qh", "p", 0),
-    ("m2", "p", 0),
-    ("ev", "t", 2),
-    ("sc", "t", 2),
-    ("ev", "t", 3),
-    ("sc", "t", 3),
-    ("cast", 2, 0, 4, "s"),
-    ("qw", 2),
-    ("mp", 2),
-    ("cast", 3, 2, 4, "v"),
-    ("gp", 1),
-    ("qh", "p", 1),
-    ("m2", "p", 1),
-    ("ev", "p", 0),
-    ("sc", "p", 0),
-    ("cast", 3, 0, 2, "s"),
-    ("qw", 3),
-    ("mp", 3),
-    ("gp", 2),
-    ("qh", "p", 2),
-    ("m2", "p", 2),
-    ("ev", "p", 1),
-    ("sc", "p", 1),
-    ("gp", 3),
-    ("qh", "p", 3),
-    ("m2", "p", 3),
-    ("ev", "p", 2),
-    ("sc", "p", 2),
-    ("ev", "p", 3),
-    ("sc", "p", 3),
-]
-WZ_PARTS = [1,1,1,1]
-CAST_PARTS = [1,1,1,1]
-CAST_ON = {}
-ON = {"h_scales_t0": ("zs", 0), "h_scales_t1": ("zs", 128), "h_scales_t2": ("wz_raw0_0", 2048), "h_scales_t3": ("wz_raw0_0", 3072), "sums_t0": ("wz_raw0_0", 0), "sums_t1": ("wz_raw0_0", 1024), "hidden_p0": ("wz_raw1_0", 0), "sums_t2": ("wz_raw1_0", 1024), "sums_t3": ("wz_raw1_0", 2048), "hidden_p1": ("wz_raw2_0", 0), "sums_p0": ("wz_raw2_0", 1024), "hidden_p2": ("wz_raw3_0", 0), "sums_p1": ("wz_raw3_0", 1024), "sums_p2": ("wz_codes3", 0)}
-BANK = {}
-POOL_PLANES = ["w2s"]
-ACT_PLANES = []
+QUADRANT = 32
+Z_PLANE_AT = 0
+LAST_WZ_CODES_AT = Z_PLANE_AT + Q
+RAW_AT = LAST_WZ_CODES_AT + 4 * H
+RAW_BYTES = 16 * H
+SEAT_BYTES = 2 * H
+LAST_ON_SCALAR = 2
 
 
 def tile_moe_mmo_gelu_kernel(
@@ -134,278 +38,248 @@ def tile_moe_mmo_gelu_kernel(
     nc = tc.nc
     with ExitStack() as ctx:
         keep = ctx.enter_context(tc.tile_pool(name="keep", bufs=1))
-        stage = ctx.enter_context(tc.tile_pool(name="stage", bufs=1))
+        shared = ctx.enter_context(tc.tile_pool(name="shared", bufs=1))
         psum = ctx.enter_context(tc.psum_pool(name="psum", bufs=1))
-        place = {}
-        top = [0]
 
-        def sb(name, shape, dtype):
+        def own(name, shape, dtype):
             return keep.tile(shape, dtype, name=name, align_bytes=64)
 
-        def sg(name, shape, dtype, size):
-            if name in ON:
-                host, shift = ON[name]
-                place[name] = place[host] + shift
-            else:
-                place[name] = top[0]
-                top[0] = top[0] + size
-            return stage.tile(shape, dtype, name=name, align_bytes=64, offset=place[name])
+        def on_bytes(offset):
+            def make(name, shape, dtype):
+                return shared.tile(shape, dtype, name=name, align_bytes=64, offset=offset)
 
-        offs_t = keep.tile([P, S // 16], U16, name="offs_t")
-        offs2_t = keep.tile([P, S // 16], U16, name="offs2_t")
-        xw = [sb("xw%d" % s, [P, T], I32) for s in range(2)]
-        xs = sb("xs", [P, 2, T], U8)
-        zw = sg("zw", [P, Q], I32, 4 * Q)
-        zs = sg("zs", [P, 1, Q], U8, Q)
-        w1s = sb("w1s", [P, 2 * E, H], U8)
-        w2s = sb("w2s", [P, E, N], U8)
-        ident = sb("ident", [P, P], F32)
-        ones = sb("ones", [P, 32], F32)
-        column = sb("column", [P, 32], F32)
-        row = sb("row", [P, 32], F32)
-        zero = sb("zero", [P, 1], F32)
-        out_text = [sb("out_text%d" % h, [P, T], F32) for h in range(2)]
-        out_patch = [sb("out_patch%d" % h, [P, Q], F32) for h in range(2)]
-        planes = {
-            "xs": (xs, x_scales.rearrange("s b t -> b s t")),
-            "zs": (zs, z_scales.rearrange("s b t -> b s t")),
-            "w1s": (w1s, w1_scales.rearrange("e s b i -> b (e s) i")),
-            "w2s": (w2s, w2_scales.rearrange("e s b n -> b (e s) n")),
+            return make
+
+        def after_rounding(e, seat):
+            return on_bytes(RAW_AT + e * RAW_BYTES + seat * SEAT_BYTES)
+
+        offsets = {k: keep.tile([P, S // 16], U16, name="offsets_" + k) for k in "tp"}
+        x_window = [own("x_window%d" % g, [P, T], I32) for g in range(2)]
+        z_window = own("z_window", [P, Q], I32)
+        x_plane = own("x_plane", [P, 2, T], U8)
+        z_plane = on_bytes(Z_PLANE_AT)("z_plane", [P, 1, Q], U8)
+        w1_plane = own("w1_plane", [P, 2 * E, H], U8)
+        w2_plane = own("w2_plane", [P, E, N], U8)
+        wz_raw = [on_bytes(RAW_AT + e * RAW_BYTES)("wz_raw%d" % e, [P, 4, H], F32) for e in range(E)]
+        result = {
+            "t": [own("result_t%d" % h, [P, T], F32) for h in range(2)],
+            "p": [own("result_p%d" % h, [P, Q], F32) for h in range(2)],
         }
 
-        def zero_plane(plane, engine):
-            engine.memset(plane[:].rearrange("p a w -> p (a w)").bitcast(I32), 0)
+        def zero_plane(plane):
+            nc.vector.memset(plane[:].rearrange("p a w -> p (a w)").bitcast(I32), 0)
 
-        def load_plane(name, queue):
-            plane, rows = planes[name]
+        def load_plane(queue, plane, rows):
             for r in range(4):
                 queue.dma_start(plane[r:P:32, :, :].bitcast(I32), rows[r:16:4, :, :].bitcast(I32))
 
-        zero_plane(xs, nc.vector)
-        gate_rows = {}
-        for k, source in (("t", gate1), ("p", gate2)):
-            gate_rows[k] = sb("gate_row_" + k, [P, 4], F32)
-            nc.gpsimd.dma_start(gate_rows[k][:], source[0].rearrange("(p j) -> p j", j=4))
-        for name in POOL_PLANES:
-            zero_plane(planes[name][0], nc.vector)
-            load_plane(name, nc.gpsimd)
+        zero_plane(x_plane)
+        gate1_row = own("gate1_row", [P, 4], F32)
+        nc.gpsimd.dma_start(gate1_row[:], gate1[0].rearrange("(p j) -> p j", j=4))
+        zero_plane(w2_plane)
+        load_plane(nc.gpsimd, w2_plane, w2_scales.rearrange("e g b n -> b (e g) n"))
+
+        zero = own("zero", [P, 1], F32)
+        ones = own("ones", [P, QUADRANT], F32)
+        column_number = own("column_number", [P, QUADRANT], F32)
+        row_number = own("row_number", [P, QUADRANT], F32)
+        identity = own("identity", [P, P], F32)
         nc.vector.memset(zero[:], 0.0)
         nc.vector.memset(ones[:], 1.0)
-        for name in ["w1s", "zs", "w2s"]:
-            if name not in POOL_PLANES:
-                zero_plane(planes[name][0], nc.vector)
-        for name in ACT_PLANES:
-            load_plane(name, nc.scalar)
-        nc.vector.tensor_tensor_scan(column[:], ones[:], ones[:], 0.0, MULT, ADD)
-        nc.vector.memset(ident[:], 0.0)
-        nc.vector.transpose(row[:], column[:])
-        for a in range(4):
-            rows = slice(32 * a, 32 * a + 32)
-            nc.vector.tensor_tensor(ident[rows, rows], column[rows, :], row[rows, :], IS_EQUAL)
+        zero_plane(w1_plane)
+        zero_plane(z_plane)
+        nc.vector.tensor_tensor_scan(column_number[:], ones[:], ones[:], 0.0, MULT, ADD)
+        nc.vector.memset(identity[:], 0.0)
+        nc.vector.transpose(row_number[:], column_number[:])
+        for a in range(P // QUADRANT):
+            rows = slice(QUADRANT * a, QUADRANT * (a + 1))
+            nc.vector.tensor_tensor(identity[rows, rows], column_number[rows, :], row_number[rows, :], IS_EQUAL)
+
         for h in range(2):
-            nc.scalar.activation(out_text[h][:], zero[:].to_broadcast([P, T]), GELU)
+            nc.scalar.activation(result["t"][h][:], zero[:].to_broadcast([P, T]), GELU)
 
-        w1w, w2w, gate, wz_raw = {}, {}, {}, {}
-        for a, k in enumerate("tp"):
-            spread = psum.tile([P, 4, P], F32, name="bank_p%d" % a)
-            for j in range(4):
-                nc.tensor.transpose(spread[:, j, :], gate_rows[k][:, j : j + 1].to_broadcast([P, P]), ident[:])
-            whole = sb("gate_" + k, [P, S], F32)
-            nc.scalar.copy(whole[:].rearrange("p (q j) -> p q j", j=4), spread[:].rearrange("p j q -> p q j"))
-            for e in range(E):
-                gate[k, e] = whole[:, e * C : (e + 1) * C]
+        gate = {k: own("gate_" + k, [P, S], F32) for k in "tp"}
+        spread = psum.tile([P, 4, P], F32, name="bank_p0")
+        for j in range(4):
+            nc.tensor.transpose(spread[:, j, :], gate1_row[:, j : j + 1].to_broadcast([P, P]), identity[:])
+        nc.scalar.copy(gate["t"][:].rearrange("p (q j) -> p q j", j=4), spread[:].rearrange("p j q -> p q j"))
 
-        def load(item):
-            kind = item[0]
-            if kind in planes:
-                load_plane(kind, nc.sync)
-            elif kind == "offs":
-                nc.sync.dma_start(offs_t[:], offs)
-            elif kind == "offs2":
-                nc.sync.dma_start(offs2_t[:], offs2)
-            elif kind == "xw":
-                nc.sync.dma_start(xw[item[1]][:], x_words[item[1]].rearrange("p t d -> p (t d)").bitcast(I32))
-            elif kind == "zw":
-                nc.sync.dma_start(zw[:], z_words[0].rearrange("p t d -> p (t d)").bitcast(I32))
-            elif kind == "w1w":
-                lo, hi = item[1], item[2]
-                t = sb("w1w%d" % lo, [P, 2 * (hi - lo), 2 * H], U8)
-                nc.sync.dma_start(t[:].bitcast(I32), w1_words[lo:hi].rearrange("e s p b -> p (e s) b").bitcast(I32))
-                for e in range(lo, hi):
-                    w1w[e] = t[:, 2 * (e - lo) : 2 * (e - lo) + 2, :]
-            elif kind == "w2w":
-                lo, hi = item[1], item[2]
-                t = sb("w2w%d" % lo, [P, hi - lo, 2 * N], U8)
-                nc.sync.dma_start(t[:].bitcast(I32), w2_words[lo:hi].rearrange("e s p b -> p (e s) b").bitcast(I32))
-                for e in range(lo, hi):
-                    w2w[e] = t[:, e - lo, :]
-            else:
-                e, part = item[1], item[2]
-                width = H // WZ_PARTS[e]
-                t = sg("wz_raw%d_%d" % (e, part), [P, 4, width], F32, 16 * width)
-                wz_raw[e, part] = t
-                nc.sync.dma_start(t[:], wz[e].rearrange("(p j) c -> p j c", j=4)[:, :, part * width : (part + 1) * width])
+        w1, w2 = {}, {}
 
-        for item in LOADS:
-            load(item)
-
-        xg, xsg, zg, zsg, st = {}, {}, {}, {}, {}
-
-        def gxs(s, lo, hi):
-            t = sg("xsg%d_%d" % (s, lo), [P, (hi - lo) * C], U8, (hi - lo) * C)
-            nc.vector.tensor_copy(t[:], xs[:, s, :].indirect(offs_t[:, 8 * lo : 8 * hi]))
+        def load_experts(views, name, words, lo, hi):
+            passes, row_bytes = words.shape[1], words.shape[3]
+            tile = own("%s_%d" % (name, lo), [P, (hi - lo) * passes, row_bytes], U8)
+            nc.sync.dma_start(tile[:].bitcast(I32), words[lo:hi].rearrange("e g p b -> p (e g) b").bitcast(I32))
             for e in range(lo, hi):
-                xsg[s, e] = t[:, (e - lo) * C : (e - lo + 1) * C]
+                views[e] = tile[:, (e - lo) * passes : (e - lo + 1) * passes, :]
 
-        def gxw(s, lo, hi):
-            t = sg("xg%d_%d" % (s, lo), [P, (hi - lo) * C], U32, 4 * (hi - lo) * C)
-            nc.vector.tensor_copy(t[:], xw[s][:].bitcast(U32).indirect(offs_t[:, 8 * lo : 8 * hi]))
-            for e in range(lo, hi):
-                xg[s, e] = t[:, (e - lo) * C : (e - lo + 1) * C]
+        def load_wz(e):
+            nc.sync.dma_start(wz_raw[e][:], wz[e].rearrange("(p j) i -> p j i", j=4))
 
-        def gzs(lo, hi):
-            t = sg("zsg%d" % lo, [P, (hi - lo) * C], U8, (hi - lo) * C)
-            nc.vector.tensor_copy(t[:], zs[:, 0, :].indirect(offs2_t[:, 8 * lo : 8 * hi]))
-            for e in range(lo, hi):
-                zsg[e] = t[:, (e - lo) * C : (e - lo + 1) * C]
+        nc.sync.dma_start(x_window[0][:], x_words[0].rearrange("p t d -> p (t d)").bitcast(I32))
+        nc.sync.dma_start(offsets["t"][:], offs)
+        nc.sync.dma_start(x_window[1][:], x_words[1].rearrange("p t d -> p (t d)").bitcast(I32))
+        load_plane(nc.sync, x_plane, x_scales.rearrange("g b t -> b g t"))
+        load_experts(w1, "w1", w1_words, 0, 1)
+        load_plane(nc.sync, w1_plane, w1_scales.rearrange("e g b i -> b (e g) i"))
+        nc.sync.dma_start(offsets["p"][:], offs2)
+        load_experts(w1, "w1", w1_words, 1, 2)
+        nc.sync.dma_start(z_window[:], z_words[0].rearrange("p t d -> p (t d)").bitcast(I32))
+        load_experts(w1, "w1", w1_words, 2, E)
+        load_plane(nc.sync, z_plane, z_scales.rearrange("g b t -> b g t"))
+        load_experts(w2, "w2", w2_words, 0, 2)
+        load_wz(0)
+        load_wz(1)
+        load_experts(w2, "w2", w2_words, 2, E)
+        load_wz(2)
+        load_wz(3)
+        nc.sync.dma_start(gate["p"][:], gate2)
 
-        def gzw(lo, hi):
-            t = sg("zg%d" % lo, [P, (hi - lo) * C], U32, 4 * (hi - lo) * C)
-            nc.vector.tensor_copy(t[:], zw[:].bitcast(U32).indirect(offs2_t[:, 8 * lo : 8 * hi]))
-            for e in range(lo, hi):
-                zg[e] = t[:, (e - lo) * C : (e - lo + 1) * C]
+        def gather(name, window, k, dtype, groups):
+            views = []
+            for lo, hi in groups:
+                slots = own("%s%d" % (name, lo), [P, (hi - lo) * C], dtype)
+                nc.vector.tensor_copy(slots[:], window.indirect(offsets[k][:, 8 * lo : 8 * hi]))
+                views = views + [slots[:, e * C : (e + 1) * C] for e in range(hi - lo)]
+            return views
 
-        def mt(e):
-            acc = psum.tile([P, H], F32, name="bank_t%d" % e)
-            st["acc_t", e] = acc
-            for s in range(2):
+        x_slots = [gather("x_slots%d_" % g, x_window[g][:].bitcast(U32), "t", U32, [(0, E)]) for g in range(2)]
+        x_slot_scales = [[], []]
+        for group in [(0, 1), (1, 2), (2, E)]:
+            for g in range(2):
+                x_slot_scales[g] = x_slot_scales[g] + gather("x_slot_scales%d_" % g, x_plane[:, g, :], "t", U8, [group])
+        halves = [(0, E // 2), (E // 2, E)]
+        z_slots = gather("z_slots", z_window[:].bitcast(U32), "p", U32, halves)
+        z_slot_scales = gather("z_slot_scales", z_plane[:, 0, :], "p", U8, halves)
+
+        bank, hidden, sums_in_psum, wz_rounded = {}, {}, {}, {}
+
+        def text_product(e):
+            bank["t", e] = psum.tile([P, H], F32, name="bank_t%d" % e)
+            for g in range(2):
                 nc.tensor.matmul_mx(
-                    out=acc[:],
-                    lhsT=xg[s, e].bitcast(FP8X4),
-                    lhsT_scale=xsg[s, e],
-                    rhs=w1w[e][:, s, :].bitcast(FP4X4),
-                    rhs_scale=w1s[:, 2 * e + s, :],
-                    start=(s == 0),
-                    stop=(s == 1),
+                    out=bank["t", e][:],
+                    lhsT=x_slots[g][e].bitcast(FP8X4),
+                    lhsT_scale=x_slot_scales[g][e],
+                    rhs=w1[e][:, g, :].bitcast(FP4X4),
+                    rhs_scale=w1_plane[:, 2 * e + g, :],
+                    start=(g == 0),
+                    stop=(g == 1),
                 )
 
-        def gt(e):
-            hrow = sg("hrow%d" % e, [P, 2, P, 2], BF16, 1024)
-            st["hrow", e] = hrow
-            nc.scalar.activation(hrow[:], st["acc_t", e][:].rearrange("c (p u k) -> c u p k", u=2, k=2), GELU)
+        def text_gelu(e):
+            pairs = own("pairs%d" % e, [P, 2, P, 2], BF16)
+            nc.scalar.activation(pairs[:], bank["t", e][:].rearrange("c (p u v) -> c u p v", u=2, v=2), GELU)
+            return pairs
 
-        def tt(e):
-            turned = st["acc_t", e][:, 0 : 2 * C].rearrange("p (u c) -> p u c", u=2)
-            st["turned", e] = turned
-            words = st["hrow", e][:].rearrange("c u p k -> c (u p k)").bitcast(F32)
+        def text_turn(e, pairs):
+            turned = bank["t", e][:, 0 : 2 * C].rearrange("p (u c) -> p u c", u=2)
+            words = pairs[:].rearrange("c u p v -> c (u p v)").bitcast(F32)
             for u in range(2):
-                nc.tensor.transpose(turned[:, u, :], words[:, u * P : (u + 1) * P], ident[:])
-
-        def ct(e):
-            hidden = sg("hidden_t%d" % e, [P, C * 4], BF16, 1024)
-            st["hidden", "t", e] = hidden
+                nc.tensor.transpose(turned[:, u, :], words[:, u * P : (u + 1) * P], identity[:])
+            hidden["t", e] = own("hidden_t%d" % e, [P, 4 * C], BF16)
             nc.scalar.copy(
-                hidden[:].bitcast(F32).rearrange("p (c u) -> p c u", u=2),
-                st["turned", e].rearrange("p u c -> p c u"),
+                hidden["t", e][:].bitcast(F32).rearrange("p (c u) -> p c u", u=2), turned.rearrange("p u c -> p c u")
             )
 
-        def cast(e, lo, hi, on):
-            if ("wz_bf", e) not in st:
-                st["wz_bf", e] = sg("wz_bf%d" % e, [P, 4 * H], BF16, 4096)
-            engine = {"v": nc.vector.tensor_copy, "s": nc.scalar.copy}[on]
-            engine(
-                st["wz_bf", e][:].rearrange("p (t m j) -> p m j t", t=4, j=4)[:, :, :, lo:hi],
-                wz_raw[e, 0][:].rearrange("p j (m t) -> p m j t", t=4)[:, :, :, lo:hi],
+        def round_wz(e, copy, lo, hi):
+            if e not in wz_rounded:
+                wz_rounded[e] = own("wz_rounded%d" % e, [P, 4 * H], BF16)
+            copy(
+                wz_rounded[e][:].rearrange("p (t m j) -> p m j t", t=4, j=4)[:, :, :, lo:hi],
+                wz_raw[e][:].rearrange("p j (m t) -> p m j t", t=4)[:, :, :, lo:hi],
             )
 
-        def qw(e):
-            codes = sg("wz_codes%d" % e, [P, H], U32, 2048)
-            scales = sg("wz_scales%d" % e, [P, H], U8, 512)
-            st["wzq", e] = (codes, scales)
-            nc.vector.quantize_mx(out=codes[:].bitcast(FP8X4), scales=scales[:], in_=st["wz_bf", e][:])
-
-        def mp(e):
-            codes, scales = st["wzq", e]
-            acc = psum.tile([P, H], F32, name=BANK.get(e, "bank_p%d" % e))
-            st["acc_p", e] = acc
+        def patch_product(e, make):
+            codes = make("wz_codes%d" % e, [P, H], U32)
+            scales = own("wz_scales%d" % e, [P, H], U8)
+            nc.vector.quantize_mx(out=codes[:].bitcast(FP8X4), scales=scales[:], in_=wz_rounded[e][:])
+            bank["p", e] = psum.tile([P, H], F32, name="bank_p%d" % e)
             for t in range(4):
                 nc.tensor.matmul_mx(
-                    out=acc[:, t * C : (t + 1) * C],
+                    out=bank["p", e][:, t * C : (t + 1) * C],
                     lhsT=codes[:, t * P : (t + 1) * P].bitcast(FP8X4),
                     lhsT_scale=scales[:, t * P : (t + 1) * P],
-                    rhs=zg[e].bitcast(FP8X4),
-                    rhs_scale=zsg[e],
+                    rhs=z_slots[e].bitcast(FP8X4),
+                    rhs_scale=z_slot_scales[e],
                     start=True,
                     stop=True,
                 )
 
-        def gp(e):
-            hidden = sg("hidden_p%d" % e, [P, C * 4], BF16, 1024)
-            st["hidden", "p", e] = hidden
+        def patch_gelu(e, make):
+            hidden["p", e] = make("hidden_p%d" % e, [P, 4 * C], BF16)
             nc.scalar.activation(
-                hidden[:].rearrange("p (c t) -> p c t", t=4), st["acc_p", e][:].rearrange("p (t c) -> p c t", t=4), GELU
+                hidden["p", e][:].rearrange("p (c t) -> p c t", t=4),
+                bank["p", e][:].rearrange("p (t c) -> p c t", t=4),
+                GELU,
             )
 
-        def qh(k, e):
-            codes = sg("h_codes_%s%d" % (k, e), [P, C], U32, 512)
-            scales = sg("h_scales_%s%d" % (k, e), [P, C], U8, 128)
-            st["hq", k, e] = (codes, scales)
-            nc.vector.quantize_mx(out=codes[:].bitcast(FP8X4), scales=scales[:], in_=st["hidden", k, e][:])
-
-        def m2(k, e):
-            codes, scales = st["hq", k, e]
-            acc = st["acc_" + k, e][:, 2 * C : 4 * C].rearrange("p (h c) -> p h c", h=2)
-            st["acc2", k, e] = acc
+        def second_product(k, e, make):
+            codes = own("hidden_codes_%s%d" % (k, e), [P, C], U32)
+            scales = make("hidden_scales_%s%d" % (k, e), [P, C], U8)
+            nc.vector.quantize_mx(out=codes[:].bitcast(FP8X4), scales=scales[:], in_=hidden[k, e][:])
+            sums_in_psum[k, e] = bank[k, e][:, 2 * C : 4 * C].rearrange("p (h c) -> p h c", h=2)
             for h in range(2):
                 nc.tensor.matmul_mx(
-                    out=acc[:, h, :],
-                    lhsT=w2w[e][:, 2 * P * h : 2 * P * (h + 1)].bitcast(FP4X4),
-                    lhsT_scale=w2s[:, e, P * h : P * (h + 1)],
+                    out=sums_in_psum[k, e][:, h, :],
+                    lhsT=w2[e][:, 0, 2 * P * h : 2 * P * (h + 1)].bitcast(FP4X4),
+                    lhsT_scale=w2_plane[:, e, P * h : P * (h + 1)],
                     rhs=codes[:].bitcast(FP8X4),
                     rhs_scale=scales[:],
                     start=True,
                     stop=True,
                 )
 
-        def ev(k, e):
-            sums = sg("sums_%s%d" % (k, e), [P, 2, C], F32, 1024)
-            st["sums", k, e] = sums
-            nc.scalar.copy(sums[:], st["acc2", k, e])
-
-        def sch(k, e, h):
-            window, offsets = (out_text, offs_t) if k == "t" else (out_patch, offs2_t)
-            nc.vector.tensor_tensor(
-                window[h][:].indirect(offsets[:, 8 * e : 8 * e + 8]), st["sums", k, e][:, h, :], gate[k, e], MULT
-            )
-            if e == E - 1:
-                columns = slice(0, T) if k == "t" else slice(T, T + Q)
-                nc.sync.dma_start(out[h * P : (h + 1) * P, columns], window[h][:])
-
-        def sc(k, e):
+        def scatter(k, e, make):
+            sums = make("sums_%s%d" % (k, e), [P, 2, C], F32)
+            nc.scalar.copy(sums[:], sums_in_psum[k, e])
+            columns = slice(0, T) if k == "t" else slice(T, T + Q)
             for h in range(2):
-                sch(k, e, h)
+                nc.vector.tensor_tensor(
+                    result[k][h][:].indirect(offsets[k][:, 8 * e : 8 * e + 8]),
+                    sums[:, h, :],
+                    gate[k][:, e * C : (e + 1) * C],
+                    MULT,
+                )
+                if e == E - 1:
+                    nc.sync.dma_start(out[h * P : (h + 1) * P, columns], result[k][h][:])
 
-        def text(e):
-            mt(e)
-            gt(e)
-            tt(e)
-            ct(e)
-            qh("t", e)
-            m2("t", e)
-            ev("t", e)
+        for e in range(E):
+            text_product(e)
+        pairs_of = [text_gelu(e) for e in range(E)]
+        for e in range(E):
+            text_turn(e, pairs_of[e])
 
-        def patch(e):
-            qw(e)
-            mp(e)
-            gp(e)
-            qh("p", e)
-            m2("p", e)
-            ev("p", e)
+        for e in range(2):
+            second_product("t", e, on_bytes(Z_PLANE_AT + e * C))
+        round_wz(0, nc.vector.tensor_copy, 0, 4)
+        patch_product(0, own)
+        for e in range(2, E):
+            second_product("t", e, after_rounding(0, e))
+        for e in range(2):
+            scatter("t", e, after_rounding(0, e))
 
-        def casts(e):
-            for part in range(CAST_PARTS[e]):
-                cast(e, part)
+        round_wz(1, nc.scalar.copy, 0, 4)
+        patch_product(1, own)
+        patch_gelu(0, after_rounding(1, 0))
+        second_product("p", 0, own)
+        for e in range(2, E):
+            scatter("t", e, after_rounding(1, e - 1))
 
-        steps = {"mt": mt, "gt": gt, "tt": tt, "ct": ct, "qh": qh, "m2": m2, "ev": ev, "cast": cast, "qw": qw, "mp": mp, "gp": gp, "gxs": gxs, "gxw": gxw, "gzs": gzs, "gzw": gzw, "text": text, "patch": patch, "casts": casts, "sc": sc, "sch": sch}
-        for step in STEPS:
-            steps[step[0]](*step[1:])
+        round_wz(2, nc.scalar.copy, 0, 4)
+        patch_product(2, own)
+        round_wz(3, nc.vector.tensor_copy, LAST_ON_SCALAR, 4)
+        patch_gelu(1, after_rounding(2, 0))
+        second_product("p", 1, own)
+        scatter("p", 0, after_rounding(2, 1))
+
+        round_wz(3, nc.scalar.copy, 0, LAST_ON_SCALAR)
+        patch_product(3, on_bytes(LAST_WZ_CODES_AT))
+        patch_gelu(2, after_rounding(3, 0))
+        second_product("p", 2, own)
+        scatter("p", 1, after_rounding(3, 1))
+
+        patch_gelu(3, own)
+        second_product("p", 3, own)
+        scatter("p", 2, on_bytes(LAST_WZ_CODES_AT))
+        scatter("p", 3, own)

@@ -28,8 +28,8 @@ Z_PLANE_AT = 0
 LAST_WZ_CODES_AT = Z_PLANE_AT + Q
 RAW_AT = LAST_WZ_CODES_AT + 4 * H
 RAW_BYTES = 16 * H
-SEAT_BYTES = 2 * H
-LAST_ON_SCALAR = 2
+SEAT_BYTES = 4 * H
+LAST_ON_SCALAR = 3
 
 
 def tile_moe_mmo_gelu_kernel(
@@ -177,10 +177,10 @@ def tile_moe_mmo_gelu_kernel(
             words = pairs[:].rearrange("c u p v -> c (u p v)").bitcast(F32)
             for u in range(2):
                 nc.tensor.transpose(turned[:, u, :], words[:, u * P : (u + 1) * P], identity[:])
-            hidden["t", e] = own("hidden_t%d" % e, [P, 4 * C], BF16)
-            nc.scalar.copy(
-                hidden["t", e][:].bitcast(F32).rearrange("p (c u) -> p c u", u=2), turned.rearrange("p u c -> p c u")
-            )
+            if e % 2 == 0:
+                hidden["t", e] = own("hidden_t%d" % e, [P, 2 * 4 * C], BF16)
+            half = hidden["t", e - e % 2][:, (e % 2) * 4 * C : (e % 2 + 1) * 4 * C]
+            nc.scalar.copy(half.bitcast(F32).rearrange("p (c u) -> p c u", u=2), turned.rearrange("p u c -> p c u"))
 
         def round_wz(e, copy, lo, hi):
             if e not in wz_rounded:
@@ -214,34 +214,37 @@ def tile_moe_mmo_gelu_kernel(
                 GELU,
             )
 
-        def second_product(k, e, make):
-            codes = own("hidden_codes_%s%d" % (k, e), [P, C], U32)
-            scales = make("hidden_scales_%s%d" % (k, e), [P, C], U8)
-            nc.vector.quantize_mx(out=codes[:].bitcast(FP8X4), scales=scales[:], in_=hidden[k, e][:])
-            sums_in_psum[k, e] = bank[k, e][:, 2 * C : 4 * C].rearrange("p (h c) -> p h c", h=2)
-            for h in range(2):
-                nc.tensor.matmul_mx(
-                    out=sums_in_psum[k, e][:, h, :],
-                    lhsT=w2[e][:, 0, 2 * P * h : 2 * P * (h + 1)].bitcast(FP4X4),
-                    lhsT_scale=w2_plane[:, e, P * h : P * (h + 1)],
-                    rhs=codes[:].bitcast(FP8X4),
-                    rhs_scale=scales[:],
-                    start=True,
-                    stop=True,
-                )
+        def second_product(k, lo, hi, make):
+            width = (hi - lo) * C
+            codes = own("hidden_codes_%s%d" % (k, lo), [P, width], U32)
+            scales = make("hidden_scales_%s%d" % (k, lo), [P, width], U8)
+            nc.vector.quantize_mx(out=codes[:].bitcast(FP8X4), scales=scales[:], in_=hidden[k, lo][:])
+            sums_in_psum[k, lo] = bank[k, lo][:, H - 2 * width : H].rearrange("p (h c) -> p h c", h=2)
+            for e in range(lo, hi):
+                slots = slice((e - lo) * C, (e - lo + 1) * C)
+                for h in range(2):
+                    nc.tensor.matmul_mx(
+                        out=sums_in_psum[k, lo][:, h, slots],
+                        lhsT=w2[e][:, 0, 2 * P * h : 2 * P * (h + 1)].bitcast(FP4X4),
+                        lhsT_scale=w2_plane[:, e, P * h : P * (h + 1)],
+                        rhs=codes[:, slots].bitcast(FP8X4),
+                        rhs_scale=scales[:, slots],
+                        start=True,
+                        stop=True,
+                    )
 
-        def scatter(k, e, make):
-            sums = make("sums_%s%d" % (k, e), [P, 2, C], F32)
-            nc.scalar.copy(sums[:], sums_in_psum[k, e])
+        def scatter(k, lo, hi, make):
+            sums = make("sums_%s%d" % (k, lo), [P, 2, (hi - lo) * C], F32)
+            nc.scalar.copy(sums[:], sums_in_psum[k, lo])
             columns = slice(0, T) if k == "t" else slice(T, T + Q)
             for h in range(2):
                 nc.vector.tensor_tensor(
-                    result[k][h][:].indirect(offsets[k][:, 8 * e : 8 * e + 8]),
+                    result[k][h][:].indirect(offsets[k][:, 8 * lo : 8 * hi]),
                     sums[:, h, :],
-                    gate[k][:, e * C : (e + 1) * C],
+                    gate[k][:, lo * C : hi * C],
                     MULT,
                 )
-                if e == E - 1:
+                if hi == E:
                     nc.sync.dma_start(out[h * P : (h + 1) * P, columns], result[k][h][:])
 
         for e in range(E):
@@ -250,36 +253,32 @@ def tile_moe_mmo_gelu_kernel(
         for e in range(E):
             text_turn(e, pairs_of[e])
 
-        for e in range(2):
-            second_product("t", e, on_bytes(Z_PLANE_AT + e * C))
+        second_product("t", 0, 2, on_bytes(Z_PLANE_AT))
         round_wz(0, nc.vector.tensor_copy, 0, 4)
         patch_product(0, own)
-        for e in range(2, E):
-            second_product("t", e, after_rounding(0, e))
-        for e in range(2):
-            scatter("t", e, after_rounding(0, e))
+        second_product("t", 2, E, after_rounding(0, 0))
+        scatter("t", 0, 2, after_rounding(0, 1))
 
         round_wz(1, nc.scalar.copy, 0, 4)
         patch_product(1, own)
         patch_gelu(0, after_rounding(1, 0))
-        second_product("p", 0, own)
-        for e in range(2, E):
-            scatter("t", e, after_rounding(1, e - 1))
+        second_product("p", 0, 1, own)
+        scatter("t", 2, E, after_rounding(1, 1))
 
         round_wz(2, nc.scalar.copy, 0, 4)
         patch_product(2, own)
         round_wz(3, nc.vector.tensor_copy, LAST_ON_SCALAR, 4)
         patch_gelu(1, after_rounding(2, 0))
-        second_product("p", 1, own)
-        scatter("p", 0, after_rounding(2, 1))
+        second_product("p", 1, 2, own)
+        scatter("p", 0, 1, after_rounding(2, 1))
 
         round_wz(3, nc.scalar.copy, 0, LAST_ON_SCALAR)
         patch_product(3, on_bytes(LAST_WZ_CODES_AT))
         patch_gelu(2, after_rounding(3, 0))
-        second_product("p", 2, own)
-        scatter("p", 1, after_rounding(3, 1))
+        second_product("p", 2, 3, own)
+        scatter("p", 1, 2, after_rounding(3, 1))
 
         patch_gelu(3, own)
-        second_product("p", 3, own)
-        scatter("p", 2, on_bytes(LAST_WZ_CODES_AT))
-        scatter("p", 3, own)
+        second_product("p", 3, E, own)
+        scatter("p", 2, 3, on_bytes(LAST_WZ_CODES_AT))
+        scatter("p", 3, E, own)

@@ -29,7 +29,7 @@ LAST_WZ_CODES_AT = Z_PLANE_AT + Q
 RAW_AT = LAST_WZ_CODES_AT + 4 * H
 RAW_BYTES = 16 * H
 SEAT_BYTES = 4 * H
-LAST_ON_SCALAR = 3
+LAST_ON_SCALAR = 2
 
 
 def tile_moe_mmo_gelu_kernel(
@@ -74,8 +74,10 @@ def tile_moe_mmo_gelu_kernel(
                 queue.dma_start(plane[r:P:32, :, :].bitcast(I32), rows[r:16:4, :, :].bitcast(I32))
 
         zero_plane(x_plane)
-        gate1_row = own("gate1_row", [P, 4], F32)
-        nc.gpsimd.dma_start(gate1_row[:], gate1[0].rearrange("(p j) -> p j", j=4))
+        gate_row = {}
+        for k, source in (("t", gate1), ("p", gate2)):
+            gate_row[k] = own("gate_row_" + k, [P, 4], F32)
+            nc.gpsimd.dma_start(gate_row[k][:], source[0].rearrange("(q j) -> q j", j=4))
         zero_plane(w2_plane)
         load_plane(nc.gpsimd, w2_plane, w2_scales.rearrange("e g b n -> b (e g) n"))
 
@@ -98,11 +100,13 @@ def tile_moe_mmo_gelu_kernel(
         for h in range(2):
             nc.scalar.activation(result["t"][h][:], zero[:].to_broadcast([P, T]), GELU)
 
-        gate = {k: own("gate_" + k, [P, S], F32) for k in "tp"}
-        spread = psum.tile([P, 4, P], F32, name="bank_p0")
-        for j in range(4):
-            nc.tensor.transpose(spread[:, j, :], gate1_row[:, j : j + 1].to_broadcast([P, P]), identity[:])
-        nc.scalar.copy(gate["t"][:].rearrange("p (q j) -> p q j", j=4), spread[:].rearrange("p j q -> p q j"))
+        gate = {}
+        for a, k in enumerate("tp"):
+            spread = psum.tile([P, 4, P], F32, name="bank_p%d" % a)
+            for j in range(4):
+                nc.tensor.transpose(spread[:, j, :], gate_row[k][:, j : j + 1].to_broadcast([P, P]), identity[:])
+            gate[k] = own("gate_" + k, [P, S], F32)
+            nc.scalar.copy(gate[k][:].rearrange("p (q j) -> p q j", j=4), spread[:].rearrange("p j q -> p q j"))
 
         w1, w2 = {}, {}
 
@@ -133,7 +137,6 @@ def tile_moe_mmo_gelu_kernel(
         load_experts(w2, "w2", w2_words, 2, E)
         load_wz(2)
         load_wz(3)
-        nc.sync.dma_start(gate["p"][:], gate2)
 
         def gather(name, window, k, dtype, groups):
             views = []

@@ -25,11 +25,14 @@ FLOPS = 2 * S * (K * H + L * H + 2 * H * N)
 
 QUADRANT = 32
 Z_PLANE_AT = 0
-LAST_WZ_CODES_AT = Z_PLANE_AT + Q
-RAW_AT = LAST_WZ_CODES_AT + 4 * H
+TEXT_CODES_AT = Z_PLANE_AT + Q
+ROUNDED_AT = TEXT_CODES_AT + 4 * 2 * C
+RAW_AT = ROUNDED_AT + 8 * H
 RAW_BYTES = 16 * H
 SEAT_BYTES = 4 * H
-LAST_ON_SCALAR = 2
+LAST_ON_SCALAR = 64
+FIRST_PIECE_1 = 96
+FIRST_PIECE_2 = 48
 
 
 def tile_moe_mmo_gelu_kernel(
@@ -74,10 +77,8 @@ def tile_moe_mmo_gelu_kernel(
                 queue.dma_start(plane[r:P:32, :, :].bitcast(I32), rows[r:16:4, :, :].bitcast(I32))
 
         zero_plane(x_plane)
-        gate_row = {}
-        for k, source in (("t", gate1), ("p", gate2)):
-            gate_row[k] = own("gate_row_" + k, [P, 4], F32)
-            nc.gpsimd.dma_start(gate_row[k][:], source[0].rearrange("(q j) -> q j", j=4))
+        gate_row = own("gate_row", [P, 4], F32)
+        nc.gpsimd.dma_start(gate_row[:], gate1[0].rearrange("(q j) -> q j", j=4))
         zero_plane(w2_plane)
         load_plane(nc.gpsimd, w2_plane, w2_scales.rearrange("e g b n -> b (e g) n"))
 
@@ -100,13 +101,11 @@ def tile_moe_mmo_gelu_kernel(
         for h in range(2):
             nc.scalar.activation(result["t"][h][:], zero[:].to_broadcast([P, T]), GELU)
 
-        gate = {}
-        for a, k in enumerate("tp"):
-            spread = psum.tile([P, 4, P], F32, name="bank_p%d" % a)
-            for j in range(4):
-                nc.tensor.transpose(spread[:, j, :], gate_row[k][:, j : j + 1].to_broadcast([P, P]), identity[:])
-            gate[k] = own("gate_" + k, [P, S], F32)
-            nc.scalar.copy(gate[k][:].rearrange("p (q j) -> p q j", j=4), spread[:].rearrange("p j q -> p q j"))
+        gate = {k: own("gate_" + k, [P, S], F32) for k in "tp"}
+        spread = psum.tile([P, 4, P], F32, name="bank_p0")
+        for j in range(4):
+            nc.tensor.transpose(spread[:, j, :], gate_row[:, j : j + 1].to_broadcast([P, P]), identity[:])
+        nc.scalar.copy(gate["t"][:].rearrange("p (q j) -> p q j", j=4), spread[:].rearrange("p j q -> p q j"))
 
         w1, w2 = {}, {}
 
@@ -131,12 +130,13 @@ def tile_moe_mmo_gelu_kernel(
         nc.sync.dma_start(z_window[:], z_words[0].rearrange("p t d -> p (t d)").bitcast(I32))
         load_experts(w1, "w1", w1_words, 2, E)
         load_plane(nc.sync, z_plane, z_scales.rearrange("g b t -> b g t"))
-        load_experts(w2, "w2", w2_words, 0, 2)
         load_wz(0)
+        load_experts(w2, "w2", w2_words, 0, 2)
         load_wz(1)
         load_experts(w2, "w2", w2_words, 2, E)
         load_wz(2)
         load_wz(3)
+        nc.sync.dma_start(gate["p"][:], gate2)
 
         def gather(name, window, k, dtype, groups):
             views = []
@@ -185,16 +185,16 @@ def tile_moe_mmo_gelu_kernel(
             half = hidden["t", e - e % 2][:, (e % 2) * 4 * C : (e % 2 + 1) * 4 * C]
             nc.scalar.copy(half.bitcast(F32).rearrange("p (c u) -> p c u", u=2), turned.rearrange("p u c -> p c u"))
 
-        def round_wz(e, copy, lo, hi):
+        def round_wz(e, copy, lo, hi, make=own):
             if e not in wz_rounded:
-                wz_rounded[e] = own("wz_rounded%d" % e, [P, 4 * H], BF16)
+                wz_rounded[e] = make("wz_rounded%d" % e, [P, 4 * H], BF16)
             copy(
-                wz_rounded[e][:].rearrange("p (t m j) -> p m j t", t=4, j=4)[:, :, :, lo:hi],
-                wz_raw[e][:].rearrange("p j (m t) -> p m j t", t=4)[:, :, :, lo:hi],
+                wz_rounded[e][:].rearrange("p (t m j) -> p m j t", t=4, j=4)[:, lo:hi, :, :],
+                wz_raw[e][:].rearrange("p j (m t) -> p m j t", t=4)[:, lo:hi, :, :],
             )
 
-        def patch_product(e, make):
-            codes = make("wz_codes%d" % e, [P, H], U32)
+        def patch_product(e):
+            codes = own("wz_codes%d" % e, [P, H], U32)
             scales = own("wz_scales%d" % e, [P, H], U8)
             nc.vector.quantize_mx(out=codes[:].bitcast(FP8X4), scales=scales[:], in_=wz_rounded[e][:])
             bank["p", e] = psum.tile([P, H], F32, name="bank_p%d" % e)
@@ -217,9 +217,9 @@ def tile_moe_mmo_gelu_kernel(
                 GELU,
             )
 
-        def second_product(k, lo, hi, make):
+        def second_product(k, lo, hi, make, make_codes=own):
             width = (hi - lo) * C
-            codes = own("hidden_codes_%s%d" % (k, lo), [P, width], U32)
+            codes = make_codes("hidden_codes_%s%d" % (k, lo), [P, width], U32)
             scales = make("hidden_scales_%s%d" % (k, lo), [P, width], U8)
             nc.vector.quantize_mx(out=codes[:].bitcast(FP8X4), scales=scales[:], in_=hidden[k, lo][:])
             sums_in_psum[k, lo] = bank[k, lo][:, H - 2 * width : H].rearrange("p (h c) -> p h c", h=2)
@@ -236,14 +236,14 @@ def tile_moe_mmo_gelu_kernel(
                         stop=True,
                     )
 
-        def scatter(k, lo, hi, make):
-            sums = make("sums_%s%d" % (k, lo), [P, 2, (hi - lo) * C], F32)
-            nc.scalar.copy(sums[:], sums_in_psum[k, lo])
+        def scatter(k, lo, hi, make, h0=0, h1=2):
+            sums = make("sums_%s%d_%d" % (k, lo, h0), [P, h1 - h0, (hi - lo) * C], F32)
+            nc.scalar.copy(sums[:], sums_in_psum[k, lo][:, h0:h1, :])
             columns = slice(0, T) if k == "t" else slice(T, T + Q)
-            for h in range(2):
+            for h in range(h0, h1):
                 nc.vector.tensor_tensor(
                     result[k][h][:].indirect(offsets[k][:, 8 * lo : 8 * hi]),
-                    sums[:, h, :],
+                    sums[:, h - h0, :],
                     gate[k][:, lo * C : hi * C],
                     MULT,
                 )
@@ -257,31 +257,34 @@ def tile_moe_mmo_gelu_kernel(
             text_turn(e, pairs_of[e])
 
         second_product("t", 0, 2, on_bytes(Z_PLANE_AT))
-        round_wz(0, nc.vector.tensor_copy, 0, 4)
-        patch_product(0, own)
-        second_product("t", 2, E, after_rounding(0, 0))
-        scatter("t", 0, 2, after_rounding(0, 1))
+        round_wz(0, nc.vector.tensor_copy, 0, P)
+        patch_product(0)
+        second_product("t", 2, E, after_rounding(0, 0), on_bytes(TEXT_CODES_AT))
+        scatter("t", 0, 2, own)
 
-        round_wz(1, nc.scalar.copy, 0, 4)
-        patch_product(1, own)
-        patch_gelu(0, after_rounding(1, 0))
+        round_wz(1, nc.scalar.copy, 0, FIRST_PIECE_1, on_bytes(ROUNDED_AT))
+        scatter("t", 2, E, own, 0, 1)
+        patch_gelu(0, on_bytes(TEXT_CODES_AT))
         second_product("p", 0, 1, own)
-        scatter("t", 2, E, after_rounding(1, 1))
+        round_wz(1, nc.scalar.copy, FIRST_PIECE_1, P)
+        patch_product(1)
 
-        round_wz(2, nc.scalar.copy, 0, 4)
-        patch_product(2, own)
-        round_wz(3, nc.vector.tensor_copy, LAST_ON_SCALAR, 4)
-        patch_gelu(1, after_rounding(2, 0))
+        round_wz(2, nc.scalar.copy, 0, FIRST_PIECE_2)
+        scatter("t", 2, E, after_rounding(1, 0), 1, 2)
+        round_wz(2, nc.scalar.copy, FIRST_PIECE_2, P)
+        round_wz(3, nc.vector.tensor_copy, LAST_ON_SCALAR, P)
+        patch_product(2)
+        patch_gelu(1, own)
         second_product("p", 1, 2, own)
-        scatter("p", 0, 1, after_rounding(2, 1))
+        scatter("p", 0, 1, on_bytes(ROUNDED_AT), 0, 1)
 
         round_wz(3, nc.scalar.copy, 0, LAST_ON_SCALAR)
-        patch_product(3, on_bytes(LAST_WZ_CODES_AT))
-        patch_gelu(2, after_rounding(3, 0))
+        patch_product(3)
+        scatter("p", 0, 1, on_bytes(ROUNDED_AT + 4 * C), 1, 2)
+        patch_gelu(2, own)
         second_product("p", 2, 3, own)
-        scatter("p", 1, 2, after_rounding(3, 1))
-
+        scatter("p", 1, 2, own)
         patch_gelu(3, own)
         second_product("p", 3, E, own)
-        scatter("p", 2, 3, on_bytes(LAST_WZ_CODES_AT))
+        scatter("p", 2, 3, own)
         scatter("p", 3, E, own)

@@ -25,14 +25,12 @@ FLOPS = 2 * S * (K * H + L * H + 2 * H * N)
 
 QUADRANT = 32
 Z_PLANE_AT = 0
-TEXT_CODES_AT = Z_PLANE_AT + Q
-ROUNDED_AT = TEXT_CODES_AT + 4 * 2 * C
-RAW_AT = ROUNDED_AT + 8 * H
+FIRST_SUMS_AT = Z_PLANE_AT + Q
+LAST_WZ_CODES_AT = FIRST_SUMS_AT + 4 * C
+RAW_AT = LAST_WZ_CODES_AT + 4 * H
 RAW_BYTES = 16 * H
 SEAT_BYTES = 4 * H
 LAST_ON_SCALAR = 64
-FIRST_PIECE_1 = 96
-FIRST_PIECE_2 = 48
 
 
 def tile_moe_mmo_gelu_kernel(
@@ -77,8 +75,6 @@ def tile_moe_mmo_gelu_kernel(
                 queue.dma_start(plane[r:P:32, :, :].bitcast(I32), rows[r:16:4, :, :].bitcast(I32))
 
         zero_plane(x_plane)
-        gate_row = own("gate_row", [P, 4], F32)
-        nc.gpsimd.dma_start(gate_row[:], gate1[0].rearrange("(q j) -> q j", j=4))
         zero_plane(w2_plane)
         load_plane(nc.gpsimd, w2_plane, w2_scales.rearrange("e g b n -> b (e g) n"))
 
@@ -101,12 +97,6 @@ def tile_moe_mmo_gelu_kernel(
         for h in range(2):
             nc.scalar.activation(result["t"][h][:], zero[:].to_broadcast([P, T]), GELU)
 
-        gate = {k: own("gate_" + k, [P, S], F32) for k in "tp"}
-        spread = psum.tile([P, 4, P], F32, name="bank_p0")
-        for j in range(4):
-            nc.tensor.transpose(spread[:, j, :], gate_row[:, j : j + 1].to_broadcast([P, P]), identity[:])
-        nc.scalar.copy(gate["t"][:].rearrange("p (q j) -> p q j", j=4), spread[:].rearrange("p j q -> p q j"))
-
         w1, w2 = {}, {}
 
         def load_experts(views, name, words, lo, hi):
@@ -119,6 +109,14 @@ def tile_moe_mmo_gelu_kernel(
         def load_wz(e):
             nc.sync.dma_start(wz_raw[e][:], wz[e].rearrange("(p j) i -> p j i", j=4))
 
+        gate = {}
+
+        def load_gate(k, source, lo, hi):
+            tile = own("gate_%s%d" % (k, lo), [P, (hi - lo) * C], F32)
+            nc.sync.dma_start(tile[:], source[:, lo * C : hi * C])
+            for e in range(lo, hi):
+                gate[k, e] = (tile, lo)
+
         nc.sync.dma_start(x_window[0][:], x_words[0].rearrange("p t d -> p (t d)").bitcast(I32))
         nc.sync.dma_start(offsets["t"][:], offs)
         nc.sync.dma_start(x_window[1][:], x_words[1].rearrange("p t d -> p (t d)").bitcast(I32))
@@ -128,15 +126,17 @@ def tile_moe_mmo_gelu_kernel(
         nc.sync.dma_start(offsets["p"][:], offs2)
         load_experts(w1, "w1", w1_words, 1, 2)
         nc.sync.dma_start(z_window[:], z_words[0].rearrange("p t d -> p (t d)").bitcast(I32))
-        load_experts(w1, "w1", w1_words, 2, E)
         load_plane(nc.sync, z_plane, z_scales.rearrange("g b t -> b g t"))
-        load_wz(0)
+        load_experts(w1, "w1", w1_words, 2, E)
         load_experts(w2, "w2", w2_words, 0, 2)
+        load_wz(0)
+        load_gate("t", gate1, 0, 2)
         load_wz(1)
         load_experts(w2, "w2", w2_words, 2, E)
+        load_gate("t", gate1, 2, E)
         load_wz(2)
         load_wz(3)
-        nc.sync.dma_start(gate["p"][:], gate2)
+        load_gate("p", gate2, 0, E)
 
         def gather(name, window, k, dtype, groups):
             views = []
@@ -155,7 +155,7 @@ def tile_moe_mmo_gelu_kernel(
         z_slots = gather("z_slots", z_window[:].bitcast(U32), "p", U32, halves)
         z_slot_scales = gather("z_slot_scales", z_plane[:, 0, :], "p", U8, halves)
 
-        bank, hidden, sums_in_psum, wz_rounded = {}, {}, {}, {}
+        bank, hidden, sums_in_psum, sums, wz_rounded = {}, {}, {}, {}, {}
 
         def text_product(e):
             bank["t", e] = psum.tile([P, H], F32, name="bank_t%d" % e)
@@ -175,26 +175,26 @@ def tile_moe_mmo_gelu_kernel(
             nc.scalar.activation(pairs[:], bank["t", e][:].rearrange("c (p u v) -> c u p v", u=2, v=2), GELU)
             return pairs
 
-        def text_turn(e, pairs):
+        def text_turn(e, pairs, lo, hi):
             turned = bank["t", e][:, 0 : 2 * C].rearrange("p (u c) -> p u c", u=2)
             words = pairs[:].rearrange("c u p v -> c (u p v)").bitcast(F32)
             for u in range(2):
                 nc.tensor.transpose(turned[:, u, :], words[:, u * P : (u + 1) * P], identity[:])
-            if e % 2 == 0:
-                hidden["t", e] = own("hidden_t%d" % e, [P, 2 * 4 * C], BF16)
-            half = hidden["t", e - e % 2][:, (e % 2) * 4 * C : (e % 2 + 1) * 4 * C]
+            if e == lo:
+                hidden["t", e] = own("hidden_t%d" % e, [P, (hi - lo) * 4 * C], BF16)
+            half = hidden["t", lo][:, (e - lo) * 4 * C : (e - lo + 1) * 4 * C]
             nc.scalar.copy(half.bitcast(F32).rearrange("p (c u) -> p c u", u=2), turned.rearrange("p u c -> p c u"))
 
-        def round_wz(e, copy, lo, hi, make=own):
+        def round_wz(e, copy, lo, hi):
             if e not in wz_rounded:
-                wz_rounded[e] = make("wz_rounded%d" % e, [P, 4 * H], BF16)
+                wz_rounded[e] = own("wz_rounded%d" % e, [P, 4 * H], BF16)
             copy(
                 wz_rounded[e][:].rearrange("p (t m j) -> p m j t", t=4, j=4)[:, lo:hi, :, :],
                 wz_raw[e][:].rearrange("p j (m t) -> p m j t", t=4)[:, lo:hi, :, :],
             )
 
-        def patch_product(e):
-            codes = own("wz_codes%d" % e, [P, H], U32)
+        def patch_product(e, make=own):
+            codes = make("wz_codes%d" % e, [P, H], U32)
             scales = own("wz_scales%d" % e, [P, H], U8)
             nc.vector.quantize_mx(out=codes[:].bitcast(FP8X4), scales=scales[:], in_=wz_rounded[e][:])
             bank["p", e] = psum.tile([P, H], F32, name="bank_p%d" % e)
@@ -217,9 +217,9 @@ def tile_moe_mmo_gelu_kernel(
                 GELU,
             )
 
-        def second_product(k, lo, hi, make, make_codes=own):
+        def second_product(k, lo, hi, make):
             width = (hi - lo) * C
-            codes = make_codes("hidden_codes_%s%d" % (k, lo), [P, width], U32)
+            codes = own("hidden_codes_%s%d" % (k, lo), [P, width], U32)
             scales = make("hidden_scales_%s%d" % (k, lo), [P, width], U8)
             nc.vector.quantize_mx(out=codes[:].bitcast(FP8X4), scales=scales[:], in_=hidden[k, lo][:])
             sums_in_psum[k, lo] = bank[k, lo][:, H - 2 * width : H].rearrange("p (h c) -> p h c", h=2)
@@ -236,55 +236,72 @@ def tile_moe_mmo_gelu_kernel(
                         stop=True,
                     )
 
-        def scatter(k, lo, hi, make, h0=0, h1=2):
-            sums = make("sums_%s%d_%d" % (k, lo, h0), [P, h1 - h0, (hi - lo) * C], F32)
-            nc.scalar.copy(sums[:], sums_in_psum[k, lo][:, h0:h1, :])
-            columns = slice(0, T) if k == "t" else slice(T, T + Q)
+        def copy_sums(k, lo, hi, make, h0, h1):
+            tile = make("sums_%s%d_%d" % (k, lo, h0), [P, h1 - h0, (hi - lo) * C], F32)
+            nc.scalar.copy(tile[:], sums_in_psum[k, lo][:, h0:h1, :])
             for h in range(h0, h1):
-                nc.vector.tensor_tensor(
-                    result[k][h][:].indirect(offsets[k][:, 8 * lo : 8 * hi]),
-                    sums[:, h - h0, :],
-                    gate[k][:, lo * C : hi * C],
-                    MULT,
-                )
-                if hi == E:
-                    nc.sync.dma_start(out[h * P : (h + 1) * P, columns], result[k][h][:])
+                sums[k, lo, h] = tile[:, h - h0, :]
+
+        def scatter_half(k, lo, hi, h):
+            tile, first = gate[k, lo]
+            nc.vector.tensor_tensor(
+                result[k][h][:].indirect(offsets[k][:, 8 * lo : 8 * hi]),
+                sums[k, lo, h],
+                tile[:, (lo - first) * C : (hi - first) * C],
+                MULT,
+            )
+            if hi == E:
+                columns = slice(0, T) if k == "t" else slice(T, T + Q)
+                nc.sync.dma_start(out[h * P : (h + 1) * P, columns], result[k][h][:])
+
+        def scatter(k, lo, hi, make, h0=0, h1=2):
+            copy_sums(k, lo, hi, make, h0, h1)
+            for h in range(h0, h1):
+                scatter_half(k, lo, hi, h)
 
         for e in range(E):
             text_product(e)
         pairs_of = [text_gelu(e) for e in range(E)]
-        for e in range(E):
-            text_turn(e, pairs_of[e])
+        for e in range(2):
+            text_turn(e, pairs_of[e], e, e + 1)
+        for e in range(2):
+            second_product("t", e, e + 1, on_bytes(Z_PLANE_AT + e * C))
+        copy_sums("t", 0, 1, on_bytes(FIRST_SUMS_AT), 0, 1)
+        copy_sums("t", 0, 1, own, 1, 2)
+        copy_sums("t", 1, 2, own, 0, 2)
+        for e in range(2, E):
+            text_turn(e, pairs_of[e], 2, E)
 
-        second_product("t", 0, 2, on_bytes(Z_PLANE_AT))
         round_wz(0, nc.vector.tensor_copy, 0, P)
+        scatter_half("t", 0, 1, 0)
         patch_product(0)
-        second_product("t", 2, E, after_rounding(0, 0), on_bytes(TEXT_CODES_AT))
-        scatter("t", 0, 2, own)
+        second_product("t", 2, E, on_bytes(FIRST_SUMS_AT))
+        scatter_half("t", 0, 1, 1)
+        scatter_half("t", 1, 2, 0)
+        scatter_half("t", 1, 2, 1)
 
-        round_wz(1, nc.scalar.copy, 0, FIRST_PIECE_1, on_bytes(ROUNDED_AT))
-        scatter("t", 2, E, own, 0, 1)
-        patch_gelu(0, on_bytes(TEXT_CODES_AT))
-        second_product("p", 0, 1, own)
-        round_wz(1, nc.scalar.copy, FIRST_PIECE_1, P)
+        round_wz(1, nc.scalar.copy, 0, P)
         patch_product(1)
+        scatter("t", 2, E, own, 0, 1)
+        patch_gelu(0, after_rounding(1, 0))
+        second_product("p", 0, 1, own)
+        scatter("t", 2, E, own, 1, 2)
 
-        round_wz(2, nc.scalar.copy, 0, FIRST_PIECE_2)
-        scatter("t", 2, E, after_rounding(1, 0), 1, 2)
-        round_wz(2, nc.scalar.copy, FIRST_PIECE_2, P)
-        round_wz(3, nc.vector.tensor_copy, LAST_ON_SCALAR, P)
+        round_wz(2, nc.scalar.copy, 0, P)
         patch_product(2)
-        patch_gelu(1, own)
+        round_wz(3, nc.vector.tensor_copy, LAST_ON_SCALAR, P)
+        patch_gelu(1, after_rounding(2, 0))
         second_product("p", 1, 2, own)
-        scatter("p", 0, 1, on_bytes(ROUNDED_AT), 0, 1)
 
         round_wz(3, nc.scalar.copy, 0, LAST_ON_SCALAR)
-        patch_product(3)
-        scatter("p", 0, 1, on_bytes(ROUNDED_AT + 4 * C), 1, 2)
-        patch_gelu(2, own)
+        patch_product(3, on_bytes(LAST_WZ_CODES_AT))
+        scatter("p", 0, 1, after_rounding(3, 0), 0, 1)
+        patch_gelu(2, after_rounding(3, 1))
         second_product("p", 2, 3, own)
-        scatter("p", 1, 2, own)
+        scatter("p", 0, 1, after_rounding(3, 2), 1, 2)
+        scatter("p", 1, 2, after_rounding(3, 3), 0, 1)
         patch_gelu(3, own)
         second_product("p", 3, E, own)
+        scatter("p", 1, 2, on_bytes(LAST_WZ_CODES_AT), 1, 2)
         scatter("p", 2, 3, own)
         scatter("p", 3, E, own)

@@ -24,13 +24,15 @@ S = E * C
 FLOPS = 2 * S * (K * H + L * H + 2 * H * N)
 
 QUADRANT = 32
-Z_PLANE_AT = 0
-FIRST_SUMS_AT = Z_PLANE_AT + Q
-LAST_WZ_CODES_AT = FIRST_SUMS_AT + 4 * C
+Z_WINDOW_AT = 0
+TEXT_CODES_AT = Z_WINDOW_AT + 4 * Q
+LAST_WZ_CODES_AT = TEXT_CODES_AT + 4 * 2 * C
 RAW_AT = LAST_WZ_CODES_AT + 4 * H
 RAW_BYTES = 16 * H
 SEAT_BYTES = 4 * H
 LAST_ON_SCALAR = 64
+FIRST_ON_SCALAR = 32
+SECOND_PIECE = 80
 
 
 def tile_moe_mmo_gelu_kernel(
@@ -56,9 +58,9 @@ def tile_moe_mmo_gelu_kernel(
 
         offsets = {k: keep.tile([P, S // 16], U16, name="offsets_" + k) for k in "tp"}
         x_window = [own("x_window%d" % g, [P, T], I32) for g in range(2)]
-        z_window = own("z_window", [P, Q], I32)
+        z_window = on_bytes(Z_WINDOW_AT)("z_window", [P, Q], I32)
         x_plane = own("x_plane", [P, 2, T], U8)
-        z_plane = on_bytes(Z_PLANE_AT)("z_plane", [P, 1, Q], U8)
+        z_plane = own("z_plane", [P, 1, Q], U8)
         w1_plane = own("w1_plane", [P, 2 * E, H], U8)
         w2_plane = own("w2_plane", [P, E, N], U8)
         wz_raw = [on_bytes(RAW_AT + e * RAW_BYTES)("wz_raw%d" % e, [P, 4, H], F32) for e in range(E)]
@@ -75,8 +77,8 @@ def tile_moe_mmo_gelu_kernel(
                 queue.dma_start(plane[r:P:32, :, :].bitcast(I32), rows[r:16:4, :, :].bitcast(I32))
 
         zero_plane(x_plane)
-        zero_plane(w2_plane)
-        load_plane(nc.gpsimd, w2_plane, w2_scales.rearrange("e g b n -> b (e g) n"))
+        zero_plane(z_plane)
+        load_plane(nc.gpsimd, z_plane, z_scales.rearrange("g b t -> b g t"))
 
         zero = own("zero", [P, 1], F32)
         ones = own("ones", [P, QUADRANT], F32)
@@ -86,7 +88,7 @@ def tile_moe_mmo_gelu_kernel(
         nc.vector.memset(zero[:], 0.0)
         nc.vector.memset(ones[:], 1.0)
         zero_plane(w1_plane)
-        zero_plane(z_plane)
+        zero_plane(w2_plane)
         nc.vector.tensor_tensor_scan(column_number[:], ones[:], ones[:], 0.0, MULT, ADD)
         nc.vector.memset(identity[:], 0.0)
         nc.vector.transpose(row_number[:], column_number[:])
@@ -123,17 +125,17 @@ def tile_moe_mmo_gelu_kernel(
         load_plane(nc.sync, x_plane, x_scales.rearrange("g b t -> b g t"))
         load_experts(w1, "w1", w1_words, 0, 1)
         load_plane(nc.sync, w1_plane, w1_scales.rearrange("e g b i -> b (e g) i"))
+        load_experts(w1, "w1", w1_words, 1, 3)
+        load_experts(w1, "w1", w1_words, 3, E)
         nc.sync.dma_start(offsets["p"][:], offs2)
-        load_experts(w1, "w1", w1_words, 1, 2)
         nc.sync.dma_start(z_window[:], z_words[0].rearrange("p t d -> p (t d)").bitcast(I32))
-        load_plane(nc.sync, z_plane, z_scales.rearrange("g b t -> b g t"))
-        load_experts(w1, "w1", w1_words, 2, E)
-        load_experts(w2, "w2", w2_words, 0, 2)
         load_wz(0)
-        load_gate("t", gate1, 0, 2)
+        gate_row = own("gate_row", [P, 4], F32)
+        nc.sync.dma_start(gate_row[:], gate1[0].rearrange("(q j) -> q j", j=4))
+        load_plane(nc.sync, w2_plane, w2_scales.rearrange("e g b n -> b (e g) n"))
+        load_experts(w2, "w2", w2_words, 0, 2)
         load_wz(1)
         load_experts(w2, "w2", w2_words, 2, E)
-        load_gate("t", gate1, 2, E)
         load_wz(2)
         load_wz(3)
         load_gate("p", gate2, 0, E)
@@ -152,8 +154,8 @@ def tile_moe_mmo_gelu_kernel(
             for g in range(2):
                 x_slot_scales[g] = x_slot_scales[g] + gather("x_slot_scales%d_" % g, x_plane[:, g, :], "t", U8, [group])
         halves = [(0, E // 2), (E // 2, E)]
-        z_slots = gather("z_slots", z_window[:].bitcast(U32), "p", U32, halves)
         z_slot_scales = gather("z_slot_scales", z_plane[:, 0, :], "p", U8, halves)
+        z_slots = gather("z_slots", z_window[:].bitcast(U32), "p", U32, halves)
 
         bank, hidden, sums_in_psum, sums, wz_rounded = {}, {}, {}, {}, {}
 
@@ -175,15 +177,18 @@ def tile_moe_mmo_gelu_kernel(
             nc.scalar.activation(pairs[:], bank["t", e][:].rearrange("c (p u v) -> c u p v", u=2, v=2), GELU)
             return pairs
 
-        def text_turn(e, pairs, lo, hi):
-            turned = bank["t", e][:, 0 : 2 * C].rearrange("p (u c) -> p u c", u=2)
-            words = pairs[:].rearrange("c u p v -> c (u p v)").bitcast(F32)
-            for u in range(2):
-                nc.tensor.transpose(turned[:, u, :], words[:, u * P : (u + 1) * P], identity[:])
-            if e == lo:
-                hidden["t", e] = own("hidden_t%d" % e, [P, (hi - lo) * 4 * C], BF16)
-            half = hidden["t", lo][:, (e - lo) * 4 * C : (e - lo + 1) * 4 * C]
-            nc.scalar.copy(half.bitcast(F32).rearrange("p (c u) -> p c u", u=2), turned.rearrange("p u c -> p c u"))
+        def text_turn(lo, hi, first):
+            turned = bank["t", hi - 1][:, 0 : (hi - lo) * 2 * C].rearrange("p (e u c) -> p e u c", u=2, c=C)
+            for e in range(lo, hi):
+                words = pairs_of[e][:].rearrange("c u p v -> c (u p v)").bitcast(F32)
+                for u in range(2):
+                    nc.tensor.transpose(turned[:, e - lo, u, :], words[:, u * P : (u + 1) * P], identity[:])
+            if lo == first:
+                hidden["t", lo] = own("hidden_t%d" % lo, [P, 2 * 4 * C], BF16)
+            part = hidden["t", first][:, (lo - first) * 4 * C : (hi - first) * 4 * C]
+            nc.scalar.copy(
+                part.bitcast(F32).rearrange("p (e c u) -> p e c u", u=2, c=C), turned.rearrange("p e u c -> p e c u")
+            )
 
         def round_wz(e, copy, lo, hi):
             if e not in wz_rounded:
@@ -193,9 +198,9 @@ def tile_moe_mmo_gelu_kernel(
                 wz_raw[e][:].rearrange("p j (m t) -> p m j t", t=4)[:, lo:hi, :, :],
             )
 
-        def patch_product(e, make=own):
+        def patch_product(e, make=own, make_scales=own):
             codes = make("wz_codes%d" % e, [P, H], U32)
-            scales = own("wz_scales%d" % e, [P, H], U8)
+            scales = make_scales("wz_scales%d" % e, [P, H], U8)
             nc.vector.quantize_mx(out=codes[:].bitcast(FP8X4), scales=scales[:], in_=wz_rounded[e][:])
             bank["p", e] = psum.tile([P, H], F32, name="bank_p%d" % e)
             for t in range(4):
@@ -217,9 +222,9 @@ def tile_moe_mmo_gelu_kernel(
                 GELU,
             )
 
-        def second_product(k, lo, hi, make):
+        def second_product(k, lo, hi, make, make_codes=own):
             width = (hi - lo) * C
-            codes = own("hidden_codes_%s%d" % (k, lo), [P, width], U32)
+            codes = make_codes("hidden_codes_%s%d" % (k, lo), [P, width], U32)
             scales = make("hidden_scales_%s%d" % (k, lo), [P, width], U8)
             nc.vector.quantize_mx(out=codes[:].bitcast(FP8X4), scales=scales[:], in_=hidden[k, lo][:])
             sums_in_psum[k, lo] = bank[k, lo][:, H - 2 * width : H].rearrange("p (h c) -> p h c", h=2)
@@ -262,46 +267,46 @@ def tile_moe_mmo_gelu_kernel(
         for e in range(E):
             text_product(e)
         pairs_of = [text_gelu(e) for e in range(E)]
-        for e in range(2):
-            text_turn(e, pairs_of[e], e, e + 1)
-        for e in range(2):
-            second_product("t", e, e + 1, on_bytes(Z_PLANE_AT + e * C))
-        copy_sums("t", 0, 1, on_bytes(FIRST_SUMS_AT), 0, 1)
-        copy_sums("t", 0, 1, own, 1, 2)
-        copy_sums("t", 1, 2, own, 0, 2)
-        for e in range(2, E):
-            text_turn(e, pairs_of[e], 2, E)
+        text_turn(0, 2, 0)
+        text_turn(2, 3, 2)
+        text_turn(3, E, 2)
+        second_product("t", 0, 2, on_bytes(Z_WINDOW_AT), on_bytes(TEXT_CODES_AT))
 
-        round_wz(0, nc.vector.tensor_copy, 0, P)
-        scatter_half("t", 0, 1, 0)
-        patch_product(0)
-        second_product("t", 2, E, on_bytes(FIRST_SUMS_AT))
-        scatter_half("t", 0, 1, 1)
-        scatter_half("t", 1, 2, 0)
-        scatter_half("t", 1, 2, 1)
+        round_wz(0, nc.vector.tensor_copy, FIRST_ON_SCALAR, P)
+        round_wz(0, nc.scalar.copy, 0, FIRST_ON_SCALAR)
+        spread = psum.tile([P, 4, P], F32, name="bank_p0")
+        for j in range(4):
+            nc.tensor.transpose(spread[:, j, :], gate_row[:, j : j + 1].to_broadcast([P, P]), identity[:])
+        gate_t = own("gate_t", [P, S], F32)
+        nc.scalar.copy(gate_t[:].rearrange("p (q j) -> p q j", j=4), spread[:].rearrange("p j q -> p q j"))
+        for e in range(E):
+            gate["t", e] = (gate_t, 0)
+        second_product("t", 2, E, after_rounding(0, 0))
+        patch_product(0, own, on_bytes(TEXT_CODES_AT))
+        scatter("t", 0, 2, own)
 
-        round_wz(1, nc.scalar.copy, 0, P)
-        patch_product(1)
+        round_wz(1, nc.scalar.copy, 0, SECOND_PIECE)
         scatter("t", 2, E, own, 0, 1)
+        round_wz(1, nc.scalar.copy, SECOND_PIECE, P)
+        patch_product(1)
         patch_gelu(0, after_rounding(1, 0))
         second_product("p", 0, 1, own)
-        scatter("t", 2, E, own, 1, 2)
+        scatter("t", 2, E, after_rounding(1, 1), 1, 2)
 
         round_wz(2, nc.scalar.copy, 0, P)
         patch_product(2)
         round_wz(3, nc.vector.tensor_copy, LAST_ON_SCALAR, P)
         patch_gelu(1, after_rounding(2, 0))
         second_product("p", 1, 2, own)
+        scatter("p", 0, 1, after_rounding(2, 1))
 
         round_wz(3, nc.scalar.copy, 0, LAST_ON_SCALAR)
         patch_product(3, on_bytes(LAST_WZ_CODES_AT))
-        scatter("p", 0, 1, after_rounding(3, 0), 0, 1)
-        patch_gelu(2, after_rounding(3, 1))
+        patch_gelu(2, after_rounding(3, 0))
         second_product("p", 2, 3, own)
-        scatter("p", 0, 1, after_rounding(3, 2), 1, 2)
-        scatter("p", 1, 2, after_rounding(3, 3), 0, 1)
+        scatter("p", 1, 2, after_rounding(3, 1))
+
         patch_gelu(3, own)
         second_product("p", 3, E, own)
-        scatter("p", 1, 2, on_bytes(LAST_WZ_CODES_AT), 1, 2)
-        scatter("p", 2, 3, own)
+        scatter("p", 2, 3, on_bytes(LAST_WZ_CODES_AT))
         scatter("p", 3, E, own)

@@ -24,10 +24,12 @@ S = E * C
 FLOPS = 2 * S * (K * H + L * H + 2 * H * N)
 
 QUADRANT = 32
-Z_WINDOW_AT = 0
-TEXT_CODES_AT = Z_WINDOW_AT + 4 * Q
-LAST_WZ_CODES_AT = TEXT_CODES_AT + 4 * 2 * C
-RAW_AT = LAST_WZ_CODES_AT + 4 * H
+Z_WINDOW = 704
+Z_PLANE_AT = 0
+TEXT_CODES_AT = Z_PLANE_AT + Z_WINDOW
+LATE_TEXT_CODES_AT = TEXT_CODES_AT + 4 * 2 * C
+SECOND_WZ_CODES_AT = LATE_TEXT_CODES_AT + 4 * 2 * C
+RAW_AT = SECOND_WZ_CODES_AT + 4 * H
 RAW_BYTES = 16 * H
 SEAT_BYTES = 4 * H
 LAST_ON_SCALAR = 64
@@ -58,9 +60,9 @@ def tile_moe_mmo_gelu_kernel(
 
         offsets = {k: keep.tile([P, S // 16], U16, name="offsets_" + k) for k in "tp"}
         x_window = [own("x_window%d" % g, [P, T], I32) for g in range(2)]
-        z_window = on_bytes(Z_WINDOW_AT)("z_window", [P, Q], I32)
+        z_window = own("z_window", [P, Z_WINDOW], I32)
         x_plane = own("x_plane", [P, 2, T], U8)
-        z_plane = own("z_plane", [P, 1, Q], U8)
+        z_plane = on_bytes(Z_PLANE_AT)("z_plane", [P, 1, Z_WINDOW], U8)
         w1_plane = own("w1_plane", [P, 2 * E, H], U8)
         w2_plane = own("w2_plane", [P, E, N], U8)
         wz_raw = [on_bytes(RAW_AT + e * RAW_BYTES)("wz_raw%d" % e, [P, 4, H], F32) for e in range(E)]
@@ -74,7 +76,7 @@ def tile_moe_mmo_gelu_kernel(
 
         def load_plane(queue, plane, rows):
             for r in range(4):
-                queue.dma_start(plane[r:P:32, :, :].bitcast(I32), rows[r:16:4, :, :].bitcast(I32))
+                queue.dma_start(plane[r:P:32, :, 0 : rows.shape[2]].bitcast(I32), rows[r:16:4, :, :].bitcast(I32))
 
         zero_plane(x_plane)
         zero_plane(z_plane)
@@ -89,6 +91,7 @@ def tile_moe_mmo_gelu_kernel(
         nc.vector.memset(ones[:], 1.0)
         zero_plane(w1_plane)
         zero_plane(w2_plane)
+        nc.vector.memset(z_window[:, Q:Z_WINDOW], 0)
         nc.vector.tensor_tensor_scan(column_number[:], ones[:], ones[:], 0.0, MULT, ADD)
         nc.vector.memset(identity[:], 0.0)
         nc.vector.transpose(row_number[:], column_number[:])
@@ -127,8 +130,8 @@ def tile_moe_mmo_gelu_kernel(
         load_plane(nc.sync, w1_plane, w1_scales.rearrange("e g b i -> b (e g) i"))
         load_experts(w1, "w1", w1_words, 1, 3)
         load_experts(w1, "w1", w1_words, 3, E)
+        nc.sync.dma_start(z_window[:, 0:Q], z_words[0].rearrange("p t d -> p (t d)").bitcast(I32))
         nc.sync.dma_start(offsets["p"][:], offs2)
-        nc.sync.dma_start(z_window[:], z_words[0].rearrange("p t d -> p (t d)").bitcast(I32))
         load_wz(0)
         gate_row = own("gate_row", [P, 4], F32)
         nc.sync.dma_start(gate_row[:], gate1[0].rearrange("(q j) -> q j", j=4))
@@ -153,9 +156,9 @@ def tile_moe_mmo_gelu_kernel(
         for group in [(0, 1), (1, 2), (2, E)]:
             for g in range(2):
                 x_slot_scales[g] = x_slot_scales[g] + gather("x_slot_scales%d_" % g, x_plane[:, g, :], "t", U8, [group])
-        halves = [(0, E // 2), (E // 2, E)]
-        z_slot_scales = gather("z_slot_scales", z_plane[:, 0, :], "p", U8, halves)
+        halves = [(0, E)]
         z_slots = gather("z_slots", z_window[:].bitcast(U32), "p", U32, halves)
+        z_slot_scales = gather("z_slot_scales", z_plane[:, 0, :], "p", U8, halves)
 
         bank, hidden, sums_in_psum, sums, wz_rounded = {}, {}, {}, {}, {}
 
@@ -270,7 +273,7 @@ def tile_moe_mmo_gelu_kernel(
         text_turn(0, 2, 0)
         text_turn(2, 3, 2)
         text_turn(3, E, 2)
-        second_product("t", 0, 2, on_bytes(Z_WINDOW_AT), on_bytes(TEXT_CODES_AT))
+        second_product("t", 0, 2, on_bytes(Z_PLANE_AT), on_bytes(TEXT_CODES_AT))
 
         round_wz(0, nc.vector.tensor_copy, FIRST_ON_SCALAR, P)
         round_wz(0, nc.scalar.copy, 0, FIRST_ON_SCALAR)
@@ -281,32 +284,32 @@ def tile_moe_mmo_gelu_kernel(
         nc.scalar.copy(gate_t[:].rearrange("p (q j) -> p q j", j=4), spread[:].rearrange("p j q -> p q j"))
         for e in range(E):
             gate["t", e] = (gate_t, 0)
-        second_product("t", 2, E, after_rounding(0, 0))
+        second_product("t", 2, E, after_rounding(0, 0), on_bytes(LATE_TEXT_CODES_AT))
         patch_product(0, own, on_bytes(TEXT_CODES_AT))
         scatter("t", 0, 2, own)
 
         round_wz(1, nc.scalar.copy, 0, SECOND_PIECE)
         scatter("t", 2, E, own, 0, 1)
-        round_wz(1, nc.scalar.copy, SECOND_PIECE, P)
-        patch_product(1)
-        patch_gelu(0, after_rounding(1, 0))
+        patch_gelu(0, on_bytes(LATE_TEXT_CODES_AT))
         second_product("p", 0, 1, own)
-        scatter("t", 2, E, after_rounding(1, 1), 1, 2)
+        round_wz(1, nc.scalar.copy, SECOND_PIECE, P)
+        patch_product(1, on_bytes(SECOND_WZ_CODES_AT))
+        scatter("t", 2, E, own, 1, 2)
 
         round_wz(2, nc.scalar.copy, 0, P)
         patch_product(2)
         round_wz(3, nc.vector.tensor_copy, LAST_ON_SCALAR, P)
-        patch_gelu(1, after_rounding(2, 0))
+        patch_gelu(1, own)
         second_product("p", 1, 2, own)
-        scatter("p", 0, 1, after_rounding(2, 1))
+        scatter("p", 0, 1, on_bytes(SECOND_WZ_CODES_AT), 0, 1)
 
         round_wz(3, nc.scalar.copy, 0, LAST_ON_SCALAR)
-        patch_product(3, on_bytes(LAST_WZ_CODES_AT))
-        patch_gelu(2, after_rounding(3, 0))
+        patch_product(3)
+        scatter("p", 0, 1, on_bytes(SECOND_WZ_CODES_AT + 4 * C), 1, 2)
+        patch_gelu(2, own)
         second_product("p", 2, 3, own)
-        scatter("p", 1, 2, after_rounding(3, 1))
-
+        scatter("p", 1, 2, own)
         patch_gelu(3, own)
         second_product("p", 3, E, own)
-        scatter("p", 2, 3, on_bytes(LAST_WZ_CODES_AT))
+        scatter("p", 2, 3, own)
         scatter("p", 3, E, own)

@@ -25,8 +25,8 @@ FLOPS = 2 * S * (K * H + L * H + 2 * H * N)
 
 QUADRANT = 32
 Z_WINDOW = 704
-Z_PLANE_AT = 0
-TEXT_CODES_AT = Z_PLANE_AT + Z_WINDOW
+GATE_ROW_AT = 0
+TEXT_CODES_AT = GATE_ROW_AT + 2 * C
 LATE_TEXT_CODES_AT = TEXT_CODES_AT + 4 * 2 * C
 SECOND_WZ_CODES_AT = LATE_TEXT_CODES_AT + 4 * 2 * C
 RAW_AT = SECOND_WZ_CODES_AT + 4 * H
@@ -62,7 +62,7 @@ def tile_moe_mmo_gelu_kernel(
         x_window = [own("x_window%d" % g, [P, T], I32) for g in range(2)]
         z_window = own("z_window", [P, Z_WINDOW], I32)
         x_plane = own("x_plane", [P, 2, T], U8)
-        z_plane = on_bytes(Z_PLANE_AT)("z_plane", [P, 1, Z_WINDOW], U8)
+        z_plane = own("z_plane", [P, 1, Z_WINDOW], U8)
         w1_plane = own("w1_plane", [P, 2 * E, H], U8)
         w2_plane = own("w2_plane", [P, E, N], U8)
         wz_raw = [on_bytes(RAW_AT + e * RAW_BYTES)("wz_raw%d" % e, [P, 4, H], F32) for e in range(E)]
@@ -133,7 +133,7 @@ def tile_moe_mmo_gelu_kernel(
         nc.sync.dma_start(z_window[:, 0:Q], z_words[0].rearrange("p t d -> p (t d)").bitcast(I32))
         nc.sync.dma_start(offsets["p"][:], offs2)
         load_wz(0)
-        gate_row = own("gate_row", [P, 4], F32)
+        gate_row = on_bytes(GATE_ROW_AT)("gate_row", [P, 4], F32)
         nc.sync.dma_start(gate_row[:], gate1[0].rearrange("(q j) -> q j", j=4))
         load_plane(nc.sync, w2_plane, w2_scales.rearrange("e g b n -> b (e g) n"))
         load_experts(w2, "w2", w2_words, 0, 2)
@@ -180,37 +180,35 @@ def tile_moe_mmo_gelu_kernel(
             nc.scalar.activation(pairs[:], bank["t", e][:].rearrange("c (p u v) -> c u p v", u=2, v=2), GELU)
             return pairs
 
-        def text_turn(lo, hi, first):
-            turned = bank["t", hi - 1][:, 0 : (hi - lo) * 2 * C].rearrange("p (e u c) -> p e u c", u=2, c=C)
-            for e in range(lo, hi):
-                words = pairs_of[e][:].rearrange("c u p v -> c (u p v)").bitcast(F32)
-                for u in range(2):
-                    nc.tensor.transpose(turned[:, e - lo, u, :], words[:, u * P : (u + 1) * P], identity[:])
-            if lo == first:
-                hidden["t", lo] = own("hidden_t%d" % lo, [P, 2 * 4 * C], BF16)
-            part = hidden["t", first][:, (lo - first) * 4 * C : (hi - first) * 4 * C]
-            nc.scalar.copy(
-                part.bitcast(F32).rearrange("p (e c u) -> p e c u", u=2, c=C), turned.rearrange("p e u c -> p e c u")
-            )
+        def text_turn(e, host):
+            turned = bank["t", host][:, 0 : 2 * C].rearrange("p (u c) -> p u c", u=2)
+            words = pairs_of[e][:].rearrange("c u p v -> c (u p v)").bitcast(F32)
+            for u in range(2):
+                nc.tensor.transpose(turned[:, u, :], words[:, u * P : (u + 1) * P], identity[:])
+            if e % 2 == 0:
+                hidden["t", e] = own("hidden_t%d" % e, [P, 2 * 4 * C], BF16)
+            half = hidden["t", e - e % 2][:, (e % 2) * 4 * C : (e % 2 + 1) * 4 * C]
+            nc.scalar.copy(half.bitcast(F32).rearrange("p (c u) -> p c u", u=2), turned.rearrange("p u c -> p c u"))
 
-        def round_wz(e, copy, lo, hi):
+        def round_wz(e, copy, lo, hi, t0=0, t1=4):
             if e not in wz_rounded:
                 wz_rounded[e] = own("wz_rounded%d" % e, [P, 4 * H], BF16)
             copy(
-                wz_rounded[e][:].rearrange("p (t m j) -> p m j t", t=4, j=4)[:, lo:hi, :, :],
-                wz_raw[e][:].rearrange("p j (m t) -> p m j t", t=4)[:, lo:hi, :, :],
+                wz_rounded[e][:].rearrange("p (t m j) -> p m j t", t=4, j=4)[:, lo:hi, :, t0:t1],
+                wz_raw[e][:].rearrange("p j (m t) -> p m j t", t=4)[:, lo:hi, :, t0:t1],
             )
 
-        def patch_product(e, make=own, make_scales=own):
-            codes = make("wz_codes%d" % e, [P, H], U32)
-            scales = make_scales("wz_scales%d" % e, [P, H], U8)
-            nc.vector.quantize_mx(out=codes[:].bitcast(FP8X4), scales=scales[:], in_=wz_rounded[e][:])
-            bank["p", e] = psum.tile([P, H], F32, name="bank_p%d" % e)
-            for t in range(4):
+        def patch_product(e, make=own, make_scales=own, t0=0, t1=4):
+            codes = make("wz_codes%d_%d" % (e, t0), [P, (t1 - t0) * P], U32)
+            scales = make_scales("wz_scales%d_%d" % (e, t0), [P, (t1 - t0) * P], U8)
+            nc.vector.quantize_mx(out=codes[:].bitcast(FP8X4), scales=scales[:], in_=wz_rounded[e][:, t0 * H : t1 * H])
+            if ("p", e) not in bank:
+                bank["p", e] = psum.tile([P, H], F32, name="bank_p%d" % e)
+            for t in range(t0, t1):
                 nc.tensor.matmul_mx(
                     out=bank["p", e][:, t * C : (t + 1) * C],
-                    lhsT=codes[:, t * P : (t + 1) * P].bitcast(FP8X4),
-                    lhsT_scale=scales[:, t * P : (t + 1) * P],
+                    lhsT=codes[:, (t - t0) * P : (t - t0 + 1) * P].bitcast(FP8X4),
+                    lhsT_scale=scales[:, (t - t0) * P : (t - t0 + 1) * P],
                     rhs=z_slots[e].bitcast(FP8X4),
                     rhs_scale=z_slot_scales[e],
                     start=True,
@@ -270,10 +268,11 @@ def tile_moe_mmo_gelu_kernel(
         for e in range(E):
             text_product(e)
         pairs_of = [text_gelu(e) for e in range(E)]
-        text_turn(0, 2, 0)
-        text_turn(2, 3, 2)
-        text_turn(3, E, 2)
-        second_product("t", 0, 2, on_bytes(Z_PLANE_AT), on_bytes(TEXT_CODES_AT))
+        text_turn(0, 1)
+        text_turn(1, 0)
+        text_turn(2, 2)
+        text_turn(3, 3)
+        second_product("t", 0, 2, own, on_bytes(TEXT_CODES_AT))
 
         round_wz(0, nc.vector.tensor_copy, FIRST_ON_SCALAR, P)
         round_wz(0, nc.scalar.copy, 0, FIRST_ON_SCALAR)
@@ -284,9 +283,10 @@ def tile_moe_mmo_gelu_kernel(
         nc.scalar.copy(gate_t[:].rearrange("p (q j) -> p q j", j=4), spread[:].rearrange("p j q -> p q j"))
         for e in range(E):
             gate["t", e] = (gate_t, 0)
-        second_product("t", 2, E, after_rounding(0, 0), on_bytes(LATE_TEXT_CODES_AT))
+        second_product("t", 2, E, on_bytes(GATE_ROW_AT), on_bytes(LATE_TEXT_CODES_AT))
         patch_product(0, own, on_bytes(TEXT_CODES_AT))
-        scatter("t", 0, 2, own)
+        scatter("t", 0, 2, own, 0, 1)
+        scatter("t", 0, 2, own, 1, 2)
 
         round_wz(1, nc.scalar.copy, 0, SECOND_PIECE)
         scatter("t", 2, E, own, 0, 1)
@@ -298,13 +298,14 @@ def tile_moe_mmo_gelu_kernel(
 
         round_wz(2, nc.scalar.copy, 0, P)
         patch_product(2)
-        round_wz(3, nc.vector.tensor_copy, LAST_ON_SCALAR, P)
+        round_wz(3, nc.vector.tensor_copy, 0, P, 2, 4)
+        patch_product(3, own, own, 2, 4)
         patch_gelu(1, own)
         second_product("p", 1, 2, own)
         scatter("p", 0, 1, on_bytes(SECOND_WZ_CODES_AT), 0, 1)
 
-        round_wz(3, nc.scalar.copy, 0, LAST_ON_SCALAR)
-        patch_product(3)
+        round_wz(3, nc.scalar.copy, 0, P, 0, 2)
+        patch_product(3, own, own, 0, 2)
         scatter("p", 0, 1, on_bytes(SECOND_WZ_CODES_AT + 4 * C), 1, 2)
         patch_gelu(2, own)
         second_product("p", 2, 3, own)

@@ -11,6 +11,7 @@ U8 = mybir.dt.uint8
 FP8X4 = mybir.dt.float8_e4m3fn_x4
 FP4X4 = mybir.dt.float4_e2m1fn_x4
 GELU = mybir.ActivationFunctionType.Gelu_apprx_tanh
+COPY = mybir.ActivationFunctionType.Copy
 MULT = mybir.AluOpType.mult
 ADD = mybir.AluOpType.add
 IS_EQUAL = mybir.AluOpType.is_equal
@@ -22,19 +23,7 @@ E, C = 4, 128
 H, N = 512, 256
 S = E * C
 FLOPS = 2 * S * (K * H + L * H + 2 * H * N)
-
 QUADRANT = 32
-Z_WINDOW = 704
-GATE_ROW_AT = 0
-TEXT_CODES_AT = GATE_ROW_AT + 2 * C
-LATE_TEXT_CODES_AT = TEXT_CODES_AT + 4 * 2 * C
-SECOND_WZ_CODES_AT = LATE_TEXT_CODES_AT + 4 * 2 * C
-RAW_AT = SECOND_WZ_CODES_AT + 4 * H
-RAW_BYTES = 16 * H
-SEAT_BYTES = 4 * H
-LAST_ON_SCALAR = 64
-FIRST_ON_SCALAR = 32
-SECOND_PIECE = 80
 
 
 def tile_moe_mmo_gelu_kernel(
@@ -42,33 +31,35 @@ def tile_moe_mmo_gelu_kernel(
 ):
     nc = tc.nc
     with ExitStack() as ctx:
-        keep = ctx.enter_context(tc.tile_pool(name="keep", bufs=1))
-        shared = ctx.enter_context(tc.tile_pool(name="shared", bufs=1))
+        lists = ctx.enter_context(tc.tile_pool(name="lists", bufs=1))
+        sbuf = ctx.enter_context(tc.tile_pool(name="sbuf", bufs=1))
         psum = ctx.enter_context(tc.psum_pool(name="psum", bufs=1))
 
-        def own(name, shape, dtype):
-            return keep.tile(shape, dtype, name=name, align_bytes=64)
+        places = {"free": 0}
 
-        def on_bytes(offset):
-            def make(name, shape, dtype):
-                return shared.tile(shape, dtype, name=name, align_bytes=64, offset=offset)
+        def tile(name, shape, dtype, on=None, at=0):
+            size = {F32: 4, I32: 4, U32: 4, BF16: 2, U8: 1}[dtype]
+            for n in shape[1:]:
+                size = size * n
+            if on is None:
+                places[name] = places["free"]
+                places["free"] = places["free"] + (size + 63) // 64 * 64
+            else:
+                places[name] = places[on] + at
+            return sbuf.tile(shape, dtype, name=name, align_bytes=64, offset=places[name])
 
-            return make
-
-        def after_rounding(e, seat):
-            return on_bytes(RAW_AT + e * RAW_BYTES + seat * SEAT_BYTES)
-
-        offsets = {k: keep.tile([P, S // 16], U16, name="offsets_" + k) for k in "tp"}
-        x_window = [own("x_window%d" % g, [P, T], I32) for g in range(2)]
-        z_window = own("z_window", [P, Z_WINDOW], I32)
-        x_plane = own("x_plane", [P, 2, T], U8)
-        z_plane = own("z_plane", [P, 1, Z_WINDOW], U8)
-        w1_plane = own("w1_plane", [P, 2 * E, H], U8)
-        w2_plane = own("w2_plane", [P, E, N], U8)
-        wz_raw = [on_bytes(RAW_AT + e * RAW_BYTES)("wz_raw%d" % e, [P, 4, H], F32) for e in range(E)]
+        offsets = {k: lists.tile([P, S // 16], U16, name="offsets_" + k) for k in "tp"}
+        x_window = [tile("x_window%d" % g, [P, T], I32) for g in range(2)]
+        z_window = tile("z_window", [P, Q], I32)
+        x_plane = tile("x_plane", [P, 2, T], U8)
+        z_plane = tile("z_plane", [P, 1, Q], U8)
+        w1_plane = tile("w1_plane", [P, 2 * E, H], U8)
+        w2_plane = tile("w2_plane", [P, E, N], U8)
+        pieces = [2, 1, 1, 1]
+        wz_raw = [[tile("wz_raw%d_%d" % (e, a), [P, 4, H // pieces[e]], F32) for a in range(pieces[e])] for e in range(E)]
         result = {
-            "t": [own("result_t%d" % h, [P, T], F32) for h in range(2)],
-            "p": [own("result_p%d" % h, [P, Q], F32) for h in range(2)],
+            "t": [tile("result_t%d" % h, [P, T], F32) for h in range(2)],
+            "p": [tile("result_p%d" % h, [P, Q], F32) for h in range(2)],
         }
 
         def zero_plane(plane):
@@ -76,22 +67,22 @@ def tile_moe_mmo_gelu_kernel(
 
         def load_plane(queue, plane, rows):
             for r in range(4):
-                queue.dma_start(plane[r:P:32, :, 0 : rows.shape[2]].bitcast(I32), rows[r:16:4, :, :].bitcast(I32))
+                queue.dma_start(plane[r:P:32, :, :].bitcast(I32), rows[r:16:4, :, :].bitcast(I32))
 
+        gate_row = tile("gate_row", [P, 4], F32)
         zero_plane(x_plane)
         zero_plane(z_plane)
         load_plane(nc.gpsimd, z_plane, z_scales.rearrange("g b t -> b g t"))
 
-        zero = own("zero", [P, 1], F32)
-        ones = own("ones", [P, QUADRANT], F32)
-        column_number = own("column_number", [P, QUADRANT], F32)
-        row_number = own("row_number", [P, QUADRANT], F32)
-        identity = own("identity", [P, P], F32)
+        zero = tile("zero", [P, 1], F32)
+        ones = tile("ones", [P, QUADRANT], F32)
+        column_number = tile("column_number", [P, QUADRANT], F32)
+        row_number = tile("row_number", [P, QUADRANT], F32)
+        identity = tile("identity", [P, P], F32)
         nc.vector.memset(zero[:], 0.0)
         nc.vector.memset(ones[:], 1.0)
         zero_plane(w1_plane)
         zero_plane(w2_plane)
-        nc.vector.memset(z_window[:, Q:Z_WINDOW], 0)
         nc.vector.tensor_tensor_scan(column_number[:], ones[:], ones[:], 0.0, MULT, ADD)
         nc.vector.memset(identity[:], 0.0)
         nc.vector.transpose(row_number[:], column_number[:])
@@ -106,61 +97,53 @@ def tile_moe_mmo_gelu_kernel(
 
         def load_experts(views, name, words, lo, hi):
             passes, row_bytes = words.shape[1], words.shape[3]
-            tile = own("%s_%d" % (name, lo), [P, (hi - lo) * passes, row_bytes], U8)
-            nc.sync.dma_start(tile[:].bitcast(I32), words[lo:hi].rearrange("e g p b -> p (e g) b").bitcast(I32))
+            held = tile("%s_%d" % (name, lo), [P, (hi - lo) * passes, row_bytes], U8)
+            nc.sync.dma_start(held[:].bitcast(I32), words[lo:hi].rearrange("e g p b -> p (e g) b").bitcast(I32))
             for e in range(lo, hi):
-                views[e] = tile[:, (e - lo) * passes : (e - lo + 1) * passes, :]
-
-        def load_wz(e):
-            nc.sync.dma_start(wz_raw[e][:], wz[e].rearrange("(p j) i -> p j i", j=4))
-
-        gate = {}
-
-        def load_gate(k, source, lo, hi):
-            tile = own("gate_%s%d" % (k, lo), [P, (hi - lo) * C], F32)
-            nc.sync.dma_start(tile[:], source[:, lo * C : hi * C])
-            for e in range(lo, hi):
-                gate[k, e] = (tile, lo)
+                views[e] = held[:, (e - lo) * passes : (e - lo + 1) * passes, :]
 
         nc.sync.dma_start(x_window[0][:], x_words[0].rearrange("p t d -> p (t d)").bitcast(I32))
         nc.sync.dma_start(offsets["t"][:], offs)
         nc.sync.dma_start(x_window[1][:], x_words[1].rearrange("p t d -> p (t d)").bitcast(I32))
         load_plane(nc.sync, x_plane, x_scales.rearrange("g b t -> b g t"))
         load_experts(w1, "w1", w1_words, 0, 1)
-        load_plane(nc.sync, w1_plane, w1_scales.rearrange("e g b i -> b (e g) i"))
-        load_experts(w1, "w1", w1_words, 1, 3)
-        load_experts(w1, "w1", w1_words, 3, E)
-        nc.sync.dma_start(z_window[:, 0:Q], z_words[0].rearrange("p t d -> p (t d)").bitcast(I32))
-        nc.sync.dma_start(offsets["p"][:], offs2)
-        load_wz(0)
-        gate_row = on_bytes(GATE_ROW_AT)("gate_row", [P, 4], F32)
         nc.sync.dma_start(gate_row[:], gate1[0].rearrange("(q j) -> q j", j=4))
+        load_experts(w1, "w1", w1_words, 1, 2)
+        load_plane(nc.sync, w1_plane, w1_scales.rearrange("e g b i -> b (e g) i"))
+        nc.sync.dma_start(z_window[:], z_words[0].rearrange("p t d -> p (t d)").bitcast(I32))
+        load_experts(w1, "w1", w1_words, 2, E)
+        nc.sync.dma_start(offsets["p"][:], offs2)
+        load_experts(w2, "w2", w2_words, 0, E)
         load_plane(nc.sync, w2_plane, w2_scales.rearrange("e g b n -> b (e g) n"))
-        load_experts(w2, "w2", w2_words, 0, 2)
-        load_wz(1)
-        load_experts(w2, "w2", w2_words, 2, E)
-        load_wz(2)
-        load_wz(3)
-        load_gate("p", gate2, 0, E)
+        for e in range(E):
+            width = H // pieces[e]
+            for a in range(pieces[e]):
+                nc.sync.dma_start(wz_raw[e][a][:], wz[e].rearrange("(p j) i -> p j i", j=4)[:, :, a * width : (a + 1) * width])
+        gate = {k: tile("gate_" + k, [P, S], F32) for k in "tp"}
+        nc.sync.dma_start(gate["p"][:], gate2)
 
-        def gather(name, window, k, dtype, groups):
-            views = []
-            for lo, hi in groups:
-                slots = own("%s%d" % (name, lo), [P, (hi - lo) * C], dtype)
-                nc.vector.tensor_copy(slots[:], window.indirect(offsets[k][:, 8 * lo : 8 * hi]))
-                views = views + [slots[:, e * C : (e + 1) * C] for e in range(hi - lo)]
-            return views
+        spread = psum.tile([P, 4, P], F32, name="bank_p3")
+        for j in range(4):
+            nc.tensor.transpose(spread[:, j, :], gate_row[:, j : j + 1].to_broadcast([P, P]), identity[:])
+        nc.scalar.copy(gate["t"][:].rearrange("p (q j) -> p q j", j=4), spread[:].rearrange("p j q -> p q j"))
 
-        x_slots = [gather("x_slots%d_" % g, x_window[g][:].bitcast(U32), "t", U32, [(0, E)]) for g in range(2)]
+        def gather(name, window, k, dtype, lo, hi, on=None):
+            slots = tile("%s%d" % (name, lo), [P, (hi - lo) * C], dtype, on)
+            nc.vector.tensor_copy(slots[:], window.indirect(offsets[k][:, 8 * lo : 8 * hi]))
+            return [slots[:, e * C : (e + 1) * C] for e in range(hi - lo)]
+
+        x_slots = [gather("x_slots%d_" % g, x_window[g][:].bitcast(U32), "t", U32, 0, E) for g in range(2)]
         x_slot_scales = [[], []]
-        for group in [(0, 1), (1, 2), (2, E)]:
+        for lo, hi in [(0, 1), (1, 2), (2, E)]:
             for g in range(2):
-                x_slot_scales[g] = x_slot_scales[g] + gather("x_slot_scales%d_" % g, x_plane[:, g, :], "t", U8, [group])
-        halves = [(0, E)]
-        z_slots = gather("z_slots", z_window[:].bitcast(U32), "p", U32, halves)
-        z_slot_scales = gather("z_slot_scales", z_plane[:, 0, :], "p", U8, halves)
+                x_slot_scales[g] = x_slot_scales[g] + gather("x_slot_scales%d_" % g, x_plane[:, g, :], "t", U8, lo, hi)
+        z_slots, z_slot_scales = [], []
+        for lo in (0, 2):
+            z_slots = z_slots + gather("z_slots", z_window[:].bitcast(U32), "p", U32, lo, lo + 2)
+        for lo in (0, 2):
+            z_slot_scales = z_slot_scales + gather("z_slot_scales", z_plane[:, 0, :], "p", U8, lo, lo + 2)
 
-        bank, hidden, sums_in_psum, sums, wz_rounded = {}, {}, {}, {}, {}
+        bank, hidden, gated, wz_rounded = {}, {}, {}, {}
 
         def text_product(e):
             bank["t", e] = psum.tile([P, H], F32, name="bank_t%d" % e)
@@ -175,142 +158,129 @@ def tile_moe_mmo_gelu_kernel(
                     stop=(g == 1),
                 )
 
-        def text_gelu(e):
-            pairs = own("pairs%d" % e, [P, 2, P, 2], BF16)
+        def text_hidden(e):
+            pairs = tile("pairs%d" % e, [P, 2, P, 2], BF16)
             nc.scalar.activation(pairs[:], bank["t", e][:].rearrange("c (p u v) -> c u p v", u=2, v=2), GELU)
-            return pairs
-
-        def text_turn(e, host):
-            turned = bank["t", host][:, 0 : 2 * C].rearrange("p (u c) -> p u c", u=2)
-            words = pairs_of[e][:].rearrange("c u p v -> c (u p v)").bitcast(F32)
+            turned = bank["t", e][:, 0 : 2 * C].rearrange("p (u c) -> p u c", u=2)
+            words = pairs[:].rearrange("c u p v -> c (u p v)").bitcast(F32)
             for u in range(2):
                 nc.tensor.transpose(turned[:, u, :], words[:, u * P : (u + 1) * P], identity[:])
-            if e % 2 == 0:
-                hidden["t", e] = own("hidden_t%d" % e, [P, 2 * 4 * C], BF16)
-            half = hidden["t", e - e % 2][:, (e % 2) * 4 * C : (e % 2 + 1) * 4 * C]
-            nc.scalar.copy(half.bitcast(F32).rearrange("p (c u) -> p c u", u=2), turned.rearrange("p u c -> p c u"))
-
-        def round_wz(e, copy, lo, hi, t0=0, t1=4):
-            if e not in wz_rounded:
-                wz_rounded[e] = own("wz_rounded%d" % e, [P, 4 * H], BF16)
-            copy(
-                wz_rounded[e][:].rearrange("p (t m j) -> p m j t", t=4, j=4)[:, lo:hi, :, t0:t1],
-                wz_raw[e][:].rearrange("p j (m t) -> p m j t", t=4)[:, lo:hi, :, t0:t1],
+            hidden["t", e] = tile("hidden_t%d" % e, [P, 4 * C], BF16)
+            nc.scalar.copy(
+                hidden["t", e][:].bitcast(F32).rearrange("p (c u) -> p c u", u=2), turned.rearrange("p u c -> p c u")
             )
 
-        def patch_product(e, make=own, make_scales=own, t0=0, t1=4):
-            codes = make("wz_codes%d_%d" % (e, t0), [P, (t1 - t0) * P], U32)
-            scales = make_scales("wz_scales%d_%d" % (e, t0), [P, (t1 - t0) * P], U8)
-            nc.vector.quantize_mx(out=codes[:].bitcast(FP8X4), scales=scales[:], in_=wz_rounded[e][:, t0 * H : t1 * H])
-            if ("p", e) not in bank:
-                bank["p", e] = psum.tile([P, H], F32, name="bank_p%d" % e)
-            for t in range(t0, t1):
+        def round_wz(e, a=0):
+            if a == 0:
+                wz_rounded[e] = tile("wz_rounded%d" % e, [P, 4 * H], BF16, "wz_rounded0" if e else None)
+            groups = P // pieces[e]
+            nc.vector.tensor_copy(
+                wz_rounded[e][:].rearrange("p (t m j) -> p m j t", t=4, j=4)[:, a * groups : (a + 1) * groups],
+                wz_raw[e][a][:].rearrange("p j (m t) -> p m j t", t=4),
+            )
+
+        def patch_product(e):
+            codes = tile("wz_codes%d" % e, [P, H], U32)
+            scales = tile("wz_scales%d" % e, [P, H], U8)
+            nc.vector.quantize_mx(out=codes[:].bitcast(FP8X4), scales=scales[:], in_=wz_rounded[e][:])
+            bank["p", e] = psum.tile([P, H], F32, name="bank_p%d" % e)
+            for t in range(4):
                 nc.tensor.matmul_mx(
                     out=bank["p", e][:, t * C : (t + 1) * C],
-                    lhsT=codes[:, (t - t0) * P : (t - t0 + 1) * P].bitcast(FP8X4),
-                    lhsT_scale=scales[:, (t - t0) * P : (t - t0 + 1) * P],
+                    lhsT=codes[:, t * P : (t + 1) * P].bitcast(FP8X4),
+                    lhsT_scale=scales[:, t * P : (t + 1) * P],
                     rhs=z_slots[e].bitcast(FP8X4),
                     rhs_scale=z_slot_scales[e],
                     start=True,
                     stop=True,
                 )
 
-        def patch_gelu(e, make):
-            hidden["p", e] = make("hidden_p%d" % e, [P, 4 * C], BF16)
+        def patch_hidden(e):
+            hidden["p", e] = tile("hidden_p%d" % e, [P, 4 * C], BF16)
             nc.scalar.activation(
                 hidden["p", e][:].rearrange("p (c t) -> p c t", t=4),
                 bank["p", e][:].rearrange("p (t c) -> p c t", t=4),
                 GELU,
             )
 
-        def second_product(k, lo, hi, make, make_codes=own):
-            width = (hi - lo) * C
-            codes = make_codes("hidden_codes_%s%d" % (k, lo), [P, width], U32)
-            scales = make("hidden_scales_%s%d" % (k, lo), [P, width], U8)
-            nc.vector.quantize_mx(out=codes[:].bitcast(FP8X4), scales=scales[:], in_=hidden[k, lo][:])
-            sums_in_psum[k, lo] = bank[k, lo][:, H - 2 * width : H].rearrange("p (h c) -> p h c", h=2)
-            for e in range(lo, hi):
-                slots = slice((e - lo) * C, (e - lo + 1) * C)
-                for h in range(2):
-                    nc.tensor.matmul_mx(
-                        out=sums_in_psum[k, lo][:, h, slots],
-                        lhsT=w2[e][:, 0, 2 * P * h : 2 * P * (h + 1)].bitcast(FP4X4),
-                        lhsT_scale=w2_plane[:, e, P * h : P * (h + 1)],
-                        rhs=codes[:, slots].bitcast(FP8X4),
-                        rhs_scale=scales[:, slots],
-                        start=True,
-                        stop=True,
-                    )
+        def second_product(k, e, on=None, at=0, scales_on=None):
+            codes = tile("hidden_codes_%s%d" % (k, e), [P, C], U32, on, at)
+            scales = tile("hidden_scales_%s%d" % (k, e), [P, C], U8, scales_on)
+            nc.vector.quantize_mx(out=codes[:].bitcast(FP8X4), scales=scales[:], in_=hidden[k, e][:])
+            for h in range(2):
+                nc.tensor.matmul_mx(
+                    out=bank[k, e][:, (2 + h) * C : (3 + h) * C],
+                    lhsT=w2[e][:, 0, 2 * P * h : 2 * P * (h + 1)].bitcast(FP4X4),
+                    lhsT_scale=w2_plane[:, e, P * h : P * (h + 1)],
+                    rhs=codes[:].bitcast(FP8X4),
+                    rhs_scale=scales[:],
+                    start=True,
+                    stop=True,
+                )
 
-        def copy_sums(k, lo, hi, make, h0, h1):
-            tile = make("sums_%s%d_%d" % (k, lo, h0), [P, h1 - h0, (hi - lo) * C], F32)
-            nc.scalar.copy(tile[:], sums_in_psum[k, lo][:, h0:h1, :])
-            for h in range(h0, h1):
-                sums[k, lo, h] = tile[:, h - h0, :]
-
-        def scatter_half(k, lo, hi, h):
-            tile, first = gate[k, lo]
+        def apply_gate(k, e, on=None, at=0):
+            gated[k, e] = tile("gated_%s%d" % (k, e), [P, 2, C], F32, on, at)
             nc.vector.tensor_tensor(
-                result[k][h][:].indirect(offsets[k][:, 8 * lo : 8 * hi]),
-                sums[k, lo, h],
-                tile[:, (lo - first) * C : (hi - first) * C],
+                gated[k, e][:],
+                bank[k, e][:, 2 * C : 4 * C].rearrange("p (h c) -> p h c", h=2),
+                gate[k][:, e * C : (e + 1) * C].unsqueeze(1).to_broadcast([P, 2, C]),
                 MULT,
             )
-            if hi == E:
+
+        def scatter(k, e, h, on_vector=False):
+            window = result[k][h][:].indirect(offsets[k][:, 8 * e : 8 * (e + 1)])
+            if on_vector:
+                nc.vector.tensor_copy(window, gated[k, e][:, h, :])
+            else:
+                nc.scalar.activation(window, gated[k, e][:, h, :], COPY)
+            if e == E - 1:
                 columns = slice(0, T) if k == "t" else slice(T, T + Q)
                 nc.sync.dma_start(out[h * P : (h + 1) * P, columns], result[k][h][:])
 
-        def scatter(k, lo, hi, make, h0=0, h1=2):
-            copy_sums(k, lo, hi, make, h0, h1)
-            for h in range(h0, h1):
-                scatter_half(k, lo, hi, h)
-
         for e in range(E):
             text_product(e)
-        pairs_of = [text_gelu(e) for e in range(E)]
-        text_turn(0, 1)
-        text_turn(1, 0)
-        text_turn(2, 2)
-        text_turn(3, 3)
-        second_product("t", 0, 2, own, on_bytes(TEXT_CODES_AT))
-
-        round_wz(0, nc.vector.tensor_copy, FIRST_ON_SCALAR, P)
-        round_wz(0, nc.scalar.copy, 0, FIRST_ON_SCALAR)
-        spread = psum.tile([P, 4, P], F32, name="bank_p0")
-        for j in range(4):
-            nc.tensor.transpose(spread[:, j, :], gate_row[:, j : j + 1].to_broadcast([P, P]), identity[:])
-        gate_t = own("gate_t", [P, S], F32)
-        nc.scalar.copy(gate_t[:].rearrange("p (q j) -> p q j", j=4), spread[:].rearrange("p j q -> p q j"))
         for e in range(E):
-            gate["t", e] = (gate_t, 0)
-        second_product("t", 2, E, on_bytes(GATE_ROW_AT), on_bytes(LATE_TEXT_CODES_AT))
-        patch_product(0, own, on_bytes(TEXT_CODES_AT))
-        scatter("t", 0, 2, own, 0, 1)
-        scatter("t", 0, 2, own, 1, 2)
-
-        round_wz(1, nc.scalar.copy, 0, SECOND_PIECE)
-        scatter("t", 2, E, own, 0, 1)
-        patch_gelu(0, on_bytes(LATE_TEXT_CODES_AT))
-        second_product("p", 0, 1, own)
-        round_wz(1, nc.scalar.copy, SECOND_PIECE, P)
-        patch_product(1, on_bytes(SECOND_WZ_CODES_AT))
-        scatter("t", 2, E, own, 1, 2)
-
-        round_wz(2, nc.scalar.copy, 0, P)
+            text_hidden(e)
+        second_product("t", 0, "z_window", 0, "z_plane")
+        round_wz(0, 0)
+        second_product("t", 1, "wz_raw0_0", 1024)
+        apply_gate("t", 0, "wz_raw0_0")
+        scatter("t", 0, 0)
+        scatter("t", 0, 1)
+        round_wz(0, 1)
+        second_product("t", 2, "wz_raw0_1", 1024)
+        apply_gate("t", 1, "wz_raw0_1")
+        scatter("t", 1, 0)
+        scatter("t", 1, 1)
+        second_product("t", 3, "wz_raw0_1", 1536)
+        patch_product(0)
+        apply_gate("t", 2)
+        scatter("t", 2, 0)
+        scatter("t", 2, 1)
+        patch_hidden(0)
+        round_wz(1)
+        apply_gate("t", 3, "wz_raw1_0")
+        scatter("t", 3, 0)
+        scatter("t", 3, 1)
+        patch_product(1)
+        patch_hidden(1)
+        round_wz(2)
+        second_product("p", 0, "wz_raw2_0")
         patch_product(2)
-        round_wz(3, nc.vector.tensor_copy, 0, P, 2, 4)
-        patch_product(3, own, own, 2, 4)
-        patch_gelu(1, own)
-        second_product("p", 1, 2, own)
-        scatter("p", 0, 1, on_bytes(SECOND_WZ_CODES_AT), 0, 1)
-
-        round_wz(3, nc.scalar.copy, 0, P, 0, 2)
-        patch_product(3, own, own, 0, 2)
-        scatter("p", 0, 1, on_bytes(SECOND_WZ_CODES_AT + 4 * C), 1, 2)
-        patch_gelu(2, own)
-        second_product("p", 2, 3, own)
-        scatter("p", 1, 2, own)
-        patch_gelu(3, own)
-        second_product("p", 3, E, own)
-        scatter("p", 2, 3, own)
-        scatter("p", 3, E, own)
+        patch_hidden(2)
+        round_wz(3)
+        apply_gate("p", 0)
+        second_product("p", 1, "wz_raw3_0")
+        patch_product(3)
+        patch_hidden(3)
+        scatter("p", 0, 1)
+        scatter("p", 0, 0)
+        second_product("p", 2)
+        apply_gate("p", 1, "wz_codes3")
+        scatter("p", 1, 1)
+        second_product("p", 3)
+        scatter("p", 1, 0, True)
+        for e in (2, 3):
+            apply_gate("p", e)
+            scatter("p", e, 1)
+            scatter("p", e, 0, True)

@@ -70,9 +70,11 @@ def tile_moe_mmo_gelu_kernel(
                 queue.dma_start(plane[r:P:32, :, :].bitcast(I32), rows[r:16:4, :, :].bitcast(I32))
 
         gate_row = tile("gate_row", [P, 4], F32)
+        nc.gpsimd.dma_start(gate_row[:], gate1[0].rearrange("(q j) -> q j", j=4))
+        zero_plane(w1_plane)
+        load_plane(nc.gpsimd, w1_plane, w1_scales.rearrange("e g b i -> b (e g) i"))
         zero_plane(x_plane)
         zero_plane(z_plane)
-        load_plane(nc.gpsimd, z_plane, z_scales.rearrange("g b t -> b g t"))
 
         zero = tile("zero", [P, 1], F32)
         ones = tile("ones", [P, QUADRANT], F32)
@@ -81,7 +83,6 @@ def tile_moe_mmo_gelu_kernel(
         identity = tile("identity", [P, P], F32)
         nc.vector.memset(zero[:], 0.0)
         nc.vector.memset(ones[:], 1.0)
-        zero_plane(w1_plane)
         zero_plane(w2_plane)
         nc.vector.tensor_tensor_scan(column_number[:], ones[:], ones[:], 0.0, MULT, ADD)
         nc.vector.memset(identity[:], 0.0)
@@ -102,30 +103,35 @@ def tile_moe_mmo_gelu_kernel(
             for e in range(lo, hi):
                 views[e] = held[:, (e - lo) * passes : (e - lo + 1) * passes, :]
 
+        def load_wz(e, a):
+            width = H // pieces[e]
+            nc.sync.dma_start(wz_raw[e][a][:], wz[e].rearrange("(p j) i -> p j i", j=4)[:, :, a * width : (a + 1) * width])
+
         nc.sync.dma_start(x_window[0][:], x_words[0].rearrange("p t d -> p (t d)").bitcast(I32))
         nc.sync.dma_start(offsets["t"][:], offs)
         nc.sync.dma_start(x_window[1][:], x_words[1].rearrange("p t d -> p (t d)").bitcast(I32))
         load_plane(nc.sync, x_plane, x_scales.rearrange("g b t -> b g t"))
+        load_wz(0, 0)
         load_experts(w1, "w1", w1_words, 0, 1)
-        nc.sync.dma_start(gate_row[:], gate1[0].rearrange("(q j) -> q j", j=4))
         load_experts(w1, "w1", w1_words, 1, 2)
-        load_plane(nc.sync, w1_plane, w1_scales.rearrange("e g b i -> b (e g) i"))
         nc.sync.dma_start(z_window[:], z_words[0].rearrange("p t d -> p (t d)").bitcast(I32))
-        load_experts(w1, "w1", w1_words, 2, E)
         nc.sync.dma_start(offsets["p"][:], offs2)
+        load_experts(w1, "w1", w1_words, 2, E)
         load_experts(w2, "w2", w2_words, 0, E)
+        load_plane(nc.sync, z_plane, z_scales.rearrange("g b t -> b g t"))
+        load_wz(0, 1)
         load_plane(nc.sync, w2_plane, w2_scales.rearrange("e g b n -> b (e g) n"))
-        for e in range(E):
-            width = H // pieces[e]
-            for a in range(pieces[e]):
-                nc.sync.dma_start(wz_raw[e][a][:], wz[e].rearrange("(p j) i -> p j i", j=4)[:, :, a * width : (a + 1) * width])
-        gate = {k: tile("gate_" + k, [P, S], F32) for k in "tp"}
-        nc.sync.dma_start(gate["p"][:], gate2)
+        for e in range(1, E):
+            load_wz(e, 0)
+        gate_p = tile("gate_p", [P, S], F32)
+        nc.sync.dma_start(gate_p[:], gate2)
 
         spread = psum.tile([P, 4, P], F32, name="bank_p3")
         for j in range(4):
             nc.tensor.transpose(spread[:, j, :], gate_row[:, j : j + 1].to_broadcast([P, P]), identity[:])
-        nc.scalar.copy(gate["t"][:].rearrange("p (q j) -> p q j", j=4), spread[:].rearrange("p j q -> p q j"))
+        gate_t = tile("gate_t", [P, S], F32)
+        nc.scalar.copy(gate_t[:].rearrange("p (q j) -> p q j", j=4), spread[:].rearrange("p j q -> p q j"))
+        gate = {"t": gate_t, "p": gate_p}
 
         def gather(name, window, k, dtype, lo, hi, on=None):
             slots = tile("%s%d" % (name, lo), [P, (hi - lo) * C], dtype, on)
@@ -143,7 +149,7 @@ def tile_moe_mmo_gelu_kernel(
         for lo in (0, 2):
             z_slot_scales = z_slot_scales + gather("z_slot_scales", z_plane[:, 0, :], "p", U8, lo, lo + 2)
 
-        bank, hidden, gated, wz_rounded = {}, {}, {}, {}
+        bank, pairs, hidden, sums, wz_rounded = {}, {}, {}, {}, {}
 
         def text_product(e):
             bank["t", e] = psum.tile([P, H], F32, name="bank_t%d" % e)
@@ -158,30 +164,37 @@ def tile_moe_mmo_gelu_kernel(
                     stop=(g == 1),
                 )
 
-        def text_hidden(e):
-            pairs = tile("pairs%d" % e, [P, 2, P, 2], BF16)
-            nc.scalar.activation(pairs[:], bank["t", e][:].rearrange("c (p u v) -> c u p v", u=2, v=2), GELU)
-            turned = bank["t", e][:, 0 : 2 * C].rearrange("p (u c) -> p u c", u=2)
-            words = pairs[:].rearrange("c u p v -> c (u p v)").bitcast(F32)
-            for u in range(2):
-                nc.tensor.transpose(turned[:, u, :], words[:, u * P : (u + 1) * P], identity[:])
-            hidden["t", e] = tile("hidden_t%d" % e, [P, 4 * C], BF16)
-            nc.scalar.copy(
-                hidden["t", e][:].bitcast(F32).rearrange("p (c u) -> p c u", u=2), turned.rearrange("p u c -> p c u")
-            )
+        def text_gelu(e):
+            pairs[e] = tile("pairs%d" % e, [P, 2, P, 2], BF16)
+            nc.scalar.activation(pairs[e][:], bank["t", e][:].rearrange("c (p u v) -> c u p v", u=2, v=2), GELU)
 
-        def round_wz(e, a=0):
+        def hidden_of(k, lo, hi):
+            held = tile("hidden_%s%d" % (k, lo), [P, (hi - lo) * 4 * C], BF16)
+            for e in range(lo, hi):
+                hidden[k, e] = held[:, (e - lo) * 4 * C : (e - lo + 1) * 4 * C]
+            hidden[k, lo, hi] = held[:]
+
+        def text_turn(lo, hi, host):
+            turned = bank["t", host][:, 0 : (hi - lo) * 2 * C].rearrange("p (e u c) -> p e u c", u=2, c=C)
+            for e in range(lo, hi):
+                words = pairs[e][:].rearrange("c u p v -> c (u p v)").bitcast(F32)
+                for u in range(2):
+                    nc.tensor.transpose(turned[:, e - lo, u, :], words[:, u * P : (u + 1) * P], identity[:])
+            target = hidden["t", lo, hi] if hi - lo > 1 else hidden["t", lo]
+            nc.scalar.copy(target.bitcast(F32).rearrange("p (e c u) -> p e c u", u=2, c=C), turned.rearrange("p e u c -> p e c u"))
+
+        def round_wz(e, a=0, copy=nc.vector.tensor_copy):
             if a == 0:
-                wz_rounded[e] = tile("wz_rounded%d" % e, [P, 4 * H], BF16, "wz_rounded0" if e else None)
+                wz_rounded[e] = tile("wz_rounded%d" % e, [P, 4 * H], BF16)
             groups = P // pieces[e]
-            nc.vector.tensor_copy(
+            copy(
                 wz_rounded[e][:].rearrange("p (t m j) -> p m j t", t=4, j=4)[:, a * groups : (a + 1) * groups],
                 wz_raw[e][a][:].rearrange("p j (m t) -> p m j t", t=4),
             )
 
-        def patch_product(e):
+        def patch_product(e, scales_on=None):
             codes = tile("wz_codes%d" % e, [P, H], U32)
-            scales = tile("wz_scales%d" % e, [P, H], U8)
+            scales = tile("wz_scales%d" % e, [P, H], U8, scales_on)
             nc.vector.quantize_mx(out=codes[:].bitcast(FP8X4), scales=scales[:], in_=wz_rounded[e][:])
             bank["p", e] = psum.tile([P, H], F32, name="bank_p%d" % e)
             for t in range(4):
@@ -196,91 +209,94 @@ def tile_moe_mmo_gelu_kernel(
                 )
 
         def patch_hidden(e):
-            hidden["p", e] = tile("hidden_p%d" % e, [P, 4 * C], BF16)
             nc.scalar.activation(
-                hidden["p", e][:].rearrange("p (c t) -> p c t", t=4),
+                hidden["p", e].rearrange("p (c t) -> p c t", t=4),
                 bank["p", e][:].rearrange("p (t c) -> p c t", t=4),
                 GELU,
             )
 
-        def second_product(k, e, on=None, at=0, scales_on=None):
-            codes = tile("hidden_codes_%s%d" % (k, e), [P, C], U32, on, at)
-            scales = tile("hidden_scales_%s%d" % (k, e), [P, C], U8, scales_on)
-            nc.vector.quantize_mx(out=codes[:].bitcast(FP8X4), scales=scales[:], in_=hidden[k, e][:])
-            for h in range(2):
-                nc.tensor.matmul_mx(
-                    out=bank[k, e][:, (2 + h) * C : (3 + h) * C],
-                    lhsT=w2[e][:, 0, 2 * P * h : 2 * P * (h + 1)].bitcast(FP4X4),
-                    lhsT_scale=w2_plane[:, e, P * h : P * (h + 1)],
-                    rhs=codes[:].bitcast(FP8X4),
-                    rhs_scale=scales[:],
-                    start=True,
-                    stop=True,
-                )
+        def second_product(k, lo, hi, hosts, on=None, at=0, scales_on=None):
+            width = (hi - lo) * C
+            codes = tile("hidden_codes_%s%d" % (k, lo), [P, width], U32, on, at)
+            scales = tile("hidden_scales_%s%d" % (k, lo), [P, width], U8, scales_on)
+            source = hidden[k, lo, hi] if hi - lo > 1 else hidden[k, lo]
+            nc.vector.quantize_mx(out=codes[:].bitcast(FP8X4), scales=scales[:], in_=source)
+            for h in (1, 0):
+                first = H - width * (1 if hosts[0] != hosts[1] else 2 - h)
+                sums[k, lo, h] = bank[k, hosts[h]][:, first : first + width]
+                for e in range(lo, hi):
+                    slots = slice((e - lo) * C, (e - lo + 1) * C)
+                    nc.tensor.matmul_mx(
+                        out=sums[k, lo, h][:, slots],
+                        lhsT=w2[e][:, 0, 2 * P * h : 2 * P * (h + 1)].bitcast(FP4X4),
+                        lhsT_scale=w2_plane[:, e, P * h : P * (h + 1)],
+                        rhs=codes[:, slots].bitcast(FP8X4),
+                        rhs_scale=scales[:, slots],
+                        start=True,
+                        stop=True,
+                    )
 
-        def apply_gate(k, e, on=None, at=0):
-            gated[k, e] = tile("gated_%s%d" % (k, e), [P, 2, C], F32, on, at)
-            nc.vector.tensor_tensor(
-                gated[k, e][:],
-                bank[k, e][:, 2 * C : 4 * C].rearrange("p (h c) -> p h c", h=2),
-                gate[k][:, e * C : (e + 1) * C].unsqueeze(1).to_broadcast([P, 2, C]),
-                MULT,
-            )
+        def apply_gate(k, lo, hi, h, target):
+            nc.vector.tensor_tensor(target, sums[k, lo, h], gate[k][:, lo * C : hi * C], MULT)
 
-        def scatter(k, e, h, on_vector=False):
-            window = result[k][h][:].indirect(offsets[k][:, 8 * e : 8 * (e + 1)])
+        def scatter(k, lo, hi, h, source, on_vector=False):
+            window = result[k][h][:].indirect(offsets[k][:, 8 * lo : 8 * hi])
             if on_vector:
-                nc.vector.tensor_copy(window, gated[k, e][:, h, :])
+                nc.vector.tensor_copy(window, source)
             else:
-                nc.scalar.activation(window, gated[k, e][:, h, :], COPY)
-            if e == E - 1:
+                nc.scalar.activation(window, source, COPY)
+            if hi == E:
                 columns = slice(0, T) if k == "t" else slice(T, T + Q)
                 nc.sync.dma_start(out[h * P : (h + 1) * P, columns], result[k][h][:])
 
+        def gate_and_scatter(k, lo, hi, h, on=None, at=0):
+            gated = tile("gated_%s%d_%d" % (k, lo, h), [P, (hi - lo) * C], F32, on, at)
+            apply_gate(k, lo, hi, h, gated[:])
+            scatter(k, lo, hi, h, gated[:])
+
+        round_wz(0, 0, nc.scalar.copy)
+        for lo in (0, 2):
+            hidden_of("t", lo, lo + 2)
+        hidden_of("p", 0, 2)
+        hidden_of("p", 2, 3)
+        hidden_of("p", 3, 4)
         for e in range(E):
             text_product(e)
         for e in range(E):
-            text_hidden(e)
-        second_product("t", 0, "z_window", 0, "z_plane")
-        round_wz(0, 0)
-        second_product("t", 1, "wz_raw0_0", 1024)
-        apply_gate("t", 0, "wz_raw0_0")
-        scatter("t", 0, 0)
-        scatter("t", 0, 1)
+            text_gelu(e)
+            if e < 2:
+                text_turn(e, e + 1, e)
+        second_product("t", 0, 2, (0, 1), None, 0, "z_plane")
         round_wz(0, 1)
-        second_product("t", 2, "wz_raw0_1", 1024)
-        apply_gate("t", 1, "wz_raw0_1")
-        scatter("t", 1, 0)
-        scatter("t", 1, 1)
-        second_product("t", 3, "wz_raw0_1", 1536)
-        patch_product(0)
-        apply_gate("t", 2)
-        scatter("t", 2, 0)
-        scatter("t", 2, 1)
+        gate_and_scatter("t", 0, 2, 1, "wz_raw0_1")
+        text_turn(2, E, 1)
+        patch_product(0, "hidden_codes_t0")
         patch_hidden(0)
         round_wz(1)
-        apply_gate("t", 3, "wz_raw1_0")
-        scatter("t", 3, 0)
-        scatter("t", 3, 1)
+        gate_and_scatter("t", 0, 2, 0, "wz_raw1_0")
         patch_product(1)
         patch_hidden(1)
+        second_product("t", 2, E, (2, 3), "wz_rounded1")
         round_wz(2)
-        second_product("p", 0, "wz_raw2_0")
+        gate_and_scatter("t", 2, E, 1, "wz_raw2_0")
         patch_product(2)
         patch_hidden(2)
+        second_product("p", 0, 2, (0, 1), "wz_rounded2")
         round_wz(3)
-        apply_gate("p", 0)
-        second_product("p", 1, "wz_raw3_0")
+        gate_and_scatter("t", 2, E, 0, "wz_raw3_0")
         patch_product(3)
+        second_product("p", 2, 3, (2, 2), "wz_rounded3")
         patch_hidden(3)
-        scatter("p", 0, 1)
-        scatter("p", 0, 0)
-        second_product("p", 2)
-        apply_gate("p", 1, "wz_codes3")
-        scatter("p", 1, 1)
-        second_product("p", 3)
-        scatter("p", 1, 0, True)
-        for e in (2, 3):
-            apply_gate("p", e)
-            scatter("p", e, 1)
-            scatter("p", e, 0, True)
+        gated = {(lo, h): tile("gated_p%d_%d" % (lo, h), [P, (hi - lo) * C], F32) for lo, hi in ((0, 2), (2, 3), (3, E)) for h in range(2)}
+        for h in range(2):
+            apply_gate("p", 0, 2, h, gated[0, h][:])
+        for h in range(2):
+            scatter("p", 0, 2, h, gated[0, h][:], h == 0)
+        for h in (1, 0):
+            apply_gate("p", 2, 3, h, gated[2, h][:])
+        second_product("p", 3, E, (3, 3))
+        for h in (1, 0):
+            scatter("p", 2, 3, h, gated[2, h][:], h == 0)
+        for h in (1, 0):
+            apply_gate("p", 3, E, h, gated[3, h][:])
+            scatter("p", 3, E, h, gated[3, h][:], h == 0)

@@ -55,7 +55,7 @@ def tile_moe_mmo_gelu_kernel(
         z_plane = tile("z_plane", [P, 1, Q], U8)
         w1_plane = tile("w1_plane", [P, 2 * E, H], U8)
         w2_plane = tile("w2_plane", [P, E, N], U8)
-        pieces = [2, 1, 1, 1]
+        pieces = [1, 1, 1, 1]
         wz_raw = [[tile("wz_raw%d_%d" % (e, a), [P, 4, H // pieces[e]], F32) for a in range(pieces[e])] for e in range(E)]
         result = {
             "t": [tile("result_t%d" % h, [P, T], F32) for h in range(2)],
@@ -70,11 +70,10 @@ def tile_moe_mmo_gelu_kernel(
                 queue.dma_start(plane[r:P:32, :, :].bitcast(I32), rows[r:16:4, :, :].bitcast(I32))
 
         gate_row = tile("gate_row", [P, 4], F32)
-        nc.gpsimd.dma_start(gate_row[:], gate1[0].rearrange("(q j) -> q j", j=4))
-        zero_plane(w1_plane)
-        load_plane(nc.gpsimd, w1_plane, w1_scales.rearrange("e g b i -> b (e g) i"))
         zero_plane(x_plane)
         zero_plane(z_plane)
+        load_plane(nc.gpsimd, z_plane, z_scales.rearrange("g b t -> b g t"))
+        zero_plane(w1_plane)
 
         zero = tile("zero", [P, 1], F32)
         ones = tile("ones", [P, QUADRANT], F32)
@@ -111,17 +110,16 @@ def tile_moe_mmo_gelu_kernel(
         nc.sync.dma_start(offsets["t"][:], offs)
         nc.sync.dma_start(x_window[1][:], x_words[1].rearrange("p t d -> p (t d)").bitcast(I32))
         load_plane(nc.sync, x_plane, x_scales.rearrange("g b t -> b g t"))
-        load_wz(0, 0)
         load_experts(w1, "w1", w1_words, 0, 1)
+        nc.sync.dma_start(gate_row[:], gate1[0].rearrange("(q j) -> q j", j=4))
+        load_plane(nc.sync, w1_plane, w1_scales.rearrange("e g b i -> b (e g) i"))
         load_experts(w1, "w1", w1_words, 1, 2)
         nc.sync.dma_start(z_window[:], z_words[0].rearrange("p t d -> p (t d)").bitcast(I32))
         nc.sync.dma_start(offsets["p"][:], offs2)
         load_experts(w1, "w1", w1_words, 2, E)
         load_experts(w2, "w2", w2_words, 0, E)
-        load_plane(nc.sync, z_plane, z_scales.rearrange("g b t -> b g t"))
-        load_wz(0, 1)
         load_plane(nc.sync, w2_plane, w2_scales.rearrange("e g b n -> b (e g) n"))
-        for e in range(1, E):
+        for e in range(E):
             load_wz(e, 0)
         gate_p = tile("gate_p", [P, S], F32)
         nc.sync.dma_start(gate_p[:], gate2)
@@ -192,21 +190,25 @@ def tile_moe_mmo_gelu_kernel(
                 wz_raw[e][a][:].rearrange("p j (m t) -> p m j t", t=4),
             )
 
-        def patch_product(e, scales_on=None):
-            codes = tile("wz_codes%d" % e, [P, H], U32)
-            scales = tile("wz_scales%d" % e, [P, H], U8, scales_on)
-            nc.vector.quantize_mx(out=codes[:].bitcast(FP8X4), scales=scales[:], in_=wz_rounded[e][:])
+        def patch_product(e, parts=1):
             bank["p", e] = psum.tile([P, H], F32, name="bank_p%d" % e)
-            for t in range(4):
-                nc.tensor.matmul_mx(
-                    out=bank["p", e][:, t * C : (t + 1) * C],
-                    lhsT=codes[:, t * P : (t + 1) * P].bitcast(FP8X4),
-                    lhsT_scale=scales[:, t * P : (t + 1) * P],
-                    rhs=z_slots[e].bitcast(FP8X4),
-                    rhs_scale=z_slot_scales[e],
-                    start=True,
-                    stop=True,
-                )
+            width = H // parts
+            for a in range(parts):
+                codes = tile("wz_codes%d_%d" % (e, a), [P, width], U32)
+                scales = tile("wz_scales%d_%d" % (e, a), [P, width], U8)
+                source = wz_rounded[e][:, 4 * a * width : 4 * (a + 1) * width]
+                nc.vector.quantize_mx(out=codes[:].bitcast(FP8X4), scales=scales[:], in_=source)
+                for u in range(width // P):
+                    t = a * width // P + u
+                    nc.tensor.matmul_mx(
+                        out=bank["p", e][:, t * C : (t + 1) * C],
+                        lhsT=codes[:, u * P : (u + 1) * P].bitcast(FP8X4),
+                        lhsT_scale=scales[:, u * P : (u + 1) * P],
+                        rhs=z_slots[e].bitcast(FP8X4),
+                        rhs_scale=z_slot_scales[e],
+                        start=True,
+                        stop=True,
+                    )
 
         def patch_hidden(e):
             nc.scalar.activation(
@@ -249,17 +251,25 @@ def tile_moe_mmo_gelu_kernel(
                 columns = slice(0, T) if k == "t" else slice(T, T + Q)
                 nc.sync.dma_start(out[h * P : (h + 1) * P, columns], result[k][h][:])
 
-        def gate_and_scatter(k, lo, hi, h, on=None, at=0):
+        def gate_and_scatter(k, lo, hi, h, on=None, at=0, on_vector=False):
             gated = tile("gated_%s%d_%d" % (k, lo, h), [P, (hi - lo) * C], F32, on, at)
             apply_gate(k, lo, hi, h, gated[:])
-            scatter(k, lo, hi, h, gated[:])
+            scatter(k, lo, hi, h, gated[:], on_vector)
 
-        round_wz(0, 0, nc.scalar.copy)
+        def gate_both(e):
+            gated = tile("gated_p%d" % e, [P, 2, C], F32)
+            nc.vector.tensor_tensor(
+                gated[:],
+                bank["p", e][:, 2 * C : 4 * C].rearrange("p (h c) -> p h c", h=2),
+                gate["p"][:, e * C : (e + 1) * C].unsqueeze(1).to_broadcast([P, 2, C]),
+                MULT,
+            )
+            return gated
+
         for lo in (0, 2):
             hidden_of("t", lo, lo + 2)
-        hidden_of("p", 0, 2)
-        hidden_of("p", 2, 3)
-        hidden_of("p", 3, 4)
+        for e in range(E):
+            hidden_of("p", e, e + 1)
         for e in range(E):
             text_product(e)
         for e in range(E):
@@ -267,36 +277,35 @@ def tile_moe_mmo_gelu_kernel(
             if e < 2:
                 text_turn(e, e + 1, e)
         second_product("t", 0, 2, (0, 1), None, 0, "z_plane")
-        round_wz(0, 1)
-        gate_and_scatter("t", 0, 2, 1, "wz_raw0_1")
+        gate_and_scatter("t", 0, 2, 1)
         text_turn(2, E, 1)
-        patch_product(0, "hidden_codes_t0")
+        round_wz(0)
+        gate_and_scatter("t", 0, 2, 0, "wz_raw0_0")
+        patch_product(0)
         patch_hidden(0)
+        second_product("t", 2, E, (2, 3), "wz_rounded0")
         round_wz(1)
-        gate_and_scatter("t", 0, 2, 0, "wz_raw1_0")
+        gate_and_scatter("t", 2, E, 1, "wz_raw1_0")
         patch_product(1)
         patch_hidden(1)
-        second_product("t", 2, E, (2, 3), "wz_rounded1")
         round_wz(2)
-        gate_and_scatter("t", 2, E, 1, "wz_raw2_0")
+        gate_and_scatter("t", 2, E, 0, "wz_raw2_0")
+        second_product("p", 0, 1, (0, 0), "wz_raw2_0", 1024)
         patch_product(2)
         patch_hidden(2)
-        second_product("p", 0, 2, (0, 1), "wz_rounded2")
         round_wz(3)
-        gate_and_scatter("t", 2, E, 0, "wz_raw3_0")
-        patch_product(3)
-        second_product("p", 2, 3, (2, 2), "wz_rounded3")
+        gated = gate_both(0)
+        for h in (1, 0):
+            scatter("p", 0, 1, h, gated[:, h, :])
+        second_product("p", 1, 2, (1, 1), "wz_raw3_0")
+        patch_product(3, 2)
         patch_hidden(3)
-        gated = {(lo, h): tile("gated_p%d_%d" % (lo, h), [P, (hi - lo) * C], F32) for lo, hi in ((0, 2), (2, 3), (3, E)) for h in range(2)}
-        for h in range(2):
-            apply_gate("p", 0, 2, h, gated[0, h][:])
-        for h in range(2):
-            scatter("p", 0, 2, h, gated[0, h][:], h == 0)
-        for h in (1, 0):
-            apply_gate("p", 2, 3, h, gated[2, h][:])
+        second_product("p", 2, 3, (2, 2), "wz_rounded3", 2048)
+        gate_and_scatter("p", 1, 2, 1, None, 0, True)
+        gate_and_scatter("p", 1, 2, 0, "wz_codes3_1")
+        gate_and_scatter("p", 2, 3, 0)
         second_product("p", 3, E, (3, 3))
-        for h in (1, 0):
-            scatter("p", 2, 3, h, gated[2, h][:], h == 0)
-        for h in (1, 0):
-            apply_gate("p", 3, E, h, gated[3, h][:])
-            scatter("p", 3, E, h, gated[3, h][:], h == 0)
+        gate_and_scatter("p", 2, 3, 1, "hidden_p3", 0, True)
+        gated = gate_both(3)
+        for h in (0, 1):
+            scatter("p", 3, E, h, gated[:, h, :], h == 1)

@@ -65,14 +65,15 @@ def tile_moe_mmo_gelu_kernel(
         def zero_plane(plane):
             nc.vector.memset(plane[:].rearrange("p a w -> p (a w)").bitcast(I32), 0)
 
-        def load_plane(queue, plane, rows):
-            for r in range(4):
+        def load_plane(queue, plane, rows, lo=0, hi=4):
+            for r in range(lo, hi):
                 queue.dma_start(plane[r:P:32, :, :].bitcast(I32), rows[r:16:4, :, :].bitcast(I32))
 
         gate_row = tile("gate_row", [P, 4], F32)
+        nc.gpsimd.dma_start(gate_row[:], gate1[0].rearrange("(q j) -> q j", j=4))
         zero_plane(x_plane)
         zero_plane(z_plane)
-        load_plane(nc.gpsimd, z_plane, z_scales.rearrange("g b t -> b g t"))
+        load_plane(nc.gpsimd, z_plane, z_scales.rearrange("g b t -> b g t"), 0, 2)
         zero_plane(w1_plane)
 
         zero = tile("zero", [P, 1], F32)
@@ -111,11 +112,11 @@ def tile_moe_mmo_gelu_kernel(
         nc.sync.dma_start(x_window[1][:], x_words[1].rearrange("p t d -> p (t d)").bitcast(I32))
         load_plane(nc.sync, x_plane, x_scales.rearrange("g b t -> b g t"))
         load_experts(w1, "w1", w1_words, 0, 1)
-        nc.sync.dma_start(gate_row[:], gate1[0].rearrange("(q j) -> q j", j=4))
         load_plane(nc.sync, w1_plane, w1_scales.rearrange("e g b i -> b (e g) i"))
         load_experts(w1, "w1", w1_words, 1, 2)
         nc.sync.dma_start(z_window[:], z_words[0].rearrange("p t d -> p (t d)").bitcast(I32))
         nc.sync.dma_start(offsets["p"][:], offs2)
+        load_plane(nc.sync, z_plane, z_scales.rearrange("g b t -> b g t"), 2, 4)
         load_experts(w1, "w1", w1_words, 2, E)
         load_experts(w2, "w2", w2_words, 0, E)
         load_plane(nc.sync, w2_plane, w2_scales.rearrange("e g b n -> b (e g) n"))

@@ -23,6 +23,7 @@ E, C = 4, 128
 H, N = 512, 256
 S = E * C
 FLOPS = 2 * S * (K * H + L * H + 2 * H * N)
+Z_WINDOW = 704
 QUADRANT = 32
 
 
@@ -50,9 +51,9 @@ def tile_moe_mmo_gelu_kernel(
 
         offsets = {k: lists.tile([P, S // 16], U16, name="offsets_" + k) for k in "tp"}
         x_window = [tile("x_window%d" % g, [P, T], I32) for g in range(2)]
-        z_window = tile("z_window", [P, Q], I32)
+        z_window = tile("z_window", [P, Z_WINDOW], I32)
         x_plane = tile("x_plane", [P, 2, T], U8)
-        z_plane = tile("z_plane", [P, 1, Q], U8)
+        z_plane = tile("z_plane", [P, 1, Z_WINDOW], U8)
         w1_plane = tile("w1_plane", [P, 2 * E, H], U8)
         w2_plane = tile("w2_plane", [P, E, N], U8)
         pieces = [1, 1, 1, 1]
@@ -67,7 +68,7 @@ def tile_moe_mmo_gelu_kernel(
 
         def load_plane(queue, plane, rows, lo=0, hi=4):
             for r in range(lo, hi):
-                queue.dma_start(plane[r:P:32, :, :].bitcast(I32), rows[r:16:4, :, :].bitcast(I32))
+                queue.dma_start(plane[r:P:32, :, 0 : rows.shape[2]].bitcast(I32), rows[r:16:4, :, :].bitcast(I32))
 
         gate_row = tile("gate_row", [P, 4], F32)
         nc.gpsimd.dma_start(gate_row[:], gate1[0].rearrange("(q j) -> q j", j=4))
@@ -84,6 +85,7 @@ def tile_moe_mmo_gelu_kernel(
         nc.vector.memset(zero[:], 0.0)
         nc.vector.memset(ones[:], 1.0)
         zero_plane(w2_plane)
+        nc.vector.memset(z_window[:, Q:Z_WINDOW], 0)
         nc.vector.tensor_tensor_scan(column_number[:], ones[:], ones[:], 0.0, MULT, ADD)
         nc.vector.memset(identity[:], 0.0)
         nc.vector.transpose(row_number[:], column_number[:])
@@ -114,9 +116,9 @@ def tile_moe_mmo_gelu_kernel(
         load_experts(w1, "w1", w1_words, 0, 1)
         load_plane(nc.sync, w1_plane, w1_scales.rearrange("e g b i -> b (e g) i"))
         load_experts(w1, "w1", w1_words, 1, 2)
-        nc.sync.dma_start(z_window[:], z_words[0].rearrange("p t d -> p (t d)").bitcast(I32))
-        nc.sync.dma_start(offsets["p"][:], offs2)
+        nc.sync.dma_start(z_window[:, 0:Q], z_words[0].rearrange("p t d -> p (t d)").bitcast(I32))
         load_plane(nc.sync, z_plane, z_scales.rearrange("g b t -> b g t"), 2, 4)
+        nc.sync.dma_start(offsets["p"][:], offs2)
         load_experts(w1, "w1", w1_words, 2, E)
         load_experts(w2, "w2", w2_words, 0, E)
         load_plane(nc.sync, w2_plane, w2_scales.rearrange("e g b n -> b (e g) n"))
@@ -139,16 +141,13 @@ def tile_moe_mmo_gelu_kernel(
 
         x_slots = [gather("x_slots%d_" % g, x_window[g][:].bitcast(U32), "t", U32, 0, E) for g in range(2)]
         x_slot_scales = [[], []]
-        for lo, hi in [(0, 1), (1, 2), (2, E)]:
+        for lo, hi in [(0, 1), (1, E)]:
             for g in range(2):
                 x_slot_scales[g] = x_slot_scales[g] + gather("x_slot_scales%d_" % g, x_plane[:, g, :], "t", U8, lo, hi)
-        z_slots, z_slot_scales = [], []
-        for lo in (0, 2):
-            z_slots = z_slots + gather("z_slots", z_window[:].bitcast(U32), "p", U32, lo, lo + 2)
-        for lo in (0, 2):
-            z_slot_scales = z_slot_scales + gather("z_slot_scales", z_plane[:, 0, :], "p", U8, lo, lo + 2)
+        z_slots = gather("z_slots", z_window[:].bitcast(U32), "p", U32, 0, E)
+        z_slot_scales = gather("z_slot_scales", z_plane[:, 0, :], "p", U8, 0, E)
 
-        bank, pairs, hidden, sums, wz_rounded = {}, {}, {}, {}, {}
+        bank, pairs, hidden, sums, both, wz_rounded = {}, {}, {}, {}, {}, {}
 
         def text_product(e):
             bank["t", e] = psum.tile([P, H], F32, name="bank_t%d" % e)
@@ -182,34 +181,32 @@ def tile_moe_mmo_gelu_kernel(
             target = hidden["t", lo, hi] if hi - lo > 1 else hidden["t", lo]
             nc.scalar.copy(target.bitcast(F32).rearrange("p (e c u) -> p e c u", u=2, c=C), turned.rearrange("p e u c -> p e c u"))
 
-        def round_wz(e, a=0, copy=nc.vector.tensor_copy):
-            if a == 0:
-                wz_rounded[e] = tile("wz_rounded%d" % e, [P, 4 * H], BF16)
-            groups = P // pieces[e]
-            copy(
-                wz_rounded[e][:].rearrange("p (t m j) -> p m j t", t=4, j=4)[:, a * groups : (a + 1) * groups],
-                wz_raw[e][a][:].rearrange("p j (m t) -> p m j t", t=4),
-            )
+        def round_wz(e):
+            for a in range(2):
+                wz_rounded[e, a] = tile("wz_rounded%d_%d" % (e, a), [P, 2 * H], BF16)
+                nc.vector.tensor_copy(
+                    wz_rounded[e, a][:].rearrange("p (t m j) -> p m j t", t=2, j=4),
+                    wz_raw[e][0][:].rearrange("p j (m t) -> p m j t", t=4)[:, :, :, 2 * a : 2 * a + 2],
+                )
 
-        def patch_product(e, parts=1):
-            bank["p", e] = psum.tile([P, H], F32, name="bank_p%d" % e)
-            width = H // parts
-            for a in range(parts):
-                codes = tile("wz_codes%d_%d" % (e, a), [P, width], U32)
-                scales = tile("wz_scales%d_%d" % (e, a), [P, width], U8)
-                source = wz_rounded[e][:, 4 * a * width : 4 * (a + 1) * width]
-                nc.vector.quantize_mx(out=codes[:].bitcast(FP8X4), scales=scales[:], in_=source)
-                for u in range(width // P):
-                    t = a * width // P + u
-                    nc.tensor.matmul_mx(
-                        out=bank["p", e][:, t * C : (t + 1) * C],
-                        lhsT=codes[:, u * P : (u + 1) * P].bitcast(FP8X4),
-                        lhsT_scale=scales[:, u * P : (u + 1) * P],
-                        rhs=z_slots[e].bitcast(FP8X4),
-                        rhs_scale=z_slot_scales[e],
-                        start=True,
-                        stop=True,
-                    )
+        def patch_product(e, a):
+            if a == 0:
+                bank["p", e] = psum.tile([P, H], F32, name="bank_p%d" % e)
+            codes = tile("wz_codes%d_%d" % (e, a), [P, 2 * P], U32)
+            if (e, a) == (3, 1):
+                places["free"] = places["free"] + 2048
+            scales = tile("wz_scales%d_%d" % (e, a), [P, 2 * P], U8)
+            nc.vector.quantize_mx(out=codes[:].bitcast(FP8X4), scales=scales[:], in_=wz_rounded[e, a][:])
+            for u in range(2):
+                nc.tensor.matmul_mx(
+                    out=bank["p", e][:, (2 * a + u) * C : (2 * a + u + 1) * C],
+                    lhsT=codes[:, u * P : (u + 1) * P].bitcast(FP8X4),
+                    lhsT_scale=scales[:, u * P : (u + 1) * P],
+                    rhs=z_slots[e].bitcast(FP8X4),
+                    rhs_scale=z_slot_scales[e],
+                    start=True,
+                    stop=True,
+                )
 
         def patch_hidden(e):
             nc.scalar.activation(
@@ -218,7 +215,7 @@ def tile_moe_mmo_gelu_kernel(
                 GELU,
             )
 
-        def second_product(k, lo, hi, hosts, on=None, at=0, scales_on=None):
+        def second_product(k, lo, hi, hosts, on=None, at=0, scales_on=None, by_expert=False):
             width = (hi - lo) * C
             codes = tile("hidden_codes_%s%d" % (k, lo), [P, width], U32, on, at)
             scales = tile("hidden_scales_%s%d" % (k, lo), [P, width], U8, scales_on)
@@ -229,8 +226,9 @@ def tile_moe_mmo_gelu_kernel(
                 sums[k, lo, h] = bank[k, hosts[h]][:, first : first + width]
                 for e in range(lo, hi):
                     slots = slice((e - lo) * C, (e - lo + 1) * C)
+                    both[k, e] = bank[k, e][:, 2 * C : 4 * C].rearrange("p (h c) -> p h c", h=2)
                     nc.tensor.matmul_mx(
-                        out=sums[k, lo, h][:, slots],
+                        out=both[k, e][:, h, :] if by_expert else sums[k, lo, h][:, slots],
                         lhsT=w2[e][:, 0, 2 * P * h : 2 * P * (h + 1)].bitcast(FP4X4),
                         lhsT_scale=w2_plane[:, e, P * h : P * (h + 1)],
                         rhs=codes[:, slots].bitcast(FP8X4),
@@ -257,56 +255,74 @@ def tile_moe_mmo_gelu_kernel(
             apply_gate(k, lo, hi, h, gated[:])
             scatter(k, lo, hi, h, gated[:], on_vector)
 
-        def gate_both(e):
-            gated = tile("gated_p%d" % e, [P, 2, C], F32)
+        def gate_both(k, e, target):
             nc.vector.tensor_tensor(
-                gated[:],
-                bank["p", e][:, 2 * C : 4 * C].rearrange("p (h c) -> p h c", h=2),
-                gate["p"][:, e * C : (e + 1) * C].unsqueeze(1).to_broadcast([P, 2, C]),
+                target,
+                both[k, e],
+                gate[k][:, e * C : (e + 1) * C].unsqueeze(1).to_broadcast([P, 2, C]),
                 MULT,
             )
-            return gated
 
-        for lo in (0, 2):
-            hidden_of("t", lo, lo + 2)
-        for e in range(E):
-            hidden_of("p", e, e + 1)
+        def gate_and_scatter_both(k, e, on, at=0):
+            gated = tile("gated_%s%d" % (k, e), [P, 2, C], F32, on, at)
+            gate_both(k, e, gated[:])
+            for h in (1, 0):
+                scatter(k, e, e + 1, h, gated[:, h, :])
+
+        hidden_of("t", 0, 2)
+        hidden_of("t", 2, 3)
+        hidden_of("t", 3, E)
+        hidden_of("p", 0, 2)
+        hidden_of("p", 2, 3)
+        hidden_of("p", 3, E)
         for e in range(E):
             text_product(e)
         for e in range(E):
             text_gelu(e)
             if e < 2:
                 text_turn(e, e + 1, e)
-        second_product("t", 0, 2, (0, 1), None, 0, "z_plane")
+        second_product("t", 0, 2, (0, 1), "z_window")
+        text_turn(2, 3, 0)
         gate_and_scatter("t", 0, 2, 1)
-        text_turn(2, E, 1)
+        text_turn(3, E, 1)
+
         round_wz(0)
+        patch_product(0, 0)
         gate_and_scatter("t", 0, 2, 0, "wz_raw0_0")
-        patch_product(0)
+        patch_product(0, 1)
         patch_hidden(0)
-        second_product("t", 2, E, (2, 3), "wz_rounded0")
+        second_product("t", 2, 3, (2, 2), "wz_raw0_0", 1024)
+
         round_wz(1)
-        gate_and_scatter("t", 2, E, 1, "wz_raw1_0")
-        patch_product(1)
+        patch_product(1, 0)
+        gate_and_scatter_both("t", 2, "wz_raw1_0")
+        patch_product(1, 1)
         patch_hidden(1)
+        second_product("t", 3, E, (3, 3), "wz_raw1_0", 1024)
+
         round_wz(2)
-        gate_and_scatter("t", 2, E, 0, "wz_raw2_0")
-        second_product("p", 0, 1, (0, 0), "wz_raw2_0", 1024)
-        patch_product(2)
+        patch_product(2, 0)
+        gate_and_scatter_both("t", 3, "wz_raw2_0")
+        patch_product(2, 1)
         patch_hidden(2)
+        second_product("p", 0, 2, (0, 1), "wz_raw2_0", 1024, None, True)
+
         round_wz(3)
-        gated = gate_both(0)
-        for h in (1, 0):
-            scatter("p", 0, 1, h, gated[:, h, :])
-        second_product("p", 1, 2, (1, 1), "wz_raw3_0")
-        patch_product(3, 2)
+        patch_product(3, 0)
+        first = tile("gated_p0", [P, 2, C], F32, "wz_raw3_0")
+        gate_both("p", 0, first[:])
+        scatter("p", 0, 1, 1, first[:, 1, :])
+        patch_product(3, 1)
         patch_hidden(3)
-        second_product("p", 2, 3, (2, 2), "wz_rounded3", 2048)
-        gate_and_scatter("p", 1, 2, 1, None, 0, True)
-        gate_and_scatter("p", 1, 2, 0, "wz_codes3_1")
-        gate_and_scatter("p", 2, 3, 0)
+        second_product("p", 2, 3, (2, 2), "wz_raw3_0", 1024)
+        scatter("p", 0, 1, 0, first[:, 0, :], True)
+        rest = tile("gated_rest", [P, 2, 3 * C], F32, "wz_codes3_1")
+        gate_both("p", 1, rest[:, :, 0:C])
+        scatter("p", 1, 2, 0, rest[:, 0, 0:C])
+        gate_both("p", 2, rest[:, :, C : 2 * C])
+        scatter("p", 1, 3, 1, rest[:, 1, 0 : 2 * C])
         second_product("p", 3, E, (3, 3))
-        gate_and_scatter("p", 2, 3, 1, "hidden_p3", 0, True)
-        gated = gate_both(3)
-        for h in (0, 1):
-            scatter("p", 3, E, h, gated[:, h, :], h == 1)
+        scatter("p", 2, 3, 0, rest[:, 0, C : 2 * C], True)
+        gate_both("p", 3, rest[:, :, 2 * C : 3 * C])
+        for h in (1, 0):
+            scatter("p", 3, E, h, rest[:, h, 2 * C : 3 * C], h == 0)

@@ -122,10 +122,11 @@ def tile_moe_mmo_gelu_kernel(
         load_experts(w1, "w1", w1_words, 2, E)
         load_experts(w2, "w2", w2_words, 0, E)
         load_plane(nc.sync, w2_plane, w2_scales.rearrange("e g b n -> b (e g) n"))
-        for e in range(E):
+        for e in range(E - 1):
             load_wz(e, 0)
         gate_p = tile("gate_p", [P, S], F32)
         nc.sync.dma_start(gate_p[:], gate2)
+        load_wz(E - 1, 0)
 
         spread = psum.tile([P, 4, P], F32, name="bank_p3")
         for j in range(4):
@@ -141,7 +142,7 @@ def tile_moe_mmo_gelu_kernel(
 
         x_slots = [gather("x_slots%d_" % g, x_window[g][:].bitcast(U32), "t", U32, 0, E) for g in range(2)]
         x_slot_scales = [[], []]
-        for lo, hi in [(0, 1), (1, E)]:
+        for lo, hi in [(0, 1), (1, 2), (2, E)]:
             for g in range(2):
                 x_slot_scales[g] = x_slot_scales[g] + gather("x_slot_scales%d_" % g, x_plane[:, g, :], "t", U8, lo, hi)
         z_slots = gather("z_slots", z_window[:].bitcast(U32), "p", U32, 0, E)
@@ -193,8 +194,6 @@ def tile_moe_mmo_gelu_kernel(
             if a == 0:
                 bank["p", e] = psum.tile([P, H], F32, name="bank_p%d" % e)
             codes = tile("wz_codes%d_%d" % (e, a), [P, 2 * P], U32)
-            if (e, a) == (3, 1):
-                places["free"] = places["free"] + 2048
             scales = tile("wz_scales%d_%d" % (e, a), [P, 2 * P], U8)
             nc.vector.quantize_mx(out=codes[:].bitcast(FP8X4), scales=scales[:], in_=wz_rounded[e, a][:])
             for u in range(2):
@@ -272,9 +271,8 @@ def tile_moe_mmo_gelu_kernel(
         hidden_of("t", 0, 2)
         hidden_of("t", 2, 3)
         hidden_of("t", 3, E)
-        hidden_of("p", 0, 2)
-        hidden_of("p", 2, 3)
-        hidden_of("p", 3, E)
+        for e in range(E):
+            hidden_of("p", e, e + 1)
         for e in range(E):
             text_product(e)
         for e in range(E):
@@ -300,29 +298,33 @@ def tile_moe_mmo_gelu_kernel(
         patch_hidden(1)
         second_product("t", 3, E, (3, 3), "wz_raw1_0", 1024)
 
+        second_product("p", 0, 1, (0, 0), "wz_raw1_0", 1536)
+
         round_wz(2)
         patch_product(2, 0)
         gate_and_scatter_both("t", 3, "wz_raw2_0")
         patch_product(2, 1)
         patch_hidden(2)
-        second_product("p", 0, 2, (0, 1), "wz_raw2_0", 1024, None, True)
+        second_product("p", 1, 2, (1, 1), "wz_raw2_0", 1024)
+        first = tile("gated_p0", [P, 2, C], F32, "wz_raw2_0", 2048)
+        gate_both("p", 0, first[:])
+        for h in range(2):
+            scatter("p", 0, 1, h, first[:, h, :])
 
         round_wz(3)
         patch_product(3, 0)
-        first = tile("gated_p0", [P, 2, C], F32, "wz_raw3_0")
-        gate_both("p", 0, first[:])
-        scatter("p", 0, 1, 1, first[:, 1, :])
+        rest = tile("gated_rest", [P, 2, 3 * C], F32, "wz_raw3_0")
+        gate_both("p", 1, rest[:, :, 0:C])
         patch_product(3, 1)
         patch_hidden(3)
-        second_product("p", 2, 3, (2, 2), "wz_raw3_0", 1024)
-        scatter("p", 0, 1, 0, first[:, 0, :], True)
-        rest = tile("gated_rest", [P, 2, 3 * C], F32, "wz_codes3_1")
-        gate_both("p", 1, rest[:, :, 0:C])
-        scatter("p", 1, 2, 0, rest[:, 0, 0:C])
-        gate_both("p", 2, rest[:, :, C : 2 * C])
+        second_product("p", 2, 3, (2, 2), "wz_raw3_0", 4096)
+        scatter("p", 1, 2, 0, rest[:, 0, 0:C], True)
+        apply_gate("p", 2, 3, 1, rest[:, 1, C : 2 * C])
+        plain = tile("plain_sums", [P, C], F32)
+        nc.scalar.copy(plain[:], sums["p", 2, 0])
         scatter("p", 1, 3, 1, rest[:, 1, 0 : 2 * C])
         second_product("p", 3, E, (3, 3))
-        scatter("p", 2, 3, 0, rest[:, 0, C : 2 * C], True)
+        nc.vector.tensor_tensor(result["p"][0][:].indirect(offsets["p"][:, 16:24]), plain[:], gate_p[:, 2 * C : 3 * C], MULT)
         gate_both("p", 3, rest[:, :, 2 * C : 3 * C])
         for h in (1, 0):
             scatter("p", 3, E, h, rest[:, h, 2 * C : 3 * C], h == 0)

from contextlib import ExitStack

import concourse.mybir as mybir

F32 = mybir.dt.float32
BF16 = mybir.dt.bfloat16
I32 = mybir.dt.int32
U32 = mybir.dt.uint32
U16 = mybir.dt.uint16
U8 = mybir.dt.uint8
FP8X4 = mybir.dt.float8_e4m3fn_x4
FP4X4 = mybir.dt.float4_e2m1fn_x4
GELU = mybir.ActivationFunctionType.Gelu_apprx_tanh
COPY = mybir.ActivationFunctionType.Copy
MULT = mybir.AluOpType.mult
ADD = mybir.AluOpType.add
IS_EQUAL = mybir.AluOpType.is_equal

P = 128
K, L = 1024, 512
T, Q = 768, 512
E, C = 4, 128
H, N = 512, 256
S = E * C
FLOPS = 2 * S * (K * H + L * H + 2 * H * N)
Z_WINDOW = 704
QUADRANT = 32


def tile_moe_mmo_gelu_kernel(
    tc, x_words, x_scales, z_words, z_scales, w1_words, w1_scales, wz, w2_words, w2_scales, gate1, gate2, offs, offs2, out
):
    nc = tc.nc
    with ExitStack() as ctx:
        lists = ctx.enter_context(tc.tile_pool(name="lists", bufs=1))
        sbuf = ctx.enter_context(tc.tile_pool(name="sbuf", bufs=1))
        psum = ctx.enter_context(tc.psum_pool(name="psum", bufs=1))

        places = {"free": 0}

        def tile(name, shape, dtype, on=None, at=0):
            size = {F32: 4, I32: 4, U32: 4, BF16: 2, U8: 1}[dtype]
            for n in shape[1:]:
                size = size * n
            if on is None:
                places[name] = places["free"]
                places["free"] = places["free"] + (size + 63) // 64 * 64
            else:
                places[name] = places[on] + at
            return sbuf.tile(shape, dtype, name=name, align_bytes=64, offset=places[name])

        offsets = {k: lists.tile([P, S // 16], U16, name="offsets_" + k) for k in "tp"}
        x_window = [tile("x_window%d" % g, [P, T], I32) for g in range(2)]
        z_window = tile("z_window", [P, Z_WINDOW], I32)
        x_plane = tile("x_plane", [P, 2, T], U8)
        z_plane = tile("z_plane", [P, 1, Z_WINDOW], U8)
        w1_plane = tile("w1_plane", [P, 2 * E, H], U8)
        w2_plane = tile("w2_plane", [P, E, N], U8)
        pieces = [1, 1, 1, 1]
        wz_raw = [[tile("wz_raw%d_%d" % (e, a), [P, 4, H // pieces[e]], F32) for a in range(pieces[e])] for e in range(E)]
        result = {
            "t": [tile("result_t%d" % h, [P, T], F32) for h in range(2)],
            "p": [tile("result_p%d" % h, [P, Q], F32) for h in range(2)],
        }

        def zero_plane(plane):
            nc.vector.memset(plane[:].rearrange("p a w -> p (a w)").bitcast(I32), 0)

        def load_plane(queue, plane, rows, lo=0, hi=4):
            for r in range(lo, hi):
                queue.dma_start(plane[r:P:32, :, 0 : rows.shape[2]].bitcast(I32), rows[r:16:4, :, :].bitcast(I32))

        gate_row = tile("gate_row", [P, 4], F32)
        nc.gpsimd.dma_start(gate_row[:], gate1[0].rearrange("(q j) -> q j", j=4))
        zero_plane(x_plane)
        zero_plane(z_plane)
        load_plane(nc.gpsimd, z_plane, z_scales.rearrange("g b t -> b g t"), 0, 2)
        zero_plane(w1_plane)

        zero = tile("zero", [P, 1], F32)
        ones = tile("ones", [P, QUADRANT], F32)
        column_number = tile("column_number", [P, QUADRANT], F32)
        row_number = tile("row_number", [P, QUADRANT], F32)
        identity = tile("identity", [P, P], F32)
        nc.vector.memset(zero[:], 0.0)
        nc.vector.memset(ones[:], 1.0)
        zero_plane(w2_plane)
        nc.vector.memset(z_window[:, Q:Z_WINDOW], 0)
        nc.vector.tensor_tensor_scan(column_number[:], ones[:], ones[:], 0.0, MULT, ADD)
        nc.vector.memset(identity[:], 0.0)
        nc.vector.transpose(row_number[:], column_number[:])
        for a in range(P // QUADRANT):
            rows = slice(QUADRANT * a, QUADRANT * (a + 1))
            nc.vector.tensor_tensor(identity[rows, rows], column_number[rows, :], row_number[rows, :], IS_EQUAL)

        for h in range(2):
            nc.scalar.activation(result["t"][h][:], zero[:].to_broadcast([P, T]), GELU)

        w1, w2 = {}, {}

        def load_experts(views, name, words, lo, hi):
            passes, row_bytes = words.shape[1], words.shape[3]
            held = tile("%s_%d" % (name, lo), [P, (hi - lo) * passes, row_bytes], U8)
            nc.sync.dma_start(held[:].bitcast(I32), words[lo:hi].rearrange("e g p b -> p (e g) b").bitcast(I32))
            for e in range(lo, hi):
                views[e] = held[:, (e - lo) * passes : (e - lo + 1) * passes, :]

        def load_wz(e, a):
            width = H // pieces[e]
            nc.sync.dma_start(wz_raw[e][a][:], wz[e].rearrange("(p j) i -> p j i", j=4)[:, :, a * width : (a + 1) * width])

        nc.sync.dma_start(x_window[0][:], x_words[0].rearrange("p t d -> p (t d)").bitcast(I32))
        nc.sync.dma_start(offsets["t"][:], offs)
        nc.sync.dma_start(x_window[1][:], x_words[1].rearrange("p t d -> p (t d)").bitcast(I32))
        load_plane(nc.sync, x_plane, x_scales.rearrange("g b t -> b g t"))
        load_experts(w1, "w1", w1_words, 0, 1)
        load_plane(nc.sync, w1_plane, w1_scales.rearrange("e g b i -> b (e g) i"))
        load_experts(w1, "w1", w1_words, 1, 2)
        nc.sync.dma_start(z_window[:, 0:Q], z_words[0].rearrange("p t d -> p (t d)").bitcast(I32))
        load_plane(nc.sync, z_plane, z_scales.rearrange("g b t -> b g t"), 2, 4)
        nc.sync.dma_start(offsets["p"][:], offs2)
        load_experts(w1, "w1", w1_words, 2, E)
        load_experts(w2, "w2", w2_words, 0, E)
        load_plane(nc.sync, w2_plane, w2_scales.rearrange("e g b n -> b (e g) n"))
        for e in range(E - 1):
            load_wz(e, 0)
        gate_p = tile("gate_p", [P, S], F32)
        nc.sync.dma_start(gate_p[:], gate2)
        load_wz(E - 1, 0)

        spread = psum.tile([P, 4, P], F32, name="bank_p3")
        for j in range(4):
            nc.tensor.transpose(spread[:, j, :], gate_row[:, j : j + 1].to_broadcast([P, P]), identity[:])
        gate_t = tile("gate_t", [P, S], F32)
        nc.scalar.copy(gate_t[:].rearrange("p (q j) -> p q j", j=4), spread[:].rearrange("p j q -> p q j"))
        gate = {"t": gate_t, "p": gate_p}

        def gather(name, window, k, dtype, lo, hi, on=None):
            slots = tile("%s%d" % (name, lo), [P, (hi - lo) * C], dtype, on)
            nc.vector.tensor_copy(slots[:], window.indirect(offsets[k][:, 8 * lo : 8 * hi]))
            return [slots[:, e * C : (e + 1) * C] for e in range(hi - lo)]

        x_slots = [gather("x_slots%d_" % g, x_window[g][:].bitcast(U32), "t", U32, 0, E) for g in range(2)]
        x_slot_scales = [[], []]
        for lo, hi in [(0, 1), (1, 2), (2, E)]:
            for g in range(2):
                x_slot_scales[g] = x_slot_scales[g] + gather("x_slot_scales%d_" % g, x_plane[:, g, :], "t", U8, lo, hi)
        z_slots = gather("z_slots", z_window[:].bitcast(U32), "p", U32, 0, E)
        z_slot_scales = gather("z_slot_scales", z_plane[:, 0, :], "p", U8, 0, E)

        bank, pairs, hidden, sums, both, wz_rounded = {}, {}, {}, {}, {}, {}

        def text_product(e):
            bank["t", e] = psum.tile([P, H], F32, name="bank_t%d" % e)
            for g in range(2):
                nc.tensor.matmul_mx(
                    out=bank["t", e][:],
                    lhsT=x_slots[g][e].bitcast(FP8X4),
                    lhsT_scale=x_slot_scales[g][e],
                    rhs=w1[e][:, g, :].bitcast(FP4X4),
                    rhs_scale=w1_plane[:, 2 * e + g, :],
                    start=(g == 0),
                    stop=(g == 1),
                )

        def text_gelu(e):
            pairs[e] = tile("pairs%d" % e, [P, 2, P, 2], BF16)
            nc.scalar.activation(pairs[e][:], bank["t", e][:].rearrange("c (p u v) -> c u p v", u=2, v=2), GELU)

        def hidden_of(k, lo, hi):
            held = tile("hidden_%s%d" % (k, lo), [P, (hi - lo) * 4 * C], BF16)
            for e in range(lo, hi):
                hidden[k, e] = held[:, (e - lo) * 4 * C : (e - lo + 1) * 4 * C]
            hidden[k, lo, hi] = held[:]

        def text_turn(lo, hi, host):
            turned = bank["t", host][:, 0 : (hi - lo) * 2 * C].rearrange("p (e u c) -> p e u c", u=2, c=C)
            for e in range(lo, hi):
                words = pairs[e][:].rearrange("c u p v -> c (u p v)").bitcast(F32)
                for u in range(2):
                    nc.tensor.transpose(turned[:, e - lo, u, :], words[:, u * P : (u + 1) * P], identity[:])
            target = hidden["t", lo, hi] if hi - lo > 1 else hidden["t", lo]
            nc.scalar.copy(target.bitcast(F32).rearrange("p (e c u) -> p e c u", u=2, c=C), turned.rearrange("p e u c -> p e c u"))

        def round_wz(e):
            for a in range(2):
                wz_rounded[e, a] = tile("wz_rounded%d_%d" % (e, a), [P, 2 * H], BF16)
                nc.vector.tensor_copy(
                    wz_rounded[e, a][:].rearrange("p (t m j) -> p m j t", t=2, j=4),
                    wz_raw[e][0][:].rearrange("p j (m t) -> p m j t", t=4)[:, :, :, 2 * a : 2 * a + 2],
                )

        def patch_product(e, a):
            if a == 0:
                bank["p", e] = psum.tile([P, H], F32, name="bank_p%d" % e)
            codes = tile("wz_codes%d_%d" % (e, a), [P, 2 * P], U32)
            scales = tile("wz_scales%d_%d" % (e, a), [P, 2 * P], U8)
            nc.vector.quantize_mx(out=codes[:].bitcast(FP8X4), scales=scales[:], in_=wz_rounded[e, a][:])
            for u in range(2):
                nc.tensor.matmul_mx(
                    out=bank["p", e][:, (2 * a + u) * C : (2 * a + u + 1) * C],
                    lhsT=codes[:, u * P : (u + 1) * P].bitcast(FP8X4),
                    lhsT_scale=scales[:, u * P : (u + 1) * P],
                    rhs=z_slots[e].bitcast(FP8X4),
                    rhs_scale=z_slot_scales[e],
                    start=True,
                    stop=True,
                )

        def patch_hidden(e):
            nc.scalar.activation(
                hidden["p", e].rearrange("p (c t) -> p c t", t=4),
                bank["p", e][:].rearrange("p (t c) -> p c t", t=4),
                GELU,
            )

        def second_product(k, lo, hi, hosts, on=None, at=0, scales_on=None, by_expert=False):
            width = (hi - lo) * C
            codes = tile("hidden_codes_%s%d" % (k, lo), [P, width], U32, on, at)
            scales = tile("hidden_scales_%s%d" % (k, lo), [P, width], U8, scales_on)
            source = hidden[k, lo, hi] if hi - lo > 1 else hidden[k, lo]
            nc.vector.quantize_mx(out=codes[:].bitcast(FP8X4), scales=scales[:], in_=source)
            for h in (1, 0):
                first = H - width * (1 if hosts[0] != hosts[1] else 2 - h)
                sums[k, lo, h] = bank[k, hosts[h]][:, first : first + width]
                for e in range(lo, hi):
                    slots = slice((e - lo) * C, (e - lo + 1) * C)
                    both[k, e] = bank[k, e][:, 2 * C : 4 * C].rearrange("p (h c) -> p h c", h=2)
                    nc.tensor.matmul_mx(
                        out=both[k, e][:, h, :] if by_expert else sums[k, lo, h][:, slots],
                        lhsT=w2[e][:, 0, 2 * P * h : 2 * P * (h + 1)].bitcast(FP4X4),
                        lhsT_scale=w2_plane[:, e, P * h : P * (h + 1)],
                        rhs=codes[:, slots].bitcast(FP8X4),
                        rhs_scale=scales[:, slots],
                        start=True,
                        stop=True,
                    )

        def apply_gate(k, lo, hi, h, target):
            nc.vector.tensor_tensor(target, sums[k, lo, h], gate[k][:, lo * C : hi * C], MULT)

        def scatter(k, lo, hi, h, source, on_vector=False):
            window = result[k][h][:].indirect(offsets[k][:, 8 * lo : 8 * hi])
            if on_vector:
                nc.vector.tensor_copy(window, source)
            else:
                nc.scalar.activation(window, source, COPY)
            if hi == E:
                columns = slice(0, T) if k == "t" else slice(T, T + Q)
                nc.sync.dma_start(out[h * P : (h + 1) * P, columns], result[k][h][:])

        def gate_and_scatter(k, lo, hi, h, on=None, at=0, on_vector=False):
            gated = tile("gated_%s%d_%d" % (k, lo, h), [P, (hi - lo) * C], F32, on, at)
            apply_gate(k, lo, hi, h, gated[:])
            scatter(k, lo, hi, h, gated[:], on_vector)

        def gate_both(k, e, target):
            nc.vector.tensor_tensor(
                target,
                both[k, e],
                gate[k][:, e * C : (e + 1) * C].unsqueeze(1).to_broadcast([P, 2, C]),
                MULT,
            )

        def gate_and_scatter_both(k, e, on, at=0):
            gated = tile("gated_%s%d" % (k, e), [P, 2, C], F32, on, at)
            gate_both(k, e, gated[:])
            for h in (1, 0):
                scatter(k, e, e + 1, h, gated[:, h, :])

        hidden_of("t", 0, 2)
        hidden_of("t", 2, 3)
        hidden_of("t", 3, E)
        for e in range(E):
            hidden_of("p", e, e + 1)
        for e in range(E):
            text_product(e)
        for e in range(E):
            text_gelu(e)
            if e < 2:
                text_turn(e, e + 1, e)
        second_product("t", 0, 2, (0, 1), "z_window")
        text_turn(2, 3, 0)
        gate_and_scatter("t", 0, 2, 1)
        text_turn(3, E, 1)

        round_wz(0)
        patch_product(0, 0)
        gate_and_scatter("t", 0, 2, 0, "wz_raw0_0")
        patch_product(0, 1)
        patch_hidden(0)
        second_product("t", 2, 3, (2, 2), "wz_raw0_0", 1024)

        round_wz(1)
        patch_product(1, 0)
        gate_and_scatter_both("t", 2, "wz_raw1_0")
        patch_product(1, 1)
        patch_hidden(1)
        second_product("t", 3, E, (3, 3), "wz_raw1_0", 1024)

        second_product("p", 0, 1, (0, 0), "wz_raw1_0", 1536)

        round_wz(2)
        patch_product(2, 0)
        gate_and_scatter_both("t", 3, "wz_raw2_0")
        patch_product(2, 1)
        patch_hidden(2)
        second_product("p", 1, 2, (1, 1), "wz_raw2_0", 1024)
        first = tile("gated_p0", [P, 2, C], F32, "wz_raw2_0", 2048)
        gate_both("p", 0, first[:])
        for h in range(2):
            scatter("p", 0, 1, h, first[:, h, :])

        round_wz(3)
        patch_product(3, 0)
        rest = tile("gated_rest", [P, 2, 3 * C], F32, "wz_raw3_0")
        gate_both("p", 1, rest[:, :, 0:C])
        patch_product(3, 1)
        patch_hidden(3)
        second_product("p", 2, 3, (2, 2), "wz_raw3_0", 4096)
        scatter("p", 1, 2, 0, rest[:, 0, 0:C], True)
        apply_gate("p", 2, 3, 1, rest[:, 1, C : 2 * C])
        plain = tile("plain_sums", [P, C], F32)
        nc.scalar.copy(plain[:], sums["p", 2, 0])
        scatter("p", 1, 3, 1, rest[:, 1, 0 : 2 * C])
        second_product("p", 3, E, (3, 3))
        nc.vector.tensor_tensor(result["p"][0][:].indirect(offsets["p"][:, 16:24]), plain[:], gate_p[:, 2 * C : 3 * C], MULT)
        gate_both("p", 3, rest[:, :, 2 * C : 3 * C])
        for h in (1, 0):
            scatter("p", 3, E, h, rest[:, h, 2 * C : 3 * C], h == 0)
